import numpy as np, ml_dtypes
CORES = [16,18,20,22]
N = 4
BF = ml_dtypes.bfloat16
W, S, RO, LIM = 4096, 256, 4, 6
HEARER = [[1, 2, 3, 0], [2, 3, 0, 1], [3, 0, 1, 2], [1, 2, 3, 0]]
def world(rng, skew):
    m = rng.integers(2, 5, (8, 1, 1)); pn = rng.integers(2, 9, (1, 8, 1)); noise = 0.05 + 0.45 * rng.random((N, 8, 1, 1))
    alph = np.argsort(rng.random((8, 16, 513)), axis=-1)[..., :4] - 256
    proto = (rng.random((8, 8, 16)) * m).astype(np.int64); z = (rng.random((N, 8, W)) * pn).astype(np.int64)
    e = proto[np.arange(8)[None, :, None], z]
    u = (rng.random(e.shape, dtype=np.float32) ** skew * m).astype(np.int64)
    e = np.where(rng.random(e.shape, dtype=np.float32) < noise, np.minimum(u, 3), e)
    return np.ascontiguousarray(alph[np.arange(8)[None, :, None, None], np.arange(16), e].transpose(0, 1, 3, 2))
def parts(rng, skew=1):
    X = world(rng, skew)
    As = np.minimum((W * rng.random((N, 8, 16, W)) ** skew).astype(np.int64), W - 1)
    C = np.minimum((W * rng.random((N, 8, 16, S)) ** skew).astype(np.int64), W - 1); H = np.minimum((W * rng.random((N, 8, 16, S)) ** skew).astype(np.int64), W - 1)
    R = np.argsort(rng.random((N, 8, 16, S)), axis=2); A = np.minimum((256 * rng.random((N, 8, S)) ** skew).astype(np.int64), 255)
    return X, As, C, H, R, A
def pack(X, As, C, H, R, A):
    return {"x": np.ascontiguousarray(X.reshape(N, 128, W)).astype(np.float32).astype(BF), "assoc": np.ascontiguousarray(As.reshape(N, 128, W)).astype(np.int32),
            "ctx": np.ascontiguousarray(C.reshape(N, 128, S)).astype(np.int32), "cand": np.ascontiguousarray(H.reshape(N, 128, S)).astype(np.int32),
            "pref": np.ascontiguousarray(R.reshape(N, 128, S)).astype(np.int32), "fail0": np.ascontiguousarray(A).astype(np.int32)}
def setup_inputs(rng):
    return pack(*parts(rng))
def setup_inputs_spread(rng):
    X, As, C, H, R, A = parts(rng, 3)
    X = np.where((X == X[0, :, :, :1]) & (rng.random((8, 16, 1)) < 0.5), 0, X)
    share = 0.05 + 0.4 * rng.random((N, 8, 1, 1))
    X = np.where(rng.random((N, 8, 1, W)) < share, rng.integers(-256, 257, X.shape), X)
    X = np.where((X == 0) & (rng.random(X.shape, dtype=np.float32) < 0.5), -0.0, X)
    return pack(X, As, C, H, R, A)
def endlist(rng, shape):
    return np.where(rng.random(shape) < 0.68, rng.choice(np.array([0, W - 1]), shape), rng.integers(0, W, shape))
def setup_inputs_ends(rng):
    proto = rng.choice(np.array([-1, 1]), (8, 6, 16)); e = proto[np.arange(8)[None, :, None], rng.integers(0, 6, (N, 8, W))]
    e = np.where(rng.random(e.shape, dtype=np.float32) < 0.05 + 0.3 * rng.random((N, 8, 1, 1)), -e, e)
    u = rng.random((N, 8, W, 1)); e = np.where(u < 0.15, 1, np.where(u < 0.3, -1, e))
    X = np.ascontiguousarray(256 * e.transpose(0, 1, 3, 2)); sg = 256 * rng.choice(np.array([-1, 1]), (8, 1)); a = np.arange(16)[:, None]
    X[..., 0] = -sg; X[..., W - 1] = sg
    X[..., W - 16:W - 1] = sg[:, :, None] * np.where(np.arange(16)[:, None] == np.arange(1, 16), -1, 1)
    X[..., 1:16] = -X[..., W - 16:W - 1]
    X[..., 16:32] = sg[:, :, None] * np.where((a >= 1) & (a <= np.arange(16)), 1, -1)
    As = endlist(rng, (N, 8, 16, W)); C = endlist(rng, (N, 8, 16, S)); H = endlist(rng, (N, 8, 16, S))
    C[..., S - 8:] = np.concatenate([np.array([W - 1]), np.arange(W - 16, W - 1)])[:, None]
    H[..., S - 3:] = 0; H[:, :, 15, S - 1] = W - 1; H[:, :, 14:, S - 3] = W - 1
    C[..., S - 4] = a[:, 0]; H[..., S - 4] = W - 1
    H[..., S - 8:S - 4] = 31 - np.arange(11, 15) - (a < rng.integers(1, 16, (N, 8, 1, 4)))
    C[..., 0] = W - 1; C[:, :, 0, 0] = 0; H[..., 0] = W - 1
    C[..., 1] = W - 1; H[..., 1] = 0
    R = np.where(rng.random((N, 8, 1, S)) < 0.5, a, 15 - a); R = np.where(rng.random((N, 8, 1, S)) < 0.25, np.argsort(rng.random((N, 8, 16, S)), axis=2), R)
    return pack(X, As, C, H, R, rng.choice(np.array([0, 255]), (N, 8, S)))
def setup_inputs_corners(rng):
    X, As, C, H, R, A = parts(rng); k = np.arange(16); kk = k[:, None]; o = np.arange(1, S, 2); M = len(o); sp = np.argsort(np.array(HEARER[0]))
    A = rng.choice(np.array([0, 1, 2, 3, 252, 253, 254, 255]), (N, 8, S))
    R = np.where(rng.random((N, 8, 1, S)) < 0.3, np.where(rng.random((N, 8, 1, S)) < 0.5, kk, 15 - kk), R)
    rk = R[..., o].transpose(0, 1, 3, 2)[:, :, :, None, :]
    kind = rng.integers(0, 4, (N, 8, M, 1, 1)); b = rng.integers(-256, 256, (N, 8, M, 1, 16))
    one = (rk == kk) | ((rk > kk) & (rng.random((N, 8, M, 16, 16)) < 0.5))
    dx = (((kind == 1) & one) | (kind == 2) | ((kind == 3) & (rk == 15) & (kk >= 8))) & (kk > 0)
    room = (LIM + (A[..., o] & 3))[..., None, None]; how = rng.integers(0, 4, (N, 8, M, 1, 1))
    m = np.where(how == 0, 0, np.where(how == 1, room, np.where(how == 2, room + 1, 16)))
    w = np.where(kind == 0, 0, rng.choice(np.array([0, 1, 14, 15]), (N, 8, M, 1, 1)))
    dy = np.where(kind == 3, rk < m, rk >= 16 - m) | (kk < w)
    cols = (16 * o[:, None] + k).reshape(-1)
    X[..., cols] = (b + dx).transpose(0, 1, 4, 2, 3).reshape(N, 8, 16, 16 * M)
    X[..., cols - 16] = (b + dy).transpose(0, 1, 4, 2, 3).reshape(N, 8, 16, 16 * M)[sp]
    C[..., o] = 16 * o + kk; H[..., o] = 16 * (o - 1) + kk
    C[:, 6, :, 0::2] = C[:, 6, :1, 0::2]; H[:, 2, :, 0::2] = H[:, 2, :1, 0::2]
    As[:, 3] = np.where(rng.random((N, 16, W)) < 0.5, np.arange(W), As[:, 3]); As[:, 5] = rng.choice(np.array([0, W - 1]), (N, 16, W))
    return pack(X, As, C, H, R, A)
def setup_inputs_bulk(rng):
    X, As, C, H, R, A = parts(rng); h = W // 2; v = h // 2; m = min(LIM, 8)
    ga, gb, gc, gd, ge = [int(i) for i in rng.permutation(8)[:5]]
    X[:, ga, :, :h] = 2 * rng.integers(-128, 129, (N, 16, h)); X[:, gb, :, :h] = 2 * rng.integers(-128, 129, (16, 1))
    for g in (ga, gb):
        X[:, g, :, h:] = 2 * rng.integers(-128, 128, (N, 16, W - h)) + 1
        C[:, g] = rng.integers(h, W, (N, 16, S)); C[:, g, 0] = rng.integers(0, h, (N, S))
    H[:, ga] = rng.integers(h, W, (N, 16, S)); H[:, gb] = rng.integers(0, h, (N, 16, S))
    X[:, gc] = (np.argsort(rng.random((16, 513)), axis=-1)[:, :N] - 256).T[:, :, None]; A[:, gc, ::2] = 255
    X[:, gd] = 2 * rng.integers(-128, 128, (16, 1))
    X[:, gd, 8:8 + m, v:h] += rng.integers(0, 2, (N, m, h - v)); X[:, gd, :8, h:] += rng.integers(0, 2, (N, 8, W - h))
    C[:, gd] = rng.integers(h, W, (N, 16, S)); C[:, gd, 0] = rng.integers(0, v, (N, S)); H[:, gd] = rng.integers(v, h, (N, 16, S))
    near = LIM + ((254 + RO) & 3); b = 2 * rng.integers(-128, 128, (16, 1))
    X[:, ge, :, :h] = b; X[:, ge, :, h:] = b + 1; X[:, ge, :, h + v:] = b + (np.argsort(rng.random(16)) < near)[:, None]; X[:, ge, :, ::16] = b
    C[:, ge] = h + 2 * rng.integers(0, v // 2, (N, 16, S)) + 1
    H[:, ge] = N * rng.integers(0, h // N, (N, 16, S)) + np.arange(N)[:, None, None]
    As[:, ge, 0, :h] = h + v * (np.arange(h) % N == np.array(HEARER[RO - 2])[:, None]) + 2 * rng.integers(0, v // 2, (N, h)) + 1
    A[:, ge, ::2] = 255
    return pack(X, As, C, H, R, A)
def check_inputs(d):
    bad = []
    for name, lo, hi in (("x", -256, 256), ("assoc", 0, W - 1), ("ctx", 0, W - 1), ("cand", 0, W - 1), ("pref", 0, 15), ("fail0", 0, 255)):
        v = np.asarray(d[name]).astype(np.float64)
        if not (np.min(v) >= lo and np.max(v) <= hi): bad.append("range of " + name)
        if np.any(v != np.rint(v)): bad.append("whole numbers in " + name)
    if np.any(np.sort(np.asarray(d["pref"]).astype(np.int64).reshape(-1, 8, 16, S), axis=2) != np.arange(16)[:, None]): bad.append("permutations in pref")
    return bad
def pick(a, ix):
    return np.take_along_axis(a, ix.reshape(N, 8, 1, 16 * S), 3).reshape(N, 8, 16, 16, S)
def front(R, row, fail):
    old = np.take_along_axis(R, row[:, :, None, :], 2)
    moved = np.where(np.arange(16)[:, None] == row[:, :, None, :], 0, R + (R < old))
    return np.where(fail[:, :, None, :], moved, R)
def reference(x, assoc, ctx, cand, pref, fail0):
    X = x.astype(np.float32).astype(np.int16).reshape(N, 8, 16, W); As = assoc.astype(np.int64).reshape(N, 8, 16, W)
    C = ctx.astype(np.int64).reshape(N, 8, 16, S); H = cand.astype(np.int64).reshape(N, 8, 16, S); R = pref.astype(np.int64).reshape(N, 8, 16, S); A = fail0.astype(np.int64).reshape(N, 8, S)
    for t in range(RO):
        q = np.array(HEARER[t]); sp = np.argsort(q)
        xk = pick(X, C); x0 = xk[:, :, :, 0]
        first = np.min(np.where(xk != x0[:, :, :, None], R[:, :, :, None], 16), axis=2)
        desc = np.any(R[:, :, :, None] == first[:, :, None], axis=3)
        top = np.min(first, axis=2)
        yk = pick(X, H)[q]
        miss = np.sum((yk != x0[:, :, :, None]) & desc[:, :, :, None], axis=2)
        ks = np.argmin(miss, axis=2)
        n = np.take_along_axis(H[q], ks[:, :, None, :], 2)[:, :, 0]
        y = np.take_along_axis(yk, ks[:, :, None, None, :], 3)[:, :, :, 0]
        un = y != x0; fail = np.sum(un, axis=2) > LIM + (A & 3); row = np.argmin(np.where(un, R, 16), axis=2)
        A = A + fail
        R = front(R, row, fail); R = front(R, row[sp], fail[sp])
        cn = np.take_along_axis(As, n[:, :, None, :], 3); hn = np.take_along_axis(As, n[sp][:, :, None, :], 3)
        C = np.where((first == top[:, :, None]) & (first < 16), cn, C); C[:, :, 0] = cn[:, :, 0]
        H = np.where(miss[sp] > 0, hn, H)
        if t < RO - 1:
            put = np.broadcast_to((16 * np.arange(S) + ks[sp])[:, :, None, :], (N, 8, 16, S))
            np.put_along_axis(X, put, np.where(desc, x0, y)[sp], 3)
    return {"yctx": C.reshape(N, 128, S).astype(np.float32), "ycand": H.reshape(N, 128, S).astype(np.float32), "ypref": R.reshape(N, 128, S).astype(np.float32), "yfail": A.astype(np.float32)}

@@ -1,0 +1,637 @@
+import math
+from concourse.mybir import AluOpType as OP, ActivationFunctionType as AF
+
+N = 4
+DIST = [1, 2, 3, 1]
+RO = len(DIST)
+S = 256
+W = 4096
+NH = 2
+HS = S // NH
+LN2 = math.log(2.0)
+WT = 85
+CFG = {"npc": 4,
+       "vc": ((0, 3),),
+       "vc0": ((0, 3),),
+       "vh": (),
+       "ns": (4, 4),
+       "es": (1, 1),
+       "nq": (1, 1),
+       "bitV": (1, 1), "alpha": 20.0, "win": 300.0,
+       "bonus": 1500.0, "g": 1.5, "f": 1.2, "ov": 12.0, "wake": 120.0, "hop": 2000.0}
+
+SCRATCH = {}
+for _n, _s, _d in [
+    ("X", [128, W], "bfloat16"), ("ASI", [128, W], "int32"), ("ASH", [128, W], "float32"),
+    ("XG", [128, W], "bfloat16"), ("YG", [128, W], "bfloat16"), ("DW", [128, W], "bfloat16"), ("E", [128, W], "bfloat16"), ("G", [128, W], "bfloat16"),
+    ("CIN", [128, S], "int32"), ("HIN", [128, S], "int32"), ("RIN", [128, S], "int32"), ("FIN", [8, S], "int32"), ("Q8I", [8, S], "int32"),
+    ("A8", [8, S], "bfloat16"), ("Q8", [8, S], "bfloat16"), ("AB", [128, S], "bfloat16"), ("IND", [128, S], "bfloat16"),
+    ("C", [128, S], "float32"), ("C16", [128, S], "uint16"), ("HK", [128, S], "float32"), ("H16", [128, S], "uint16"),
+    ("R", [128, S], "bfloat16"), ("R1", [128, S], "bfloat16"), ("MA", [128, S], "bfloat16"), ("LA", [128, S], "bfloat16"), ("IW", [128, S], "bfloat16"),
+    ("AB1", [128, S], "bfloat16"), ("BIT", [128, S], "bfloat16"), ("TI", [128, S], "int32"), ("TJ", [128, S], "int32"), ("KAP", [128, S], "bfloat16"),
+    ("CM", [128, S], "float32"), ("KH", [128, S], "float32"), ("HM", [128, S], "float32"), ("UND", [128, S], "bfloat16"), ("DSC", [128, S], "bfloat16"),
+    ("XD", [128, S], "bfloat16"), ("YU", [128, S], "bfloat16"), ("KT", [128, S], "float32"), ("SC", [128, S], "float32"),
+    ("K32", [128, 16], "int32"), ("N32", [128, 16], "int32"), ("KK", [128, 16], "int32"), ("OF", [128, 16], "int32"), ("OF16", [128, 16], "uint16"),
+    ("DM", [128, S], "bfloat16"), ("DMW", [128, S], "bfloat16"), ("TH", [128, S], "float32"),
+    ("OC", [128, S], "float32"), ("OH", [128, S], "float32"), ("OR", [128, S], "float32"), ("OA", [128, S], "float32"),
+    ("IP", [128, 1], "int32"), ("KI", [128, 1], "int32"), ("B4I", [128, 1], "int32"), ("COL", [128, 16], "float32"), ("COL2", [128, 2], "float32"), ("EA", [128, 1024], "bfloat16"), ("CNH", [128, 1024], "bfloat16"), ("THC", [128, 16], "float32"), ("COLB", [128, 2], "bfloat16"),
+    ("IM", [128, 128], "float32"), ("IMG", [128, 128], "float32"), ("IMK", [128, 128], "float32"), ("IMB", [128, 128], "bfloat16"),
+    ("SEL", [128, 2048], "bfloat16"), ("CNT", [128, 2048], "bfloat16"),
+    ("mB", [128, 128], "bfloat16"), ("mI", [128, 128], "bfloat16"), ("mNI", [128, 128], "bfloat16"), ("mNB", [128, 128], "bfloat16"),
+    ("mTB", [128, 128], "bfloat16"), ("mWB", [128, 128], "bfloat16"), ("mCW", [128, 128], "bfloat16"), ("mKC", [128, 128], "bfloat16"),
+    ("mNW", [128, 128], "bfloat16"), ("m4", [128, 128], "bfloat16"), ("ONES", [128, 128], "bfloat16"), ("mI2", [128, 128], "bfloat16"), ("TMP", [128, 128], "float32"), ("MK0", [128, 128], "float32"),
+    ("fI", [128, 128], "float32"), ("fP", [128, 512], "float32"), ("SD", [128, 128], "float32"), ("CII", [128, 16], "int32"), ("CI", [128, 16], "int32"),
+    ("mG8", [8, 128], "bfloat16"),
+]:
+    SCRATCH[_n] = ("sbuf", _s, _d)
+for _t in range(RO):
+    SCRATCH["M0_%d" % _t] = ("sbuf", [128, 3 * S], "bfloat16")
+    SCRATCH["L0_%d" % _t] = ("sbuf", [128, 3 * S], "bfloat16")
+    for _n in ("M1_", "L1_", "FF_", "LF_"):
+        SCRATCH[_n + str(_t)] = ("sbuf", [128, S], "bfloat16")
+    for _n in ("NS_", "LN_"):
+        SCRATCH[_n + str(_t)] = ("sbuf", [128, 16], "uint16")
+for _b in range(8):
+    SCRATCH["pb%d" % _b] = ("psum", [128, 512], "float32")
+
+SEMAPHORES = ["sT", "sV", "sS", "sG"]
+SEMAPHORES += ["ld_%s" % _n for _n in ("x", "ctx", "cand", "pref", "assoc", "fail0")] + ["st_%d" % _i for _i in range(12)]
+for _t in range(RO):
+    for _m in ("00", "01", "10", "11", "20", "21", "30", "31"):
+        SEMAPHORES += ["r%d_%s" % (_t, _m), "l%d_%s" % (_t, _m)]
+
+cP, cK, cG16, cPp, cPm, cS0, cS1, cKC, c16K, cH, c16P = range(11)
+
+_ORDER = {}
+
+
+PER_ROUND = ("L10", "L11", "L00", "L01", "NS0", "NS1", "LN0", "LN1", "x0_0", "x0_1", "x0p0", "x0p1")
+
+
+def build(g, T, topo, rank, core):
+    ops = []
+    cur_t = [0]
+    cur_h = [0]
+    GR = CFG["g"]
+
+    def key(k):
+        return k + "_r%d" % cur_t[0] if k in PER_ROUND else k
+
+    def add(q, fn, rd, wr, cost, banks=(), sem=None, val=1, lat=0.0):
+        ops.append({"q": q, "fn": fn, "rd": [key(k) for k in rd], "wr": [key(k) for k in wr], "bk": list(banks), "cost": cost, "sem": sem, "val": val, "lat": lat,
+                    "h": cur_h[0], "t": cur_t[0]})
+
+    CY = 0.83 * CFG["f"]
+
+    def vcost(n, rate=1.0):
+        return max(64, n * rate) * CY + CFG["ov"]
+
+    def V(name, rd, wr, n, rate=1.0, banks=(), extra=0.0, **kw):
+        f = {"tt": g.vector.tensor_tensor, "ts": g.vector.tensor_scalar, "cp": g.vector.tensor_copy, "tr": g.vector.transpose,
+             "scan": g.vector.tensor_tensor_scan}[name]
+        add("V", lambda: f(**kw), rd, wr, vcost(n, rate) + extra, banks)
+
+    def A(rd, wr, n, banks=(), extra=0.0, rate=1.0, **kw):
+        add("S", lambda: g.scalar.activation(**kw), rd, wr, n * rate * CY + 20 + extra, banks)
+
+    def MM(lst, rd, wr, banks):
+        def fn():
+            ins = None
+            for o, l, r, a, b, n, f in lst:
+                ins = g.tensor.matmul(out=o, lhsT=l, rhs=r, start=a, stop=b)
+            return ins
+        add("T", fn, rd, wr, sum(max(64, n) * (4 if f else 1) * 0.42 * 1.22 for o, l, r, a, b, n, f in lst) + 20, banks)
+
+    def col(i):
+        return T.COL[:, i:i + 1]
+
+    def sl(b, h):
+        return b[:, h * HS:(h + 1) * HS]
+
+    def m0(b, h, j):
+        return b[:, (3 * h + j) * HS:(3 * h + j + 1) * HS]
+
+    def ps(b, r):
+        return T["pb%d" % b][:, r * 128:(r + 1) * 128]
+
+    def ldw(q, semn, key, dst, src, lat):
+        e = g.sync if q == "Y" else g.scalar
+        add(q, lambda: e.dma_start(out=dst, in_=src), [], [key], 60, sem="ld_" + semn, val=16, lat=lat)
+
+    ldw("Y", "ctx", "CIN", T.CIN[:], T.ctx[:], 2200)
+    ldw("S", "x", "X", T.X[:], T.x[:], 4500)
+    ldw("Y", "pref", "RIN", T.RIN[:], T.pref[:], 2300)
+    ldw("Y", "cand", "HIN", T.HIN[:], T.cand[:], 2400)
+    ldw("Y", "fail0", "FIN", T.FIN[:], T.fail0[:], 2400)
+    ldw("S", "assoc", "ASI", T.ASI[:], T.assoc[:], 6500)
+    ops[-1]["rd"] = ["X"]
+
+    def iota(dst, key, pattern, base, cm, n, flag=True):
+        if flag:
+            fn = lambda: g.iota(dst, pattern, base, cm, allow_small_or_imprecise_dtypes=True)
+        else:
+            fn = lambda: g.iota(dst, pattern, base, cm)
+        add("G", fn, [], [key], 130 + 2 * n * CY)
+
+    iota(T.IP[:], "IP", [[1, 1]], 0, 1, 1, False)
+    iota(T.IM[:], "IM", [[1, 128]], 0, 0, 128)
+    iota(T.IMG[:], "IMG", [[16, 8], [0, 16]], 0, 0, 128)
+    iota(T.IMB[:], "IMB", [[1, 128]], 0, 0, 128)
+    iota(T.IMK[:], "IMK", [[0, 8], [1, 16]], 0, 0, 128)
+    iota(T.CII[:], "CII", [[256, 16]], 15, 0, 16, False)
+
+    V("cp", ["CIN"], ["C160", "C161"], S, out=T.C16[:], in_=T.CIN[:])
+
+    V("ts", ["IP"], ["KI"], 1, out=T.KI[:], in0=T.IP[:], scalar1=15, scalar2=None, op0=OP.bitwise_and)
+    V("cp", ["IP"], ["cP"], 1, out=col(cP), in_=T.IP[:])
+    V("cp", ["KI"], ["cK"], 1, out=col(cK), in_=T.KI[:])
+    V("tt", ["cP", "cK"], ["cG16"], 1, out=col(cG16), in0=col(cP), in1=col(cK), op=OP.subtract)
+
+    def mat(dst, key, src, skey, c, ckey, n=128, rate=1.0):
+        V("ts", [skey, ckey], [key], n, rate, out=dst, in0=src, scalar1=c, scalar2=None, op0=OP.is_equal)
+
+    mat(T.mI[:], "mI", T.IM[:], "IM", col(cP), "cP")
+    V("ts", ["mI"], ["mNI"], 128, 0.5, out=T.mNI[:], in0=T.mI[:], scalar1=-1.0, scalar2=None, op0=OP.mult)
+
+    def scol(i, key, src, skey, **kw):
+        V("ts", [skey], [key], 1, out=col(i), in0=src, **kw)
+
+    def state_from_pref():
+        V("cp", ["RIN"], ["R0", "R1_"], S, out=T.R[:], in_=T.RIN[:])
+    state_from_pref()
+    ops[-1]["wr"] = ["Rs0", "Rs1"]
+
+    def orders(h, t, src, rd, banks=()):
+        A(rd, ["w%d_%d" % (t, h)], HS, banks, out=m0(T["M0_%d" % t], h, 1), in_=src, func=AF.Exp, bias=col(12), scale=-11.0 * LN2)
+        ops[-1]["rd"].append("bias")
+        A(rd, ["IW%d" % h], HS, banks, out=sl(T.IW, h), in_=src, func=AF.Exp, scale=LN2)
+
+    add("V", lambda: g.vector.memset(col(12), WT * LN2), [], ["bias"], 80)
+    add("V", lambda: g.vector.memset(col(13), 6.5 * 2.0 ** 96), [], ["bias"], 80)
+    add("V", lambda: g.vector.memset(col(14), 15.0 * LN2), [], ["bias"], 80)
+    for h in range(NH):
+        orders(h, 0, sl(T.R, h), ["Rs%d" % h])
+
+    for k in range(16):
+        V("ts", ["IMB", "cG16"], ["SEL%d" % (k // 4)], 128, 0.5, out=T.SEL[:, k * 128:(k + 1) * 128], in0=T.IMB[:], scalar1=float(k), scalar2=col(cG16), op0=OP.subtract, op1=OP.is_equal)
+    for j in range(4):
+        MM([(T["pb%d" % j][:, 0:512], T.mI[:], T.SEL[:, j * 512:(j + 1) * 512], True, True, 512, False)], ["mI", "SEL%d" % j], ["ring%d" % j], [j])
+        m = 512 if j < 3 else 384
+        V("tt", ["SEL%d" % j, "SEL%d" % min(j + 1, 3), "ring%d" % j], ["CNT%d" % j], m, 1.0, [j], out=T.CNT[:, j * 512:j * 512 + m], in0=T["pb%d" % j][:, 0:m], in1=T.SEL[:, j * 512 + 128:j * 512 + 128 + m], op=OP.subtract)
+    V("cp", ["SEL3"], ["CNT3"], 128, 0.5, out=T.CNT[:, 1920:2048], in_=T.SEL[:, 1920:2048])
+    ns = CFG["ns"]
+    nx = max(ns)
+    allcnt = ["CNT%d" % j for j in range(4)]
+    allsel = ["SEL%d" % j for j in range(4)]
+    V("ts", allcnt, ["CNH"], 128 * nx, 0.5, out=T.CNH[:, 0:128 * nx], in0=T.CNT[:, 128 * (16 - nx):], scalar1=0.5, scalar2=None, op0=OP.mult)
+    for h in range(NH):
+        V("ts", ["cK"], ["c8%d" % h], 1, out=T.COL2[:, h:h + 1], in0=col(cK), scalar1=float(16 - ns[h]), scalar2=8.0, op0=OP.is_equal, op1=OP.mult)
+    for r in range(16 - nx, 16):
+        add("V", lambda r=r: g.vector.memset(T.THC[:, r:r + 1], -0.6 * 2.0 ** (WT - 11 * r)), [], ["thr%d" % r], 65)
+
+    def cntm(r, h):
+        if r >= 16 - ns[h]:
+            return T.CNH[:, 128 * (r - 16 + nx):128 * (r - 15 + nx)]
+        return T.CNT[:, 128 * r:128 * (r + 1)]
+    mat(T.mB[:], "mB", T.IMG[:], "IMG", col(cG16), "cG16")
+    add("V", lambda: g.vector.memset(T.ONES[:], 1.0), [], ["ONES"], 80)
+    A(["cK", "bias"], ["cb2"], 1, out=T.COLB[:, 0:1], in_=col(cK), func=AF.Exp, bias=col(14), scale=-LN2)
+    A(["cK", "bias"], ["cbw"], 1, out=T.COLB[:, 1:2], in_=col(cK), func=AF.Exp, bias=col(12), scale=-11.0 * LN2)
+    V("ts", ["mB", "cb2"], ["mWB"], 128, 1.0, out=T.mWB[:], in0=T.mB[:], scalar1=T.COLB[:, 0:1], scalar2=None, op0=OP.mult)
+    V("ts", ["mWB"], ["mNW"], 128, 0.5, out=T.mNW[:], in0=T.mWB[:], scalar1=-1.0, scalar2=None, op0=OP.mult)
+    V("ts", ["mI"], ["m4"], 128, 0.5, out=T.m4[:], in0=T.mI[:], scalar1=-4.0, scalar2=None, op0=OP.mult)
+    V("cp", ["HIN"], ["H160", "H161"], S, out=T.H16[:], in_=T.HIN[:])
+    V("ts", ["mB", "cbw"], ["TMP"], 128, 1.0, out=T.TMP[:], in0=T.mB[:], scalar1=T.COLB[:, 1:2], scalar2=-0.6, op0=OP.mult, op1=OP.mult)
+    V("ts", ["IMK"], ["MK0"], 128, 1.0, out=T.MK0[:], in0=T.IMK[:], scalar1=0.5, scalar2=None, op0=OP.is_gt)
+    V("tt", ["TMP", "MK0"], ["mCW"], 128, 2.0, out=T.mCW[:], in0=T.TMP[:], in1=T.MK0[:], op=OP.mult)
+    scol(cKC, "cKC", col(cK), "cK", scalar1=0.0, scalar2=-(2.0 ** -90), op0=OP.is_equal, op1=OP.add)
+    V("ts", ["mI", "cKC"], ["mKC"], 128, 1.0, out=T.mKC[:], in0=T.mI[:], scalar1=col(cKC), scalar2=None, op0=OP.mult)
+    mat(T.fI[:], "fI", T.IM[:], "IM", col(cP), "cP")
+    V("cp", ["CIN"], ["Cs0", "Cs1"], S, out=T.C[:], in_=T.CIN[:])
+    scol(cH, "cH", col(cK), "cK", scalar1=-4096.0, scalar2=61440.0, op0=OP.mult, op1=OP.add)
+    V("ts", ["HIN", "cH"], ["HK0", "HK1"], S, out=T.HK[:], in0=T.HIN[:], scalar1=col(cH), scalar2=2.0 ** -17, op0=OP.add, op1=OP.mult)
+    V("ts", ["mB"], ["mNB"], 128, 0.5, out=T.mNB[:], in0=T.mB[:], scalar1=-1.0, scalar2=None, op0=OP.mult)
+    V("ts", ["mI"], ["mI2"], 128, 0.5, out=T.mI2[:], in0=T.mI[:], scalar1=2.0, scalar2=None, op0=OP.mult)
+    V("tt", ["mI2", "mB"], ["mTB"], 128, 2.0, out=T.mTB[:], in0=T.mI2[:], in1=T.mB[:], op=OP.subtract)
+    V("ts", ["IP"], ["B4I"], 1, out=T.B4I[:], in0=T.IP[:], scalar1=4, scalar2=1, op0=OP.arith_shift_right, op1=OP.bitwise_and)
+    V("cp", ["B4I"], ["cS1"], 1, out=col(cS1), in_=T.B4I[:])
+    scol(cS0, "cS0", col(cS1), "cS1", scalar1=-1.0, scalar2=1.0, op0=OP.mult, op1=OP.add)
+    scol(cPp, "cPp", col(cP), "cP", scalar1=16.0, scalar2=None, op0=OP.add)
+    scol(cPm, "cPm", col(cP), "cP", scalar1=-16.0, scalar2=None, op0=OP.add)
+    scol(c16K, "c16K", col(cK), "cK", scalar1=16.0, scalar2=None, op0=OP.mult)
+    scol(c16P, "c16P", col(cP), "cP", scalar1=16.0, scalar2=None, op0=OP.mult)
+    for j, (c, ck, s, sk) in enumerate([(cP, "cP", cS0, "cS0"), (cPp, "cPp", cS0, "cS0"), (cPm, "cPm", cS1, "cS1"), (cP, "cP", cS1, "cS1")]):
+        V("ts", ["IM", ck, sk], ["fP"], 128, 1.0, out=T.fP[:, j * 128:(j + 1) * 128], in0=T.IM[:], scalar1=col(c), scalar2=col(s), op0=OP.is_equal, op1=OP.mult)
+    V("ts", ["IMK"], ["SD"], 128, 1.0, out=T.SD[:], in0=T.IMK[:], scalar1=0.0, scalar2=-4096.0, op0=OP.is_equal, op1=OP.mult)
+    V("ts", ["CII", "c16K"], ["CI"], 16, 1.0, out=T.CI[:], in0=T.CII[:], scalar1=col(c16K), scalar2=None, op0=OP.add)
+    V("ts", ["IMG", "c16P"], ["mG8"], 128, 1.0, out=T.mG8[:], in0=T.IMG[0:8, :], scalar1=T.COL[0:8, c16P:c16P + 1], scalar2=None, op0=OP.is_equal)
+    V("cp", ["FIN"], ["A8"], S, out=T.A8[:], in_=T.FIN[:])
+    V("ts", ["FIN"], ["Q8I"], S, out=T.Q8I[:], in0=T.FIN[:], scalar1=3, scalar2=None, op0=OP.bitwise_and)
+    V("cp", ["Q8I"], ["Q8"], S, out=T.Q8[:], in_=T.Q8I[:])
+    MM([(T.pb6[:, 0:256], T.mG8[:], T.A8[:], True, True, S, False), (T.pb6[:, 256:512], T.mG8[:], T.Q8[:], True, True, S, False)],
+       ["mG8", "A8", "Q8"], ["b6a"], [6])
+    A(["b6a"], ["AB"], S, [6], out=T.AB[:], in_=T.pb6[:, 0:256], func=AF.Copy)
+    for h in range(NH):
+        A(["b6a"], ["th0_%d" % h], HS, [6], out=m0(T.M0_0, h, 2), in_=T.pb6[:, 256 + h * HS:256 + (h + 1) * HS], func=AF.Copy)
+
+    for j in range(8):
+        V("ts", ["ASI", "cH"], ["ASH"], W // 8, 1.0, out=T.ASH[:, j * 512:(j + 1) * 512], in0=T.ASI[:, j * 512:(j + 1) * 512],
+          scalar1=col(cH), scalar2=2.0 ** -17, op0=OP.add, op1=OP.mult)
+
+    def send(t, m, dst, src_ap, dst_ap, rd, wr, lat):
+        rid, pid, _s = topo.addr(dst)
+        mask = topo.mask(core, dst)
+        ne = len(topo.engines(core, dst))
+        rs, ls = "r%d_%s" % (t, m), "l%d_%s" % (t, m)
+        add("G", lambda: g.remote_dma(out_ap=dst_ap, in_ap=src_ap, remote_sem=T.sem[rs], local_sem=T.sem[ls], pid=pid, routing_id=rid, dma_engine_mask=mask),
+            rd, [], 700)
+        ops[-1]["remote"] = (ls, ne)
+        k = len(ops) - 1
+        add("N", None, [], wr, 0, sem=rs, val=ne, lat=lat)
+        ops[-1]["after"] = k
+
+    def gather(t, h, src16, dst, key, okey, vp):
+        npc = CFG["npc"]
+        step = HS // npc
+        for j in range(npc):
+            a = h * HS + j * step
+            offs = src16[:, a:a + step]
+            o = dst[:, 16 * a:16 * (a + step)]
+            n = 16 * step
+            if (h, j) in vp:
+                V("cp", ["X", okey + str(h)], [key + "%d%d" % (h, j)], n, GR, out=o, in_=T.X[:].indirect(offs))
+            else:
+                A(["X", okey + str(h)], [key + "%d%d" % (h, j)], n, (), 45, GR, out=o, in_=T.X[:].indirect(offs), func=AF.Copy)
+
+    ring = [0]
+
+    for t in range(RO):
+        hear = T.cores[(rank + DIST[t]) % N]
+        spk = T.cores[(rank - DIST[t]) % N]
+        M0, L0 = T["M0_%d" % t], T["L0_%d" % t]
+        M1, L1 = T["M1_%d" % t], T["L1_%d" % t]
+        NS, LN = T["NS_%d" % t], T["LN_%d" % t]
+        FF, LF = T["FF_%d" % t], T["LF_%d" % t]
+        last = t == RO - 1
+        cur_t[0] = t
+        for h in range(NH):
+            hs = str(h)
+            cur_h[0] = h
+            gather(t, h, T.C16, T.XG, "XG", "C16", CFG["vc"] if t else CFG["vc0"])
+            xgk = ["XG%d%d" % (h, j) for j in range(CFG["npc"])]
+
+            b4 = 4 + h
+            nq = CFG["nq"][h]
+            qs = HS // nq
+            npq = CFG["npc"] // nq
+            V("cp", xgk, ["x0_%d" % h], HS, 0.5, out=m0(M0, h, 0), in_=T.XG[:, h * 2048:(h + 1) * 2048:16])
+            for q in range(nq):
+                qk = xgk[q * npq:(q + 1) * npq]
+
+                def xg(k, h=h, q=q, qs=qs):
+                    return T.XG[:, h * 2048 + q * qs * 16 + k:h * 2048 + (q + 1) * qs * 16:16]
+
+                def dw(k, h=h, q=q, qs=qs):
+                    return T.DW[:, h * 2048 + k * 128 + q * qs:h * 2048 + k * 128 + (q + 1) * qs]
+                wq = M0[:, (3 * h + 1) * HS + q * qs:(3 * h + 1) * HS + (q + 1) * qs]
+                sk = T["pb%d" % b4][:, q * qs:(q + 1) * qs]
+                nk = 512 // qs
+                for c in range(16 // nk):
+                    ks = range(1 + nk * c, min(16, 1 + nk + nk * c))
+                    b = ring[0] % 4
+                    ring[0] += 1
+                    for s0 in range(0, len(ks), 4):
+                        lst = []
+                        for j in range(s0, min(s0 + 4, len(ks))):
+                            o = T["pb%d" % b][:, j * qs:(j + 1) * qs]
+                            lst.append((o, T.mI[:], xg(ks[j]), True, False, qs, False))
+                            lst.append((o, T.mNI[:], xg(0), False, True, qs, False))
+                        MM(lst, qk + ["mI", "mNI"], ["ring%d" % b], [b])
+                    for j, k in enumerate(ks):
+                        V("tt", ["ring%d" % b, "w%d_%d" % (t, h)], ["DW%d%d_%d" % (h, q, k)], qs, 1.0, [b],
+                          out=dw(k), in0=T["pb%d" % b][:, j * qs:(j + 1) * qs], in1=wq, op=OP.mult)
+                    MM([(sk, T.SEL[:, k * 128:(k + 1) * 128], dw(k), k == 1, k == 15, qs, False) for k in ks],
+                       allsel + ["DW%d%d_%d" % (h, q, k) for k in ks], ["Sk" + hs], [b4])
+            A(["Sk" + hs], ["ABS" + hs], HS, [b4], out=sl(T.AB1, h), in_=ps(b4, 0), func=AF.Abs)
+
+            def G(r, h=h):
+                return T.G[:, h * 2048 + r * 128:h * 2048 + (r + 1) * 128]
+            for r in range(16):
+                if r >= 16 - CFG["ns"][h]:
+                    A(["ABS" + hs, "thr%d" % r], ["G%d_%d" % (h, r)], HS, out=G(r), in_=sl(T.AB1, h), func=AF.Sign, bias=T.THC[:, r:r + 1])
+                else:
+                    V("ts", ["ABS" + hs], ["G%d_%d" % (h, r)], HS, 0.5, out=G(r), in0=sl(T.AB1, h), scalar1=0.6 * 2.0 ** (WT - 11 * r), scalar2=None, op0=OP.is_ge)
+                if r % 4 == 3:
+                    MM([(ps(b4, 1), cntm(q, h), G(q), q == 0, q == 15, HS, False) for q in range(r - 3, r + 1)],
+                       allcnt + ["CNH"] + ["G%d_%d" % (h, q) for q in range(r - 3, r + 1)], ["cnt" + hs], [b4])
+            c8 = T.COL2[:, h:h + 1]
+            if CFG["bitV"][h]:
+                V("ts", ["cnt" + hs, "c8" + hs], ["BIT" + hs], HS, 1.0, [b4], out=sl(T.BIT, h), in0=ps(b4, 1), scalar1=c8, scalar2=0.5, op0=OP.add, op1=OP.is_gt)
+            else:
+                A(["cnt" + hs, "c8" + hs], ["BIT" + hs], HS, [b4], out=sl(T.BIT, h), in_=ps(b4, 1), func=AF.Sign, bias=c8)
+            MM([(ps(b4, 0), T.mWB[:], T.ONES[:], True, False, HS, False), (ps(b4, 0), T.mNW[:], sl(T.BIT, h), False, True, HS, False)],
+               ["mNW", "mWB", "ONES", "BIT" + hs], ["Sk" + hs], [b4])
+            V("tt", ["Sk" + hs, "IW" + hs], ["TI" + hs], HS, 1.0, [b4], out=sl(T.TI, h), in0=ps(b4, 0), in1=sl(T.IW, h), op=OP.mult)
+            V("ts", ["TI" + hs], ["TJ" + hs], HS, 1.0, out=sl(T.TJ, h), in0=sl(T.TI, h), scalar1=32768, scalar2=None, op0=OP.bitwise_and)
+            V("tt", ["TJ" + hs, "x0_%d" % h], ["x0p%d" % h], HS, 2.0, out=sl(M1, h), in0=m0(M0, h, 0), in1=sl(T.TJ, h), op=OP.add)
+            send(t, "1%d" % h, hear, sl(M1, h), sl(L1, h), ["x0p%d" % h], ["L1" + hs], CFG["hop"])
+            MM([(ps(b4, 1), T.mI[:], sl(T.AB1, h), True, False, HS, False), (ps(b4, 1), T.mCW[:], sl(T.BIT, h), False, False, HS, False),
+                (ps(b4, 1), T.mKC[:], T.ONES[:], False, True, HS, False)], ["ABS" + hs, "mI", "mCW", "mKC", "ONES", "BIT" + hs], ["cnt" + hs, "dB" + hs], [b4])
+            V("ts", ["cnt" + hs], ["KAP" + hs], HS, 1.0, [b4], out=sl(T.KAP, h), in0=ps(b4, 1), scalar1=0.0, scalar2=8192.0, op0=OP.is_gt, op1=OP.mult)
+            MM([(ps(b4, 2), T.fI[:], sl(T.C, h), True, False, HS, True), (ps(b4, 2), T.mNI[:], sl(T.KAP, h), False, True, HS, False)],
+               ["fI", "mNI", "Cs" + hs, "KAP" + hs], ["q" + hs], [b4])
+            send(t, "0%d" % h, hear, M0[:, h * 3 * HS:(h + 1) * 3 * HS], L0[:, h * 3 * HS:(h + 1) * 3 * HS], ["x0_" + hs, "w%d_%d" % (t, h), "th%d_%d" % (t, h)], ["L0" + hs], CFG["hop"] + 200)
+        for h in range(NH):
+            cur_h[0] = h
+            gather(t, h, T.H16, T.YG, "YG", "H16", CFG["vh"])
+        for h in range(NH):
+            hs = str(h)
+            cur_h[0] = h
+            ygk = ["YG%d%d" % (h, j) for j in range(CFG["npc"])]
+            b6 = 6 + h
+            V("ts", ["L1" + hs], ["DSC" + hs], HS, 0.5, out=sl(T.DSC, h), in0=sl(L1, h), scalar1=1000.0, scalar2=None, op0=OP.is_lt)
+            lst = [(ps(b6, 3), T.mI[:], m0(L0, h, 1), True, True, HS, False)]
+            if not last:
+                lst.append((ps(b6, 2), T.mI[:], sl(L1, h), True, True, HS, False))
+                V("ts", ["L1" + hs], ["UND" + hs], HS, 0.5, out=sl(T.UND, h), in0=sl(L1, h), scalar1=1000.0, scalar2=None, op0=OP.is_gt)
+            MM(lst, ["mI", "L0" + hs, "L1" + hs], ["wc" + hs, "xc" + hs], [b6])
+            if not last:
+                V("tt", ["xc" + hs, "DSC" + hs], ["XD" + hs], HS, 1.0, [b6], out=sl(T.XD, h), in0=ps(b6, 2), in1=sl(T.DSC, h), op=OP.mult)
+            MM([(ps(b6, 0), T.fI[:], sl(T.HK, h), True, False, HS, True), (ps(b6, 0), T.mNB[:], sl(T.DSC, h), False, False, HS, False)],
+               ["fI", "mNB", "HK" + hs, "DSC" + hs], ["key" + hs], [b6])
+            for c in range(4):
+                b = ring[0] % 4
+                ring[0] += 1
+                ks = range(4 * c, 4 * c + 4)
+                byS = c >= 4 - CFG["es"][h]
+                lst = []
+                for j, k in enumerate(ks):
+                    lst.append((ps(b, j), T.mI[:], T.YG[:, h * 2048 + k:(h + 1) * 2048:16], True, not byS, HS, False))
+                    if byS:
+                        lst.append((ps(b, j), T.mNI[:], sl(L1, h), False, True, HS, False))
+                MM(lst, ygk + ["mI"] + (["mNI", "L1" + hs] if byS else []), ["ring%d" % b], [b])
+                if byS:
+                    A(["ring%d" % b], ["EA" + hs], 512, [b], out=T.EA[:, h * 512:(h + 1) * 512], in_=T["pb%d" % b][:, 0:512], func=AF.Abs)
+                    A(["EA" + hs], ["E%d_%d" % (h, k) for k in ks], 512, out=T.E[:, h * 2048 + c * 512:h * 2048 + (c + 1) * 512], in_=T.EA[:, h * 512:(h + 1) * 512],
+                      func=AF.Relu, scale=-1.0, bias=1.0)
+                for j, k in enumerate(ks if not byS else ()):
+                    V("tt", ["ring%d" % b, "L1" + hs], ["E%d_%d" % (h, k)], HS, 1.0, [b],
+                      out=T.E[:, h * 2048 + k * 128:h * 2048 + (k + 1) * 128], in0=ps(b, j), in1=sl(L1, h), op=OP.is_equal)
+                MM([(ps(b6, 0), T.SEL[:, k * 128:(k + 1) * 128], T.E[:, h * 2048 + k * 128:h * 2048 + (k + 1) * 128], False, k == 15, HS, False) for k in ks],
+                   allsel + ["E%d_%d" % (h, k) for k in ks], ["key" + hs], [b6])
+            V("tr", ["key" + hs], ["KT" + hs], HS, 1.0, [b6], out=sl(T.KT, h), in_=ps(b6, 0))
+            A(["key" + hs], ["KH" + hs], HS, [b6], out=sl(T.KH, h), in_=ps(b6, 0), func=AF.Relu, scale=-1.0)
+            V("scan", ["KT" + hs, "SD"], ["SC" + hs], HS, 1.0, out=sl(T.SC, h), data0=T.SD[:], data1=sl(T.KT, h), initial=-4096.0, op0=OP.add, op1=OP.max)
+            lst = []
+            for hh in range(2):
+                for g2 in range(2):
+                    lst.append((T["pb%d" % b6][:, 128 + hh:136:2], T.fP[:, (2 * hh + g2) * 128:(2 * hh + g2 + 1) * 128],
+                                T.SC[:, h * HS + g2 * 16 + 15:(h + 1) * HS:32], g2 == 0, g2 == 1, 4, True))
+            MM(lst, ["fP", "SC" + hs], ["mk" + hs], [b6])
+            ws = slice(8 * h, 8 * h + 8)
+            V("ts", ["mk" + hs], ["K32" + hs], 8, 1.0, [b6], out=T.K32[:, ws], in0=T["pb%d" % b6][:, 128:136], scalar1=131072.0, scalar2=None, op0=OP.mult)
+            V("ts", ["K32" + hs], ["N32" + hs], 8, out=T.N32[:, ws], in0=T.K32[:, ws], scalar1=4095, scalar2=None, op0=OP.bitwise_and)
+            V("cp", ["N32" + hs], ["NS" + hs], 8, out=NS[:, ws], in_=T.N32[:, ws])
+            send(t, "2%d" % h, spk, NS[:, ws], LN[:, ws], ["NS" + hs], ["LN" + hs], CFG["hop"] - 100)
+            V("ts", ["K32" + hs], ["KK" + hs], 8, out=T.KK[:, ws], in0=T.K32[:, ws], scalar1=12, scalar2=15, op0=OP.arith_shift_right, op1=OP.bitwise_and)
+            V("tt", ["KK" + hs, "CI"], ["OF" + hs], 8, out=T.OF[:, ws], in0=T.CI[:, 0:8], in1=T.KK[:, ws], op=OP.subtract)
+            V("cp", ["OF" + hs], ["OF16" + hs], 8, out=T.OF16[:, ws], in_=T.OF[:, ws])
+            ysrc = T.YG[:, h * 2048:(h + 1) * 2048].indirect(T.OF16[:, ws])
+            if not last:
+                V("tt", ygk + ["OF16" + hs, "UND" + hs], ["YU" + hs], HS, GR, (), 40, out=sl(T.YU, h), in0=ysrc, in1=sl(T.UND, h), op=OP.mult)
+            V("tt", ygk + ["OF16" + hs, "L0" + hs], ["DM" + hs], HS, GR, (), 40, out=sl(T.DM, h), in0=ysrc, in1=m0(L0, h, 0), op=OP.not_equal)
+            V("tt", ["wc" + hs, "DM" + hs], ["DMW" + hs], HS, 1.0, [b6], out=sl(T.DMW, h), in0=ps(b6, 3), in1=sl(T.DM, h), op=OP.mult)
+            MM([(ps(b6, 2), T.mNB[:], sl(T.DM, h), True, False, HS, False), (ps(b6, 2), T.mI[:], m0(L0, h, 2), False, True, HS, False),
+                (ps(b6, 3), T.mTB[:], sl(T.DMW, h), True, True, HS, False)], ["mNB", "mI", "mTB", "DM" + hs, "DMW" + hs, "L0" + hs], ["tt" + hs, "wc" + hs, "xc" + hs], [b6])
+            A(["tt" + hs, "bias"], ["TH" + hs], HS, [b6], out=sl(T.TH, h), in_=ps(b6, 2), func=AF.Relu, scale=2.0 ** 96, bias=col(13))
+            V("tt", ["tt" + hs, "TH" + hs], ["FF%d_%d" % (t, h)], HS, 1.0, [b6], out=sl(FF, h), in0=ps(b6, 3), in1=sl(T.TH, h), op=OP.is_gt)
+            send(t, "3%d" % h, spk, sl(FF, h), sl(LF, h), ["FF%d_%d" % (t, h)], ["LF%d_%d" % (t, h)], CFG["hop"])
+        if not last:
+            for h in range(NH):
+                hs = str(h)
+                cur_h[0] = h
+                V("tt", ["YU" + hs, "XD" + hs, "OF16" + hs], ["X"], HS, 3.5, (), 40, out=T.X[:, h * 2048:(h + 1) * 2048].indirect(T.OF16[:, 8 * h:8 * h + 8]),
+                  in0=sl(T.YU, h), in1=sl(T.XD, h), op=OP.add)
+        for h in range(NH):
+            hs = str(h)
+            cur_h[0] = h
+            b4, b6 = 4 + h, 6 + h
+            ws = slice(8 * h, 8 * h + 8)
+            V("tt", ["ASI", "LN" + hs, "KAP" + hs], ["CM" + hs], HS, 1.5, (), 40, out=sl(T.CM, h), in0=T.ASI[:].indirect(LN[:, ws]), in1=sl(T.KAP, h), op=OP.min)
+            V("tt", ["CM" + hs, "q" + hs], ["Cs" + hs], HS, 1.0, [b4], out=sl(T.C, h), in0=ps(b4, 2), in1=sl(T.CM, h), op=OP.max)
+            if not last:
+                V("cp", ["Cs" + hs], ["C16" + hs], HS, 1.0, out=sl(T.C16, h), in_=sl(T.C, h))
+            V("tt", ["ASH", "NS" + hs, "KH" + hs], ["HM" + hs], HS, 1.5, (), 40, out=sl(T.HM, h), in0=T.ASH[:].indirect(NS[:, ws]), in1=sl(T.KH, h), op=OP.min)
+            V("tt", ["HM" + hs, "key" + hs], ["HK" + hs], HS, 1.0, [b6], out=sl(T.HK, h), in0=ps(b6, 0), in1=sl(T.HM, h), op=OP.max)
+            if not last:
+                V("ts", ["HK" + hs, "cH"], ["H16" + hs], HS, 1.0, out=sl(T.H16, h), in0=sl(T.HK, h), scalar1=131072.0, scalar2=col(cH), op0=OP.mult, op1=OP.subtract)
+            else:
+                V("ts", ["HK" + hs, "cH"], ["OH" + hs], HS, 1.0, out=sl(T.OH, h), in0=sl(T.HK, h), scalar1=131072.0, scalar2=col(cH), op0=OP.mult, op1=OP.subtract)
+            if t == 0:
+                MM([(ps(b4, 3), T.mI[:], sl(T.R, h), True, True, HS, False)], ["mI", "Rs" + hs], ["t2" + hs], [b4])
+            cur, ck, pc, pk = T.R, "Rs" + hs, 3, "t2" + hs
+            for role, (f, fk) in enumerate([(LF, "LF%d_%d" % (t, h)), (FF, "FF%d_%d" % (t, h))]):
+                V("tt", [pk, fk], ["MA" + hs], HS, 1.0, [b4], out=sl(T.MA, h), in0=ps(b4, pc), in1=sl(f, h), op=OP.mult)
+                MM([(ps(b4, 1), T.mB[:], sl(T.MA, h), True, True, HS, False)], ["mB", "MA" + hs], ["cnt" + hs, "dB" + hs], [b4])
+                V("tt", [ck, "cnt" + hs], ["LA" + hs], HS, 1.0, [b4], out=sl(T.LA, h), in0=ps(b4, 1), in1=sl(cur, h), op=OP.is_gt)
+                nc, nk = (2, "q" + hs) if role == 0 else (3, "t2" + hs)
+                MM([(ps(b4, nc), T.mI[:], sl(cur, h), True, False, HS, False), (ps(b4, nc), T.mNI[:], sl(T.MA, h), False, False, HS, False),
+                    (ps(b4, nc), T.mI[:], sl(T.LA, h), False, True, HS, False)], ["mI", "mNI", ck, "MA" + hs, "LA" + hs], [nk], [b4])
+                if role == 0:
+                    A([nk], ["Rq" + hs], HS, [b4], out=sl(T.R1, h), in_=ps(b4, nc), func=AF.Copy)
+                    cur, ck = T.R1, "Rq" + hs
+                elif not last:
+                    orders(h, t + 1, ps(b4, nc), [nk], [b4])
+                    A([nk], ["Rs" + hs], HS, [b4], out=sl(T.R, h), in_=ps(b4, nc), func=AF.Copy)
+                else:
+                    A([nk], ["OR" + hs], HS, [b4], out=sl(T.OR, h), in_=ps(b4, nc), func=AF.Copy)
+                pc, pk = nc, nk
+            lfs = ["LF%d_%d" % (u, h) for u in range(t + 1)]
+            if not last:
+                q0, qk = m0(M0, h, 2), "th%d_%d" % (t, h)
+                MM([(ps(b6, 1), T.mI[:], q0, True, False, HS, False), (ps(b6, 1), T.mB[:], sl(LF, h), False, True, HS, False)], ["mI", "mB", qk, lfs[t]], ["mk" + hs], [b6])
+                V("ts", ["mk" + hs], ["IND" + hs], HS, 1.0, [b6], out=sl(T.IND, h), in0=ps(b6, 1), scalar1=3.5, scalar2=-4.0, op0=OP.is_gt, op1=OP.mult)
+                MM([(ps(b6, 2), T.mI[:], q0, True, False, HS, False), (ps(b6, 2), T.mB[:], sl(LF, h), False, False, HS, False), (ps(b6, 2), T.mI[:], sl(T.IND, h), False, True, HS, False)],
+                   ["mI", "mB", qk, lfs[t], "IND" + hs], ["tt" + hs, "xc" + hs], [b6])
+                A(["tt" + hs], ["th%d_%d" % (t + 1, h)], HS, [b6], out=m0(T["M0_%d" % (t + 1)], h, 2), in_=ps(b6, 2), func=AF.Copy)
+            else:
+                MM([(ps(b6, 1), T.mI[:], sl(T.AB, h), True, False, HS, False)] + [(ps(b6, 1), T.mB[:], sl(T["LF_%d" % u], h), False, u == t, HS, False) for u in range(t + 1)],
+                   ["mI", "mB", "AB"] + lfs, ["mk" + hs], [b6])
+                A(["mk" + hs], ["OA" + hs], HS, [b6], out=sl(T.OA, h), in_=ps(b6, 1), func=AF.Copy)
+
+    def store(i, q, dst, src, rd):
+        e = g.sync if q == "Y" else g.scalar
+        add(q, lambda: e.dma_start(out=dst, in_=src), rd, ["out%d" % i], 60, sem="st_%d" % i, val=16, lat=2000)
+    for h in range(NH):
+        store(h, "Y", sl(T.yctx, h), sl(T.C, h), ["Cs%d" % h])
+        store(2 + h, "Y", sl(T.ycand, h), sl(T.OH, h), ["OH%d" % h])
+        store(4 + h, "Y", sl(T.ypref, h), sl(T.OR, h), ["OR%d" % h])
+        store(6 + h, "Y", sl(T.yfail, h), T.OA[0:128:16, h * HS:(h + 1) * HS], ["OA%d" % h])
+    return ops
+
+
+def depend(ops):
+    lastw, readers, lastb = {}, {}, {}
+    deps = []
+    for i, o in enumerate(ops):
+        d = {}
+        for k in o["rd"]:
+            for w in lastw.get(k, ()):
+                d[w] = True
+        for k in o["wr"]:
+            for w in lastw.get(k, ()):
+                d[w] = True
+            for r in readers.get(k, ()):
+                if r != i:
+                    d[r] = True
+        for b in o["bk"]:
+            if b in lastb:
+                d.setdefault(lastb[b], False)
+        if "after" in o:
+            d[o["after"]] = True
+        deps.append(d)
+        for k in o["rd"]:
+            readers.setdefault(k, []).append(i)
+        for k in o["wr"]:
+            lastw[k] = [i]
+            readers[k] = []
+        for b in o["bk"]:
+            lastb[b] = i
+    return deps
+
+
+BIAS = {'SYG1': -7000, 'Gsnd0': -8000, 'Gsnd1': -8000, 'VSC0': 40000, 'VSC1': 20000, 'VX1': 20000, 'VX0': 20000, 'SG1': -4000, 'VXD0': 20000, 'VMA0': -1000, 'Sw0': 23000, 'SIW0': 17000, 'SIW1': 17000, 'VN0': 2000, 'VN1': 1000, 'SABS0': -2000, 'SABS1': -2000, 'VASH0': 1000, 'VH0': 3000, 'VTMP0': 6000, 'Tkey1': -2000, 'VTJ0': 20000, 'VTJ1': 20000, 'YFIN0': 8000, 'YFIN1': 8000, 'SG0': -3000, 'VXG0': 1000, 'VKT1': 1000, 'VMK0': 8000, 'VMK1': 8000, 'VMA1': 1000, 'Tmk0': -2000, 'Tmk1': -1000, 'SRs0': 8000, 'VTI1': 1000, 'VmKC0': 8000, 'VmKC1': 8000, 'Twc0': 3000, 'VDSC0': 1000, 'VcKC0': 20000, 'VcKC1': 20000, 'VCNT0': -1000, 'VCNT1': -1000, 'NLF0': -17000, 'NLF1': -20000, 'Tq1': -3000, 'Tq0': -3000, 'SE0': -20000, 'Sw1': -6000, 'NLN1': -1000, 'SYG0': -2000, 'Vx0p1': 3000, 'Vx0p0': 3000, 'VmI0': 3000, 'VmI1': 3000, 'Tkey0': 1000, 'STH1': -12000, 'STH0': -9000, 'VOF1': -1000, 'Tring0': -2000, 'VDSC1': 3000, 'VHM0': 20000, 'VK1': -3000, 'SRq0': 48000, 'SX0': -20000, 'SX1': -20000, 'VUND0': -1000, 'VUND1': -1000, 'VIND0': 1000, 'VKT0': 20000, 'SOR1': -20000, 'SOR0': -20000, 'Tring1': -1000, 'SRq1': 28000, 'VKK1': 20000, 'VHM1': -3000, 'GIMK0': -8000, 'VTMP1': 9000, 'VHK0': 20000, 'VHK1': 20000, 'Tt0': 20000, 'Tt1': 20000, 'VLA1': 22000, 'SEA1': 1000, 'GCII0': 8000, 'VLA0': 2000, 'Vbias0': 8000, 'VDMW1': 3000, 'VcPm0': 8000, 'VcPm1': 8000, 'VKAP1': 3000, 'Vc16P0': -1000, 'Vc16P1': -1000, 'VFF0': 3000, 'VYU0': -1000}
+
+
+def klass(o):
+    w = o["wr"][0] if o["wr"] else "snd" + o["remote"][0].split("_")[1][0]
+    a = w.split("_")[0]
+    while a and a[-1].isdigit():
+        a = a[:-1]
+    return "%s%s%d" % (o["q"], a, o["h"])
+
+
+def schedule(ops, deps):
+    n = len(ops)
+    succ = [[] for _ in range(n)]
+    for i, d in enumerate(deps):
+        for j in d:
+            succ[j].append(i)
+    WAKE, alpha, win = CFG["wake"], CFG["alpha"], CFG["win"]
+    prio = [0.0] * n
+    for i in range(n - 1, -1, -1):
+        m = 0.0
+        for j in succ[i]:
+            m = max(m, prio[j] + (WAKE if ops[j]["q"] != ops[i]["q"] else 30.0))
+        prio[i] = m + ops[i]["cost"] + ops[i]["lat"]
+    for i in range(n):
+        if ops[i]["h"] == 0:
+            prio[i] += CFG["bonus"]
+        prio[i] += BIAS.get(klass(ops[i]), 0.0)
+    left = [len(d) for d in deps]
+    ready = [0.0] * n
+    fin = [0.0] * n
+    beg = [0.0] * n
+    avail = {}
+    free = {}
+    for i in range(n):
+        avail.setdefault(ops[i]["q"], [])
+        free.setdefault(ops[i]["q"], 0.0)
+        if left[i] == 0:
+            avail[ops[i]["q"]].append(i)
+    order = []
+    while True:
+        best = None
+        for q in avail:
+            if not avail[q]:
+                continue
+            fq = free[q] if q != "N" else 0.0
+            est = min(max(fq, ready[i]) for i in avail[q])
+            i, top = None, None
+            for z in avail[q]:
+                zs = max(fq, ready[z])
+                if zs <= est + win:
+                    sc = prio[z] - alpha * (zs - est)
+                    if top is None or sc > top:
+                        i, top = z, sc
+            st = max(fq, ready[i])
+            if best is None or st < best[0]:
+                best = (st, i, q)
+        if best is None:
+            break
+        st, i, q = best
+        avail[q].remove(i)
+        order.append(i)
+        beg[i] = st
+        free[q] = st + ops[i]["cost"]
+        fin[i] = st + ops[i]["cost"] + ops[i]["lat"]
+        for j in succ[i]:
+            ready[j] = max(ready[j], fin[i] + (WAKE if ops[j]["q"] != q else (30.0 if deps[j][i] else 0.0)))
+            left[j] -= 1
+            if left[j] == 0:
+                avail[ops[j]["q"]].append(j)
+    return order, beg, fin
+
+
+def rank_program(g, core, T, topo):
+    rank = T.rank_of(core)
+    if rank is None:
+        return
+    ops = build(g, T, topo, rank, core)
+    deps = depend(ops)
+    if "o" not in _ORDER:
+        _ORDER["o"] = schedule(ops, deps)[0]
+    order = _ORDER["o"]
+    eng = {"V": g.vector, "S": g.scalar, "T": g.tensor, "G": g, "Y": g.sync}
+    cnt = {}
+    done = {}
+    clock = {}
+    know = {q: {} for q in "VSTGY"}
+    for i in order:
+        o = ops[i]
+        q = o["q"]
+        if q == "N":
+            done[i] = (o["sem"], o["val"])
+            clock[i] = {o["sem"]: o["val"]}
+            cnt[o["sem"]] = o["val"]
+            continue
+        need = {}
+        for d, raw in deps[i].items():
+            od = ops[d]
+            if od["q"] == q and od["sem"] is None and (not raw or q in "TG"):
+                if not (q == "G"):
+                    continue
+                continue
+            s, v = done[d]
+            if know[q].get(s, 0) < v and (s not in need or need[s][0] < v):
+                need[s] = (v, d)
+        for s in list(need):
+            v, d = need[s]
+            for s2 in need:
+                if s2 != s and clock[need[s2][1]].get(s, 0) >= v:
+                    del need[s]
+                    break
+        for s in need:
+            v, d = need[s]
+            eng[q].wait_ge(T.sem[s], v)
+            for k, x in clock[d].items():
+                if know[q].get(k, 0) < x:
+                    know[q][k] = x
+        ins = o["fn"]()
+        if "remote" in o:
+            cnt[o["remote"][0]] = o["remote"][1]
+            done[i] = None
+            continue
+        s = o["sem"] or "s" + q
+        inc = o["val"] if o["sem"] else 1
+        ins.then_inc(T.sem[s], inc)
+        cnt[s] = cnt.get(s, 0) + inc
+        done[i] = (s, cnt[s])
+        c = dict(know[q])
+        c[s] = cnt[s]
+        if o["sem"] is None:
+            know_self = c
+        clock[i] = c
+    for s in cnt:
+        if know["G"].get(s, 0) < cnt[s]:
+            g.wait_ge(T.sem[s], cnt[s])

@@ -10,44 +10,55 @@ NH = 2
 HS = S // NH
 LN2 = math.log(2.0)
 WT = 85
+U = 65536.0
 CFG = {"npc": 4,
-       "vc": ((0, 3),),
-       "vc0": ((0, 3),),
+       "vc": ((0, 1),),
+       "vc0": ((0, 1), (0, 3)),
        "vh": (),
-       "ns": (4, 4),
-       "es": (1, 1),
-       "nq": (1, 1),
-       "bitV": (1, 1), "alpha": 20.0, "win": 300.0,
-       "bonus": 1500.0, "g": 1.5, "f": 1.2, "ov": 12.0, "wake": 120.0, "hop": 2000.0}
+       "ns": (0, 0),
+       "es": (0, 0),
+       "nq": (2, 1),
+       "bitV": (1, 1)}
+COST = {"cy": 1.0, "g": 1.5, "sc": 3.5, "ovV": 12.0, "ovS": 40.0, "pe": 0.51, "ovT": 20.0, "wake": 120.0, "self": 40.0, "issue": 700.0, "hop": 2000.0, "dma": 1.0}
+PERIOD = 20000.0
+OFF = {_a.split(":")[0]: float(_a.split(":")[1]) for _a in """
+DW3A:-23230 dx2A:-14900 DW0A:-13545 dx1A:-10886 UNDB:-10371 DSCA:-9718 DW1A:-8670 G0A:-6534 N32A:-6519 dx3A:-6242 sk3A:-6101 wordA:-5862 sk4A:-5804 DW6A:-5704 cnt0A:-5186 ABSA:-4432 G2A:-3850 DW2A:-3792 TIA:-3131 sk2A:-2716 DW7A:-2456 TJA:-1046 key0A:-1036 dx0B:-893 dx7A:-562 sk7A:-429 dx5A:56 E3B:474 x0pB:489 x0pA:662 BITB:722 XG1A:727 RMA:775 ABSB:867 XG0A:1080 cnt3A:1126 G1A:1226 sk0A:1321 dx2B:1401 DW4A:1505 XG3A:1664 send1A:2090 XG2A:2270 ndA:2356 G0B:2496 G2B:2513 E1B:2554 dx0A:2671 XG1B:2735 dx1B:2786 YUB:2827 DW0B:2843 key0B:2856 G3A:3378 FFB:3395 KHA:3711 send2A:3755 LBB:3978 DW5A:4115 cnt1A:4305 sk6A:4562 dx4A:4598 G1B:4646 DW3B:4650 cnt3B:4675 khB:4676 E2B:4681 dx6A:4745 sk1A:4753 sk5A:4822 cnt2A:4882 XG0B:4887 C16B:5010 wB:5139 xbA:5171 XG3B:5197 TJB:5270 K32A:5322 BITA:5322 sk3B:5459 DW2B:5472 N32B:5591 G3B:5639 DW1B:5791 x0A:6035 dx3B:6138 YG0B:6178 mkB:6205 ndB:6244 XG2B:6309 DSCB:6377 qA:6760 dBB:7123 sk2B:7230 UNDA:7984 wcA:8010 NSB:8126 SGA:8140 KKA:8273 KKB:8405 wordB:8819 sk1B:8884 sk0B:9088 send1B:9095 zB:9176 YG2A:9315 uA:9577 key2A:9686 send0B:9697 MBA:10018 E1A:10219 dBA:10387 x0B:10534 YG1A:11012 HsA:11044 DMA:11054 E0A:11189 KTB:11484 YG0A:11992 YG3A:12060 mkA:12076 cnt2B:12371 xbB:12484 YG3B:12494 TIB:12994 key3A:13077 E0B:13159 cnt1B:13428 wcB:13614 CsB:13909 LBA:13973 FFA:13979 E2A:14039 RMB:14075 cnt0B:14207 xpA:14259 K32B:14284 ttA:14292 IWA:14389 NSA:14422 OFA:14840 SCA:14867 YUA:14875 H16A:15146 YG2B:15304 KTA:15529 r2A:15650 key2B:15980 r1B:16147 YG1B:16238 THB:16317 key3B:16379 aB:16401 H16B:16406 r2B:16502 DMB:16679 uB:16725 xpB:16934 khA:16935 key1A:17150 E3A:17163 CsA:17401 key1B:17444 CMB:17514 ttB:17536 DMWA:18081 SCB:18496 XDA:19051 send3A:19116 MAA:19416 PUTB:19487 PUTA:19540 THA:19755 IWB:20130 LAA:20132 OFB:20134 MBB:20231 LAB:20249 SGB:20291 CMA:20358 r1A:20359 bA:20398 aA:20438 rmB:20538 C16A:20542 zA:20594 XDB:20842 rmA:20917 bB:21439 thB:21478 DMWB:21478 qB:21863 wA:22018 thA:23025 MAB:24069 RsA:24194 RsB:24327 send2B:25729 send3B:26436 HMA:26503 KHB:27771 HMB:29276 HsB:35289
+""".split()}
 
 SCRATCH = {}
 for _n, _s, _d in [
-    ("X", [128, W], "bfloat16"), ("ASI", [128, W], "int32"), ("ASH", [128, W], "float32"),
+    ("X", [128, W], "bfloat16"), ("ASI", [128, W], "int32"),
     ("XG", [128, W], "bfloat16"), ("YG", [128, W], "bfloat16"), ("DW", [128, W], "bfloat16"), ("E", [128, W], "bfloat16"), ("G", [128, W], "bfloat16"),
     ("CIN", [128, S], "int32"), ("HIN", [128, S], "int32"), ("RIN", [128, S], "int32"), ("FIN", [8, S], "int32"), ("Q8I", [8, S], "int32"),
-    ("A8", [8, S], "bfloat16"), ("Q8", [8, S], "bfloat16"), ("AB", [128, S], "bfloat16"), ("IND", [128, S], "bfloat16"),
-    ("C", [128, S], "float32"), ("C16", [128, S], "uint16"), ("HK", [128, S], "float32"), ("H16", [128, S], "uint16"),
-    ("R", [128, S], "bfloat16"), ("R1", [128, S], "bfloat16"), ("MA", [128, S], "bfloat16"), ("LA", [128, S], "bfloat16"), ("IW", [128, S], "bfloat16"),
-    ("AB1", [128, S], "bfloat16"), ("BIT", [128, S], "bfloat16"), ("TI", [128, S], "int32"), ("TJ", [128, S], "int32"), ("KAP", [128, S], "bfloat16"),
+    ("A8", [8, S], "bfloat16"), ("Q8", [8, S], "bfloat16"),
+    ("C", [128, S], "float32"), ("C16", [128, S], "uint16"), ("H", [128, S], "float32"), ("H16", [128, S], "uint16"),
+    ("R", [128, S], "bfloat16"), ("RM", [128, S], "bfloat16"), ("MA", [128, S], "bfloat16"), ("LA", [128, S], "bfloat16"),
+    ("MB", [128, S], "bfloat16"), ("LB", [128, S], "bfloat16"), ("IW", [128, S], "bfloat16"),
+    ("AB1", [128, S], "bfloat16"), ("BIT", [128, S], "bfloat16"), ("TI", [128, S], "int32"), ("TJ", [128, S], "int32"), ("SG", [128, S], "bfloat16"),
     ("CM", [128, S], "float32"), ("KH", [128, S], "float32"), ("HM", [128, S], "float32"), ("UND", [128, S], "bfloat16"), ("DSC", [128, S], "bfloat16"),
     ("XD", [128, S], "bfloat16"), ("YU", [128, S], "bfloat16"), ("KT", [128, S], "float32"), ("SC", [128, S], "float32"),
-    ("K32", [128, 16], "int32"), ("N32", [128, 16], "int32"), ("KK", [128, 16], "int32"), ("OF", [128, 16], "int32"), ("OF16", [128, 16], "uint16"),
+    ("RND", [128, S], "float32"), ("MS", [128, S], "bfloat16"),
+    ("K32", [128, 16], "int32"), ("N32", [128, 16], "int32"), ("KK", [128, 16], "int32"), ("OF16", [128, 16], "uint16"),
     ("DM", [128, S], "bfloat16"), ("DMW", [128, S], "bfloat16"), ("TH", [128, S], "float32"),
-    ("OC", [128, S], "float32"), ("OH", [128, S], "float32"), ("OR", [128, S], "float32"), ("OA", [128, S], "float32"),
-    ("IP", [128, 1], "int32"), ("KI", [128, 1], "int32"), ("B4I", [128, 1], "int32"), ("COL", [128, 16], "float32"), ("COL2", [128, 2], "float32"), ("EA", [128, 1024], "bfloat16"), ("CNH", [128, 1024], "bfloat16"), ("THC", [128, 16], "float32"), ("COLB", [128, 2], "bfloat16"),
-    ("IM", [128, 128], "float32"), ("IMG", [128, 128], "float32"), ("IMK", [128, 128], "float32"), ("IMB", [128, 128], "bfloat16"),
-    ("SEL", [128, 2048], "bfloat16"), ("CNT", [128, 2048], "bfloat16"),
-    ("mB", [128, 128], "bfloat16"), ("mI", [128, 128], "bfloat16"), ("mNI", [128, 128], "bfloat16"), ("mNB", [128, 128], "bfloat16"),
-    ("mTB", [128, 128], "bfloat16"), ("mWB", [128, 128], "bfloat16"), ("mCW", [128, 128], "bfloat16"), ("mKC", [128, 128], "bfloat16"),
-    ("mNW", [128, 128], "bfloat16"), ("m4", [128, 128], "bfloat16"), ("ONES", [128, 128], "bfloat16"), ("mI2", [128, 128], "bfloat16"), ("TMP", [128, 128], "float32"), ("MK0", [128, 128], "float32"),
-    ("fI", [128, 128], "float32"), ("fP", [128, 512], "float32"), ("SD", [128, 128], "float32"), ("CII", [128, 16], "int32"), ("CI", [128, 16], "int32"),
+    ("OR", [128, S], "float32"), ("OA", [8, S], "float32"),
+    ("IP", [128, 1], "int32"), ("KI", [128, 1], "int32"), ("B4I", [128, 1], "int32"), ("COL", [128, 24], "float32"), ("THC", [128, 16], "float32"), ("COLB", [128, 2], "bfloat16"),
+    ("IM", [128, 160], "bfloat16"), ("IMG", [128, 128], "bfloat16"), ("IMK", [128, 128], "bfloat16"),
+    ("Z", [128, 144], "bfloat16"), ("ZU", [128, 144], "bfloat16"), ("Z1", [128, 144], "bfloat16"), ("ZD", [128, 144], "bfloat16"), ("ZH", [128, 144], "bfloat16"), ("ZDH", [128, 144], "bfloat16"),
+    ("mB", [128, 128], "bfloat16"), ("mI", [128, 128], "bfloat16"), ("mNI", [128, 128], "bfloat16"), ("mNB", [128, 128], "bfloat16"), ("mNBU", [128, 128], "bfloat16"),
+    ("mTB", [128, 128], "bfloat16"), ("mWB", [128, 128], "bfloat16"), ("mCW", [128, 128], "bfloat16"),
+    ("mIB", [128, 128], "bfloat16"), ("mBI", [128, 128], "bfloat16"), ("mN16", [128, 128], "bfloat16"), ("mN4k", [128, 128], "bfloat16"), ("mU", [128, 128], "bfloat16"),
+    ("mTH", [128, 128], "bfloat16"), ("mZ0", [128, 128], "bfloat16"),
+    ("ONES", [128, 128], "bfloat16"), ("BIG", [128, 128], "bfloat16"), ("mI2", [128, 128], "bfloat16"), ("TMP", [128, 128], "bfloat16"), ("MK0", [128, 128], "bfloat16"),
+    ("fI", [128, 128], "float32"), ("fP", [128, 512], "float32"), ("SD", [128, 128], "float32"), ("CB", [128, 8], "float32"), ("CBI", [128, 8], "float32"),
     ("mG8", [8, 128], "bfloat16"),
 ]:
     SCRATCH[_n] = ("sbuf", _s, _d)
+for _n in ("FF", "LF"):
+    SCRATCH[_n] = ("sbuf", [128, RO * S], "bfloat16")
 for _t in range(RO):
     SCRATCH["M0_%d" % _t] = ("sbuf", [128, 3 * S], "bfloat16")
     SCRATCH["L0_%d" % _t] = ("sbuf", [128, 3 * S], "bfloat16")
-    for _n in ("M1_", "L1_", "FF_", "LF_"):
+    for _n in ("M1_", "L1_"):
         SCRATCH[_n + str(_t)] = ("sbuf", [128, S], "bfloat16")
     for _n in ("NS_", "LN_"):
         SCRATCH[_n + str(_t)] = ("sbuf", [128, 16], "uint16")
@@ -55,52 +66,53 @@ for _b in range(8):
     SCRATCH["pb%d" % _b] = ("psum", [128, 512], "float32")
 
 SEMAPHORES = ["sT", "sV", "sS", "sG"]
-SEMAPHORES += ["ld_%s" % _n for _n in ("x", "ctx", "cand", "pref", "assoc", "fail0")] + ["st_%d" % _i for _i in range(12)]
+SEMAPHORES += ["ld_%s" % _n for _n in ("x", "ctx", "cand", "pref", "assoc", "fail0")] + ["st_%d" % _i for _i in range(8)]
 for _t in range(RO):
-    for _m in ("00", "01", "10", "11", "20", "21", "30", "31"):
+    for _m in ("0", "10", "11", "20", "21", "30", "31"):
         SEMAPHORES += ["r%d_%s" % (_t, _m), "l%d_%s" % (_t, _m)]
 
-cP, cK, cG16, cPp, cPm, cS0, cS1, cKC, c16K, cH, c16P = range(11)
+cP, cK, cG16, cZ, cZ1, cPp, cPm, cS0, cS1, cKC, cOF, c16P, cW, cT, cE, cTH, cQa, cQb, cQ, cK0, c80, c81 = range(22)
 
 _ORDER = {}
 
 
-PER_ROUND = ("L10", "L11", "L00", "L01", "NS0", "NS1", "LN0", "LN1", "x0_0", "x0_1", "x0p0", "x0p1")
-
-
 def build(g, T, topo, rank, core):
     ops = []
-    cur_t = [0]
-    cur_h = [0]
-    GR = CFG["g"]
+    at = {"t": -1, "h": 0}
 
-    def key(k):
-        return k + "_r%d" % cur_t[0] if k in PER_ROUND else k
+    def add(q, name, fn, rd, wr, cost, banks=(), sem=None, val=1, lat=None):
+        ops.append({"q": q, "name": name + "AB"[at["h"]], "fn": fn, "rd": list(rd), "wr": list(wr), "bk": list(banks), "cost": cost,
+                    "sem": sem, "val": val, "lat": lat, "t": at["t"]})
 
-    def add(q, fn, rd, wr, cost, banks=(), sem=None, val=1, lat=0.0):
-        ops.append({"q": q, "fn": fn, "rd": [key(k) for k in rd], "wr": [key(k) for k in wr], "bk": list(banks), "cost": cost, "sem": sem, "val": val, "lat": lat,
-                    "h": cur_h[0], "t": cur_t[0]})
-
-    CY = 0.83 * CFG["f"]
-
-    def vcost(n, rate=1.0):
-        return max(64, n * rate) * CY + CFG["ov"]
-
-    def V(name, rd, wr, n, rate=1.0, banks=(), extra=0.0, **kw):
+    def V(name, call, rd, wr, n, rate=1.0, banks=(), **kw):
         f = {"tt": g.vector.tensor_tensor, "ts": g.vector.tensor_scalar, "cp": g.vector.tensor_copy, "tr": g.vector.transpose,
-             "scan": g.vector.tensor_tensor_scan}[name]
-        add("V", lambda: f(**kw), rd, wr, vcost(n, rate) + extra, banks)
+             "scan": g.vector.tensor_tensor_scan}[call]
+        add("V", name, lambda: f(**kw), rd, wr, (n, rate), banks)
 
-    def A(rd, wr, n, banks=(), extra=0.0, rate=1.0, **kw):
-        add("S", lambda: g.scalar.activation(**kw), rd, wr, n * rate * CY + 20 + extra, banks)
+    def join(m):
+        part = ops[-m:]
+        del ops[-m + 1:]
+        o = ops[-1]
+        for p in part[1:]:
+            o["rd"] += p["rd"]
+            o["wr"] += p["wr"]
+        o["more"] = [p["fn"] for p in part[1:]]
 
-    def MM(lst, rd, wr, banks):
+    def fill(key, ap, c, n=1):
+        add("V", key, lambda: g.vector.memset(ap, c), [], [key], (n, 0.5))
+
+    def A(name, rd, wr, n, banks=(), rate=1.0, **kw):
+        add("S", name, lambda: g.scalar.activation(**kw), rd, wr, (n, rate), banks)
+
+    def MM(name, lst, rd, wr, bank):
         def fn():
             ins = None
             for o, l, r, a, b, n, f in lst:
                 ins = g.tensor.matmul(out=o, lhsT=l, rhs=r, start=a, stop=b)
             return ins
-        add("T", fn, rd, wr, sum(max(64, n) * (4 if f else 1) * 0.42 * 1.22 for o, l, r, a, b, n, f in lst) + 20, banks)
+        whole = lst[0][3] and lst[-1][4]
+        lock = ["bank%d" % bank]
+        add("T", name, fn, rd + (lock if whole else []), wr + ([] if whole else lock), sum(max(64, n) * (4 if f else 1) for o, l, r, a, b, n, f in lst), [bank])
 
     def col(i):
         return T.COL[:, i:i + 1]
@@ -114,16 +126,19 @@ def build(g, T, topo, rank, core):
     def ps(b, r):
         return T["pb%d" % b][:, r * 128:(r + 1) * 128]
 
+    def sel(z, k):
+        return z[:, 15 - k:143 - k]
+
     def ldw(q, semn, key, dst, src, lat):
         e = g.sync if q == "Y" else g.scalar
-        add(q, lambda: e.dma_start(out=dst, in_=src), [], [key], 60, sem="ld_" + semn, val=16, lat=lat)
+        add(q, "ld" + key, lambda: e.dma_start(out=dst, in_=src), [], [key], "dma", sem="ld_" + semn, val=16, lat=lat)
 
-    ldw("Y", "ctx", "CIN", T.CIN[:], T.ctx[:], 2200)
     ldw("S", "x", "X", T.X[:], T.x[:], 4500)
+    ldw("Y", "ctx", "CIN", T.CIN[:], T.ctx[:], 2200)
     ldw("Y", "pref", "RIN", T.RIN[:], T.pref[:], 2300)
-    ldw("Y", "cand", "HIN", T.HIN[:], T.cand[:], 2400)
     ldw("Y", "fail0", "FIN", T.FIN[:], T.fail0[:], 2400)
-    ldw("S", "assoc", "ASI", T.ASI[:], T.assoc[:], 6500)
+    ldw("Y", "cand", "HIN", T.HIN[:], T.cand[:], 2400)
+    ldw("Y", "assoc", "ASI", T.ASI[:], T.assoc[:], 6500)
     ops[-1]["rd"] = ["X"]
 
     def iota(dst, key, pattern, base, cm, n, flag=True):
@@ -131,137 +146,136 @@ def build(g, T, topo, rank, core):
             fn = lambda: g.iota(dst, pattern, base, cm, allow_small_or_imprecise_dtypes=True)
         else:
             fn = lambda: g.iota(dst, pattern, base, cm)
-        add("G", fn, [], [key], 130 + 2 * n * CY)
+        add("G", key, fn, [], [key], n)
 
     iota(T.IP[:], "IP", [[1, 1]], 0, 1, 1, False)
-    iota(T.IM[:], "IM", [[1, 128]], 0, 0, 128)
+    iota(T.IM[:], "IM", [[1, 160]], 0, 0, 160)
     iota(T.IMG[:], "IMG", [[16, 8], [0, 16]], 0, 0, 128)
-    iota(T.IMB[:], "IMB", [[1, 128]], 0, 0, 128)
     iota(T.IMK[:], "IMK", [[0, 8], [1, 16]], 0, 0, 128)
-    iota(T.CII[:], "CII", [[256, 16]], 15, 0, 16, False)
+    iota(T.CBI[:], "CBI", [[-16, 8]], 127, 0, 8)
 
-    V("cp", ["CIN"], ["C160", "C161"], S, out=T.C16[:], in_=T.CIN[:])
+    def ts(key, out, src, skeys, n, rate, a, b=None, op0=OP.add, op1=None):
+        if op1 is None:
+            V(key, "ts", skeys, [key], n, rate, out=out, in0=src, scalar1=a, scalar2=None, op0=op0)
+        else:
+            V(key, "ts", skeys, [key], n, rate, out=out, in0=src, scalar1=a, scalar2=b, op0=op0, op1=op1)
 
-    V("ts", ["IP"], ["KI"], 1, out=T.KI[:], in0=T.IP[:], scalar1=15, scalar2=None, op0=OP.bitwise_and)
-    V("cp", ["IP"], ["cP"], 1, out=col(cP), in_=T.IP[:])
-    V("cp", ["KI"], ["cK"], 1, out=col(cK), in_=T.KI[:])
-    V("tt", ["cP", "cK"], ["cG16"], 1, out=col(cG16), in0=col(cP), in1=col(cK), op=OP.subtract)
+    def scol(i, key, src, skeys, a, b=None, op0=OP.add, op1=None):
+        ts(key, col(i), src, skeys, 1, 1.0, a, b, op0, op1)
 
-    def mat(dst, key, src, skey, c, ckey, n=128, rate=1.0):
-        V("ts", [skey, ckey], [key], n, rate, out=dst, in0=src, scalar1=c, scalar2=None, op0=OP.is_equal)
+    def mat(key, skey, c, ckey, op=OP.is_equal, n=128):
+        ts(key, T[key][:, 0:n], T[skey][:, 0:n], [skey, ckey], n, 0.5, c, op0=op)
 
-    mat(T.mI[:], "mI", T.IM[:], "IM", col(cP), "cP")
-    V("ts", ["mI"], ["mNI"], 128, 0.5, out=T.mNI[:], in0=T.mI[:], scalar1=-1.0, scalar2=None, op0=OP.mult)
+    def scaled(key, skey, c, n=128):
+        A(key, [skey], [key], n, out=T[key][:, 0:n], in_=T[skey][:, 0:n], func=AF.Copy, scale=c)
 
-    def scol(i, key, src, skey, **kw):
-        V("ts", [skey], [key], 1, out=col(i), in0=src, **kw)
+    def less(key, a, b, n=128):
+        V(key, "tt", [a, b], [key], n, 2.0, out=T[key][:], in0=T[a][:], in1=T[b][:], op=OP.subtract)
 
-    def state_from_pref():
-        V("cp", ["RIN"], ["R0", "R1_"], S, out=T.R[:], in_=T.RIN[:])
-    state_from_pref()
-    ops[-1]["wr"] = ["Rs0", "Rs1"]
-
-    def orders(h, t, src, rd, banks=()):
-        A(rd, ["w%d_%d" % (t, h)], HS, banks, out=m0(T["M0_%d" % t], h, 1), in_=src, func=AF.Exp, bias=col(12), scale=-11.0 * LN2)
-        ops[-1]["rd"].append("bias")
-        A(rd, ["IW%d" % h], HS, banks, out=sl(T.IW, h), in_=src, func=AF.Exp, scale=LN2)
-
-    add("V", lambda: g.vector.memset(col(12), WT * LN2), [], ["bias"], 80)
-    add("V", lambda: g.vector.memset(col(13), 6.5 * 2.0 ** 96), [], ["bias"], 80)
-    add("V", lambda: g.vector.memset(col(14), 15.0 * LN2), [], ["bias"], 80)
-    for h in range(NH):
-        orders(h, 0, sl(T.R, h), ["Rs%d" % h])
-
-    for k in range(16):
-        V("ts", ["IMB", "cG16"], ["SEL%d" % (k // 4)], 128, 0.5, out=T.SEL[:, k * 128:(k + 1) * 128], in0=T.IMB[:], scalar1=float(k), scalar2=col(cG16), op0=OP.subtract, op1=OP.is_equal)
-    for j in range(4):
-        MM([(T["pb%d" % j][:, 0:512], T.mI[:], T.SEL[:, j * 512:(j + 1) * 512], True, True, 512, False)], ["mI", "SEL%d" % j], ["ring%d" % j], [j])
-        m = 512 if j < 3 else 384
-        V("tt", ["SEL%d" % j, "SEL%d" % min(j + 1, 3), "ring%d" % j], ["CNT%d" % j], m, 1.0, [j], out=T.CNT[:, j * 512:j * 512 + m], in0=T["pb%d" % j][:, 0:m], in1=T.SEL[:, j * 512 + 128:j * 512 + 128 + m], op=OP.subtract)
-    V("cp", ["SEL3"], ["CNT3"], 128, 0.5, out=T.CNT[:, 1920:2048], in_=T.SEL[:, 1920:2048])
+    for key, dst, src in (("C16", T.C16, "CIN"), ("Rs", T.R, "RIN"), ("H16", T.H16, "HIN"), ("Cs", T.C, "CIN"), ("Hs", T.H, "HIN")):
+        V("in" + key, "cp", [src], [key + "0", key + "1"], S, out=dst[:], in_=T[src][:])
+    ts("KI", T.KI[:], T.IP[:], ["IP"], 1, 1.0, 15, op0=OP.bitwise_and)
+    V("cP", "cp", ["IP"], ["cP"], 1, out=col(cP), in_=T.IP[:])
+    V("cK", "cp", ["KI"], ["cK"], 1, out=col(cK), in_=T.KI[:])
+    V("cG16", "tt", ["cP", "cK"], ["cG16"], 1, out=col(cG16), in0=col(cP), in1=col(cK), op=OP.subtract)
+    mat("mI", "IM", col(cP), "cP")
+    scaled("mNI", "mI", -1.0)
+    for i, key, c in ((cW, "cW", WT * LN2), (cT, "cT", 6.5 * 2.0 ** 96), (cE, "cE", 15.0 * LN2)):
+        fill(key, col(i), c)
+    scol(cZ, "cZ", col(cG16), ["cG16"], 15.0)
+    scol(cZ1, "cZ1", col(cG16), ["cG16"], 16.0)
+    mat("Z", "IM", col(cZ), "cZ", n=144)
+    mat("Z1", "IM", col(cZ1), "cZ1", n=144)
+    less("ZD", "Z", "Z1", 144)
+    scaled("ZU", "Z", U, 144)
     ns = CFG["ns"]
-    nx = max(ns)
-    allcnt = ["CNT%d" % j for j in range(4)]
-    allsel = ["SEL%d" % j for j in range(4)]
-    V("ts", allcnt, ["CNH"], 128 * nx, 0.5, out=T.CNH[:, 0:128 * nx], in0=T.CNT[:, 128 * (16 - nx):], scalar1=0.5, scalar2=None, op0=OP.mult)
+    if max(ns):
+        scaled("ZH", "Z", 0.5, 144)
+        scaled("ZDH", "ZD", 0.5, 144)
     for h in range(NH):
-        V("ts", ["cK"], ["c8%d" % h], 1, out=T.COL2[:, h:h + 1], in0=col(cK), scalar1=float(16 - ns[h]), scalar2=8.0, op0=OP.is_equal, op1=OP.mult)
-    for r in range(16 - nx, 16):
-        add("V", lambda r=r: g.vector.memset(T.THC[:, r:r + 1], -0.6 * 2.0 ** (WT - 11 * r)), [], ["thr%d" % r], 65)
+        scol(c80 + h, "c8%d" % h, col(cK), ["cK"], float(16 - ns[h]), 8.0, OP.is_equal, OP.mult)
+    for r in range(16 - max(ns), 16):
+        fill("thr%d" % r, T.THC[:, r:r + 1], -0.6 * 2.0 ** (WT - 11 * r))
 
     def cntm(r, h):
         if r >= 16 - ns[h]:
-            return T.CNH[:, 128 * (r - 16 + nx):128 * (r - 15 + nx)]
-        return T.CNT[:, 128 * r:128 * (r + 1)]
-    mat(T.mB[:], "mB", T.IMG[:], "IMG", col(cG16), "cG16")
-    add("V", lambda: g.vector.memset(T.ONES[:], 1.0), [], ["ONES"], 80)
-    A(["cK", "bias"], ["cb2"], 1, out=T.COLB[:, 0:1], in_=col(cK), func=AF.Exp, bias=col(14), scale=-LN2)
-    A(["cK", "bias"], ["cbw"], 1, out=T.COLB[:, 1:2], in_=col(cK), func=AF.Exp, bias=col(12), scale=-11.0 * LN2)
-    V("ts", ["mB", "cb2"], ["mWB"], 128, 1.0, out=T.mWB[:], in0=T.mB[:], scalar1=T.COLB[:, 0:1], scalar2=None, op0=OP.mult)
-    V("ts", ["mWB"], ["mNW"], 128, 0.5, out=T.mNW[:], in0=T.mWB[:], scalar1=-1.0, scalar2=None, op0=OP.mult)
-    V("ts", ["mI"], ["m4"], 128, 0.5, out=T.m4[:], in0=T.mI[:], scalar1=-4.0, scalar2=None, op0=OP.mult)
-    V("cp", ["HIN"], ["H160", "H161"], S, out=T.H16[:], in_=T.HIN[:])
-    V("ts", ["mB", "cbw"], ["TMP"], 128, 1.0, out=T.TMP[:], in0=T.mB[:], scalar1=T.COLB[:, 1:2], scalar2=-0.6, op0=OP.mult, op1=OP.mult)
-    V("ts", ["IMK"], ["MK0"], 128, 1.0, out=T.MK0[:], in0=T.IMK[:], scalar1=0.5, scalar2=None, op0=OP.is_gt)
-    V("tt", ["TMP", "MK0"], ["mCW"], 128, 2.0, out=T.mCW[:], in0=T.TMP[:], in1=T.MK0[:], op=OP.mult)
-    scol(cKC, "cKC", col(cK), "cK", scalar1=0.0, scalar2=-(2.0 ** -90), op0=OP.is_equal, op1=OP.add)
-    V("ts", ["mI", "cKC"], ["mKC"], 128, 1.0, out=T.mKC[:], in0=T.mI[:], scalar1=col(cKC), scalar2=None, op0=OP.mult)
-    mat(T.fI[:], "fI", T.IM[:], "IM", col(cP), "cP")
-    V("cp", ["CIN"], ["Cs0", "Cs1"], S, out=T.C[:], in_=T.CIN[:])
-    scol(cH, "cH", col(cK), "cK", scalar1=-4096.0, scalar2=61440.0, op0=OP.mult, op1=OP.add)
-    V("ts", ["HIN", "cH"], ["HK0", "HK1"], S, out=T.HK[:], in0=T.HIN[:], scalar1=col(cH), scalar2=2.0 ** -17, op0=OP.add, op1=OP.mult)
-    V("ts", ["mB"], ["mNB"], 128, 0.5, out=T.mNB[:], in0=T.mB[:], scalar1=-1.0, scalar2=None, op0=OP.mult)
-    V("ts", ["mI"], ["mI2"], 128, 0.5, out=T.mI2[:], in0=T.mI[:], scalar1=2.0, scalar2=None, op0=OP.mult)
-    V("tt", ["mI2", "mB"], ["mTB"], 128, 2.0, out=T.mTB[:], in0=T.mI2[:], in1=T.mB[:], op=OP.subtract)
-    V("ts", ["IP"], ["B4I"], 1, out=T.B4I[:], in0=T.IP[:], scalar1=4, scalar2=1, op0=OP.arith_shift_right, op1=OP.bitwise_and)
-    V("cp", ["B4I"], ["cS1"], 1, out=col(cS1), in_=T.B4I[:])
-    scol(cS0, "cS0", col(cS1), "cS1", scalar1=-1.0, scalar2=1.0, op0=OP.mult, op1=OP.add)
-    scol(cPp, "cPp", col(cP), "cP", scalar1=16.0, scalar2=None, op0=OP.add)
-    scol(cPm, "cPm", col(cP), "cP", scalar1=-16.0, scalar2=None, op0=OP.add)
-    scol(c16K, "c16K", col(cK), "cK", scalar1=16.0, scalar2=None, op0=OP.mult)
-    scol(c16P, "c16P", col(cP), "cP", scalar1=16.0, scalar2=None, op0=OP.mult)
+            return sel(T.ZDH if r < 15 else T.ZH, r)
+        return sel(T.ZD if r < 15 else T.Z, r)
+    mat("mB", "IMG", col(cG16), "cG16")
+    fill("ONES", T.ONES[:], 1.0, 128)
+    fill("BIG", T.BIG[:], 32768.0, 128)
+    A("cb2", ["cK", "cE"], ["cb2"], 1300, out=T.COLB[:, 0:1], in_=col(cK), func=AF.Exp, bias=col(cE), scale=-LN2)
+    A("cbw", ["cK", "cW", "cb2"], ["cbw"], 1, out=T.COLB[:, 1:2], in_=col(cK), func=AF.Exp, bias=col(cW), scale=-11.0 * LN2)
+
+    def orders(h, t, src, rd, banks=()):
+        A("w", rd + ["cW", "cb2"], ["w%d_%d" % (t, h)], HS, banks, out=m0(T["M0_%d" % t], h, 1), in_=src, func=AF.Exp, bias=col(cW), scale=-11.0 * LN2)
+        A("IW", rd + ["cb2"], ["IW%d" % h], HS, banks, out=sl(T.IW, h), in_=src, func=AF.Exp, scale=LN2)
+
+    mat("mWB", "mB", T.COLB[:, 0:1], "cb2", OP.mult)
+    ts("TMP", T.TMP[:], T.mB[:], ["mB", "cbw"], 128, 0.5, T.COLB[:, 1:2], -0.6, OP.mult, OP.mult)
+    ts("MK0", T.MK0[:], T.IMK[:], ["IMK"], 128, 0.5, 0.5, op0=OP.is_gt)
+    V("mCW", "tt", ["TMP", "MK0"], ["mCW"], 128, 2.0, out=T.mCW[:], in0=T.TMP[:], in1=T.MK0[:], op=OP.mult)
+    scol(cKC, "cKC", col(cK), ["cK"], 0.0, -(2.0 ** -90), OP.is_equal, OP.add)
+    for key, skey, c in (("fI", "mI", 1.0), ("mN4k", "mI", -4096.0), ("mNB", "mB", -1.0), ("mNBU", "mB", -U), ("mI2", "mI", 2.0), ("mN16", "mI", -16.0)):
+        scaled(key, skey, c)
+    if max(CFG["es"]):
+        scaled("mU", "mI", U)
+    less("mTB", "mI2", "mB")
+    less("mIB", "mI", "mB")
+    scaled("mBI", "mIB", -1.0)
+    ts("B4I", T.B4I[:], T.IP[:], ["IP"], 1, 1.0, 4, 1, OP.arith_shift_right, OP.bitwise_and)
+    V("cS1", "cp", ["B4I"], ["cS1"], 1, out=col(cS1), in_=T.B4I[:])
+    scol(cS0, "cS0", col(cS1), ["cS1"], -1.0, 1.0, OP.mult, OP.add)
+    scol(cPp, "cPp", col(cP), ["cP"], 16.0)
+    scol(cPm, "cPm", col(cP), ["cP"], -16.0)
+    scol(cOF, "cOF", col(cK), ["cK"], 16.0, 1807.0, OP.mult, OP.add)
+    scol(c16P, "c16P", col(cP), ["cP"], 16.0, op0=OP.mult)
     for j, (c, ck, s, sk) in enumerate([(cP, "cP", cS0, "cS0"), (cPp, "cPp", cS0, "cS0"), (cPm, "cPm", cS1, "cS1"), (cP, "cP", cS1, "cS1")]):
-        V("ts", ["IM", ck, sk], ["fP"], 128, 1.0, out=T.fP[:, j * 128:(j + 1) * 128], in0=T.IM[:], scalar1=col(c), scalar2=col(s), op0=OP.is_equal, op1=OP.mult)
-    V("ts", ["IMK"], ["SD"], 128, 1.0, out=T.SD[:], in0=T.IMK[:], scalar1=0.0, scalar2=-4096.0, op0=OP.is_equal, op1=OP.mult)
-    V("ts", ["CII", "c16K"], ["CI"], 16, 1.0, out=T.CI[:], in0=T.CII[:], scalar1=col(c16K), scalar2=None, op0=OP.add)
-    V("ts", ["IMG", "c16P"], ["mG8"], 128, 1.0, out=T.mG8[:], in0=T.IMG[0:8, :], scalar1=T.COL[0:8, c16P:c16P + 1], scalar2=None, op0=OP.is_equal)
-    V("cp", ["FIN"], ["A8"], S, out=T.A8[:], in_=T.FIN[:])
-    V("ts", ["FIN"], ["Q8I"], S, out=T.Q8I[:], in0=T.FIN[:], scalar1=3, scalar2=None, op0=OP.bitwise_and)
-    V("cp", ["Q8I"], ["Q8"], S, out=T.Q8[:], in_=T.Q8I[:])
-    MM([(T.pb6[:, 0:256], T.mG8[:], T.A8[:], True, True, S, False), (T.pb6[:, 256:512], T.mG8[:], T.Q8[:], True, True, S, False)],
-       ["mG8", "A8", "Q8"], ["b6a"], [6])
-    A(["b6a"], ["AB"], S, [6], out=T.AB[:], in_=T.pb6[:, 0:256], func=AF.Copy)
+        ts("fP%d" % j, T.fP[:, j * 128:(j + 1) * 128], T.IM[:, 0:128], ["IM", ck, sk], 128, 1.0, col(c), col(s), OP.is_equal, OP.mult)
+    fill("SD", T.SD[:], 4096.0, 256)
+    fill("SD", T.SD[:, 0:128:16], -(2.0 ** 22), 16)
+    scaled("CB", "CBI", U, 8)
+    ts("mG8", T.mG8[:], T.IMG[0:8, :], ["IMG", "c16P"], 128, 0.5, T.COL[0:8, c16P:c16P + 1], op0=OP.is_equal)
+    V("A8", "cp", ["FIN"], ["A8"], S, out=T.A8[:], in_=T.FIN[:])
+    ts("Q8I", T.Q8I[:], T.FIN[:], ["FIN"], S, 1.0, 3, op0=OP.bitwise_and)
+    V("Q8", "cp", ["Q8I"], ["Q8"], S, out=T.Q8[:], in_=T.Q8I[:])
+    scol(cK0, "cK0", col(cK), ["cK"], 0.0, op0=OP.is_equal)
+    scol(cQa, "cQa", col(cK), ["cK"], 1.0, -4.0, OP.is_equal, OP.mult)
+    scol(cQb, "cQb", col(cK), ["cK"], 2.0, 4.0, OP.is_equal, OP.mult)
+    scol(cQ, "cQ", col(cQa), ["cQa", "cQb", "cK0"], col(cQb), col(cK0), OP.add, OP.add)
+    scol(cTH, "cTH", col(cQa), ["cQa", "cQb"], 0.75, col(cQb), OP.mult, OP.subtract)
+    mat("mTH", "mB", col(cQ), "cQ", OP.mult)
+    mat("mZ0", "mB", col(cK0), "cK0", OP.mult)
     for h in range(NH):
-        A(["b6a"], ["th0_%d" % h], HS, [6], out=m0(T.M0_0, h, 2), in_=T.pb6[:, 256 + h * HS:256 + (h + 1) * HS], func=AF.Copy)
+        at["h"] = h
+        orders(h, 0, sl(T.R, h), ["Rs%d" % h])
+        MM("z", [(ps(6 + h, 2), T.mG8[:], T.Q8[:, h * HS:(h + 1) * HS], True, True, HS, False)], ["mG8", "Q8"], ["Q2%d" % h], 6 + h)
+        A("th", ["Q2%d" % h, "cTH"], ["th0_%d" % h], HS, [6 + h], out=m0(T.M0_0, h, 2), in_=ps(6 + h, 2), func=AF.Relu, bias=col(cTH))
+        MM("r0", [(ps(4 + h, 3), T.mI[:], sl(T.R, h), True, True, HS, False)], ["mI", "Rs%d" % h], ["P3%d" % h], 4 + h)
 
-    for j in range(8):
-        V("ts", ["ASI", "cH"], ["ASH"], W // 8, 1.0, out=T.ASH[:, j * 512:(j + 1) * 512], in0=T.ASI[:, j * 512:(j + 1) * 512],
-          scalar1=col(cH), scalar2=2.0 ** -17, op0=OP.add, op1=OP.mult)
-
-    def send(t, m, dst, src_ap, dst_ap, rd, wr, lat):
+    def send(t, m, dst, src_ap, dst_ap, rd, wr, more):
         rid, pid, _s = topo.addr(dst)
         mask = topo.mask(core, dst)
         ne = len(topo.engines(core, dst))
         rs, ls = "r%d_%s" % (t, m), "l%d_%s" % (t, m)
-        add("G", lambda: g.remote_dma(out_ap=dst_ap, in_ap=src_ap, remote_sem=T.sem[rs], local_sem=T.sem[ls], pid=pid, routing_id=rid, dma_engine_mask=mask),
-            rd, [], 700)
+        add("G", "send" + m[0], lambda: g.remote_dma(out_ap=dst_ap, in_ap=src_ap, remote_sem=T.sem[rs], local_sem=T.sem[ls], pid=pid, routing_id=rid, dma_engine_mask=mask),
+            rd, [], "issue")
         ops[-1]["remote"] = (ls, ne)
         k = len(ops) - 1
-        add("N", None, [], wr, 0, sem=rs, val=ne, lat=lat)
+        add("N", "land" + m[0], None, [], wr, "hop", sem=rs, val=ne, lat=more)
         ops[-1]["after"] = k
 
-    def gather(t, h, src16, dst, key, okey, vp):
+    def gather(h, src16, dst, key, okey, vp):
         npc = CFG["npc"]
         step = HS // npc
         for j in range(npc):
             a = h * HS + j * step
             offs = src16[:, a:a + step]
             o = dst[:, 16 * a:16 * (a + step)]
-            n = 16 * step
             if (h, j) in vp:
-                V("cp", ["X", okey + str(h)], [key + "%d%d" % (h, j)], n, GR, out=o, in_=T.X[:].indirect(offs))
+                V(key + str(j), "cp", ["X", okey + str(h)], [key + "%d%d" % (h, j)], 16 * step, "g", out=o, in_=T.X[:].indirect(offs))
             else:
-                A(["X", okey + str(h)], [key + "%d%d" % (h, j)], n, (), 45, GR, out=o, in_=T.X[:].indirect(offs), func=AF.Copy)
+                A(key + str(j), ["X", okey + str(h)], [key + "%d%d" % (h, j)], 16 * step, (), "g", out=o, in_=T.X[:].indirect(offs), func=AF.Copy)
 
     ring = [0]
 
@@ -271,20 +285,21 @@ def build(g, T, topo, rank, core):
         M0, L0 = T["M0_%d" % t], T["L0_%d" % t]
         M1, L1 = T["M1_%d" % t], T["L1_%d" % t]
         NS, LN = T["NS_%d" % t], T["LN_%d" % t]
-        FF, LF = T["FF_%d" % t], T["LF_%d" % t]
+        FF, LF = T.FF[:, t * S:(t + 1) * S], T.LF[:, t * S:(t + 1) * S]
         last = t == RO - 1
-        cur_t[0] = t
+        at["t"] = t
+        l0k = "L0_%d" % t
         for h in range(NH):
             hs = str(h)
-            cur_h[0] = h
-            gather(t, h, T.C16, T.XG, "XG", "C16", CFG["vc"] if t else CFG["vc0"])
+            th = "%d_%d" % (t, h)
+            at["h"] = h
+            P, Q = 4 + h, 6 + h
+            gather(h, T.C16, T.XG, "XG", "C16", CFG["vc"] if t else CFG["vc0"])
             xgk = ["XG%d%d" % (h, j) for j in range(CFG["npc"])]
-
-            b4 = 4 + h
+            x0 = T.XG[:, h * 2048:(h + 1) * 2048:16]
             nq = CFG["nq"][h]
             qs = HS // nq
             npq = CFG["npc"] // nq
-            V("cp", xgk, ["x0_%d" % h], HS, 0.5, out=m0(M0, h, 0), in_=T.XG[:, h * 2048:(h + 1) * 2048:16])
             for q in range(nq):
                 qk = xgk[q * npq:(q + 1) * npq]
 
@@ -294,283 +309,309 @@ def build(g, T, topo, rank, core):
                 def dw(k, h=h, q=q, qs=qs):
                     return T.DW[:, h * 2048 + k * 128 + q * qs:h * 2048 + k * 128 + (q + 1) * qs]
                 wq = M0[:, (3 * h + 1) * HS + q * qs:(3 * h + 1) * HS + (q + 1) * qs]
-                sk = T["pb%d" % b4][:, q * qs:(q + 1) * qs]
-                nk = 512 // qs
-                for c in range(16 // nk):
-                    ks = range(1 + nk * c, min(16, 1 + nk + nk * c))
+                sk = T["pb%d" % P][:, q * qs:(q + 1) * qs]
+                for c in range(4):
+                    ks = range(1 + 4 * c, min(16, 5 + 4 * c))
                     b = ring[0] % 4
                     ring[0] += 1
-                    for s0 in range(0, len(ks), 4):
-                        lst = []
-                        for j in range(s0, min(s0 + 4, len(ks))):
-                            o = T["pb%d" % b][:, j * qs:(j + 1) * qs]
-                            lst.append((o, T.mI[:], xg(ks[j]), True, False, qs, False))
-                            lst.append((o, T.mNI[:], xg(0), False, True, qs, False))
-                        MM(lst, qk + ["mI", "mNI"], ["ring%d" % b], [b])
+                    lst = []
                     for j, k in enumerate(ks):
-                        V("tt", ["ring%d" % b, "w%d_%d" % (t, h)], ["DW%d%d_%d" % (h, q, k)], qs, 1.0, [b],
+                        o = T["pb%d" % b][:, j * qs:(j + 1) * qs]
+                        lst.append((o, T.mI[:], xg(k), True, False, qs, False))
+                        lst.append((o, T.mNI[:], xg(0), False, True, qs, False))
+                    nm = str(4 * q + c)
+                    MM("dx" + nm, lst, qk + ["mI", "mNI"], ["ring%d" % b], b)
+                    for j, k in enumerate(ks):
+                        V("DW" + nm, "tt", ["ring%d" % b, "w" + th], ["DW%d%d_%d" % (h, q, k)], qs, 1.0, [b],
                           out=dw(k), in0=T["pb%d" % b][:, j * qs:(j + 1) * qs], in1=wq, op=OP.mult)
-                    MM([(sk, T.SEL[:, k * 128:(k + 1) * 128], dw(k), k == 1, k == 15, qs, False) for k in ks],
-                       allsel + ["DW%d%d_%d" % (h, q, k) for k in ks], ["Sk" + hs], [b4])
-            A(["Sk" + hs], ["ABS" + hs], HS, [b4], out=sl(T.AB1, h), in_=ps(b4, 0), func=AF.Abs)
+                    join(len(ks))
+                    MM("sk" + nm, [(sk, sel(T.Z, k), dw(k), k == 1, k == 15, qs, False) for k in ks],
+                       ["Z"] + ["DW%d%d_%d" % (h, q, k) for k in ks], ["P0" + hs], P)
+            MM("xb", [(ps(Q, 3), T.mI[:], T.BIG[:], True, False, HS, False), (ps(Q, 3), T.mI[:], x0, False, True, HS, False)], xgk + ["mI", "BIG"], ["Q3" + hs], Q)
+            A("x0", xgk, ["x0" + th], HS, out=m0(M0, h, 0), in_=x0, func=AF.Copy)
+            A("ABS", ["P0" + hs], ["ABS" + hs], HS, [P], out=sl(T.AB1, h), in_=ps(P, 0), func=AF.Abs)
 
             def G(r, h=h):
                 return T.G[:, h * 2048 + r * 128:h * 2048 + (r + 1) * 128]
             for r in range(16):
-                if r >= 16 - CFG["ns"][h]:
-                    A(["ABS" + hs, "thr%d" % r], ["G%d_%d" % (h, r)], HS, out=G(r), in_=sl(T.AB1, h), func=AF.Sign, bias=T.THC[:, r:r + 1])
+                if r >= 16 - ns[h]:
+                    A("GS%d" % (r // 4), ["ABS" + hs, "thr%d" % r], ["G%d_%d" % (h, r)], HS, out=G(r), in_=sl(T.AB1, h), func=AF.Sign, bias=T.THC[:, r:r + 1])
                 else:
-                    V("ts", ["ABS" + hs], ["G%d_%d" % (h, r)], HS, 0.5, out=G(r), in0=sl(T.AB1, h), scalar1=0.6 * 2.0 ** (WT - 11 * r), scalar2=None, op0=OP.is_ge)
+                    V("G%d" % (r // 4), "ts", ["ABS" + hs], ["G%d_%d" % (h, r)], HS, 0.5, out=G(r), in0=sl(T.AB1, h), scalar1=0.6 * 2.0 ** (WT - 11 * r), scalar2=None, op0=OP.is_ge)
                 if r % 4 == 3:
-                    MM([(ps(b4, 1), cntm(q, h), G(q), q == 0, q == 15, HS, False) for q in range(r - 3, r + 1)],
-                       allcnt + ["CNH"] + ["G%d_%d" % (h, q) for q in range(r - 3, r + 1)], ["cnt" + hs], [b4])
-            c8 = T.COL2[:, h:h + 1]
+                    join(4)
+                    MM("cnt%d" % (r // 4), [(ps(P, 1), cntm(q, h), G(q), q == 0, q == 15, HS, False) for q in range(r - 3, r + 1)],
+                       ["Z", "ZD", "ZH", "ZDH"] + ["G%d_%d" % (h, q) for q in range(r - 3, r + 1)], ["P1" + hs], P)
             if CFG["bitV"][h]:
-                V("ts", ["cnt" + hs, "c8" + hs], ["BIT" + hs], HS, 1.0, [b4], out=sl(T.BIT, h), in0=ps(b4, 1), scalar1=c8, scalar2=0.5, op0=OP.add, op1=OP.is_gt)
+                V("BIT", "ts", ["P1" + hs, "c8" + hs], ["BIT" + hs], HS, 1.0, [P], out=sl(T.BIT, h), in0=ps(P, 1), scalar1=col(c80 + h), scalar2=0.5, op0=OP.add, op1=OP.is_gt)
             else:
-                A(["cnt" + hs, "c8" + hs], ["BIT" + hs], HS, [b4], out=sl(T.BIT, h), in_=ps(b4, 1), func=AF.Sign, bias=c8)
-            MM([(ps(b4, 0), T.mWB[:], T.ONES[:], True, False, HS, False), (ps(b4, 0), T.mNW[:], sl(T.BIT, h), False, True, HS, False)],
-               ["mNW", "mWB", "ONES", "BIT" + hs], ["Sk" + hs], [b4])
-            V("tt", ["Sk" + hs, "IW" + hs], ["TI" + hs], HS, 1.0, [b4], out=sl(T.TI, h), in0=ps(b4, 0), in1=sl(T.IW, h), op=OP.mult)
-            V("ts", ["TI" + hs], ["TJ" + hs], HS, 1.0, out=sl(T.TJ, h), in0=sl(T.TI, h), scalar1=32768, scalar2=None, op0=OP.bitwise_and)
-            V("tt", ["TJ" + hs, "x0_%d" % h], ["x0p%d" % h], HS, 2.0, out=sl(M1, h), in0=m0(M0, h, 0), in1=sl(T.TJ, h), op=OP.add)
-            send(t, "1%d" % h, hear, sl(M1, h), sl(L1, h), ["x0p%d" % h], ["L1" + hs], CFG["hop"])
-            MM([(ps(b4, 1), T.mI[:], sl(T.AB1, h), True, False, HS, False), (ps(b4, 1), T.mCW[:], sl(T.BIT, h), False, False, HS, False),
-                (ps(b4, 1), T.mKC[:], T.ONES[:], False, True, HS, False)], ["ABS" + hs, "mI", "mCW", "mKC", "ONES", "BIT" + hs], ["cnt" + hs, "dB" + hs], [b4])
-            V("ts", ["cnt" + hs], ["KAP" + hs], HS, 1.0, [b4], out=sl(T.KAP, h), in0=ps(b4, 1), scalar1=0.0, scalar2=8192.0, op0=OP.is_gt, op1=OP.mult)
-            MM([(ps(b4, 2), T.fI[:], sl(T.C, h), True, False, HS, True), (ps(b4, 2), T.mNI[:], sl(T.KAP, h), False, True, HS, False)],
-               ["fI", "mNI", "Cs" + hs, "KAP" + hs], ["q" + hs], [b4])
-            send(t, "0%d" % h, hear, M0[:, h * 3 * HS:(h + 1) * 3 * HS], L0[:, h * 3 * HS:(h + 1) * 3 * HS], ["x0_" + hs, "w%d_%d" % (t, h), "th%d_%d" % (t, h)], ["L0" + hs], CFG["hop"] + 200)
+                A("BIT", ["P1" + hs, "c8" + hs], ["BIT" + hs], HS, [P], out=sl(T.BIT, h), in_=ps(P, 1), func=AF.Sign, bias=col(c80 + h))
+            MM("word", [(ps(P, 0), T.mWB[:], sl(T.BIT, h), True, True, HS, False)], ["mWB", "BIT" + hs], ["P0" + hs], P)
+            V("TI", "tt", ["P0" + hs, "IW" + hs], ["TI" + hs], HS, 1.0, [P], out=sl(T.TI, h), in0=ps(P, 0), in1=sl(T.IW, h), op=OP.mult)
+            V("TJ", "ts", ["TI" + hs], ["TJ" + hs], HS, 1.0, out=sl(T.TJ, h), in0=sl(T.TI, h), scalar1=32768, scalar2=None, op0=OP.bitwise_and)
+            V("x0p", "tt", ["TJ" + hs, "Q3" + hs], ["x0p" + th], HS, 1.0, [Q], out=sl(M1, h), in0=ps(Q, 3), in1=sl(T.TJ, h), op=OP.subtract)
+            send(t, "1" + hs, hear, sl(M1, h), sl(L1, h), ["x0p" + th], ["L1" + th], 0)
+            MM("dB", [(ps(Q, 1), T.mI[:], sl(T.AB1, h), True, False, HS, False), (ps(Q, 1), T.mCW[:], sl(T.BIT, h), False, True, HS, False)],
+               ["ABS" + hs, "mI", "mCW", "BIT" + hs], ["Q1" + hs], Q)
+            A("SG", ["Q1" + hs, "cKC"], ["SG" + hs], HS, [Q], out=sl(T.SG, h), in_=ps(Q, 1), func=AF.Sign, bias=col(cKC))
+        send(t, "0", hear, M0[:], L0[:], [k + "%d_%d" % (t, h) for k in ("x0", "w", "th") for h in range(NH)], [l0k], 500)
         for h in range(NH):
-            cur_h[0] = h
-            gather(t, h, T.H16, T.YG, "YG", "H16", CFG["vh"])
+            at["h"] = h
+            gather(h, T.H16, T.YG, "YG", "H16", CFG["vh"])
         for h in range(NH):
             hs = str(h)
-            cur_h[0] = h
+            th = "%d_%d" % (t, h)
+            at["h"] = h
+            P, Q = 4 + h, 6 + h
             ygk = ["YG%d%d" % (h, j) for j in range(CFG["npc"])]
-            b6 = 6 + h
-            V("ts", ["L1" + hs], ["DSC" + hs], HS, 0.5, out=sl(T.DSC, h), in0=sl(L1, h), scalar1=1000.0, scalar2=None, op0=OP.is_lt)
-            lst = [(ps(b6, 3), T.mI[:], m0(L0, h, 1), True, True, HS, False)]
+            l1k = "L1" + th
+            es = CFG["es"][h]
+            if es < 4 or not last:
+                MM("xp", [(ps(P, 0), T.mI[:], sl(L1, h), True, True, HS, False)], ["mI", l1k], ["P0" + hs], P)
+            V("DSC", "ts", [l1k], ["DSC" + hs], HS, 0.5, out=sl(T.DSC, h), in0=sl(L1, h), scalar1=1000.0, scalar2=None, op0=OP.is_lt)
             if not last:
-                lst.append((ps(b6, 2), T.mI[:], sl(L1, h), True, True, HS, False))
-                V("ts", ["L1" + hs], ["UND" + hs], HS, 0.5, out=sl(T.UND, h), in0=sl(L1, h), scalar1=1000.0, scalar2=None, op0=OP.is_gt)
-            MM(lst, ["mI", "L0" + hs, "L1" + hs], ["wc" + hs, "xc" + hs], [b6])
-            if not last:
-                V("tt", ["xc" + hs, "DSC" + hs], ["XD" + hs], HS, 1.0, [b6], out=sl(T.XD, h), in0=ps(b6, 2), in1=sl(T.DSC, h), op=OP.mult)
-            MM([(ps(b6, 0), T.fI[:], sl(T.HK, h), True, False, HS, True), (ps(b6, 0), T.mNB[:], sl(T.DSC, h), False, False, HS, False)],
-               ["fI", "mNB", "HK" + hs, "DSC" + hs], ["key" + hs], [b6])
+                V("UND", "ts", [l1k], ["UND" + hs], HS, 0.5, out=sl(T.UND, h), in0=sl(L1, h), scalar1=1000.0, scalar2=None, op0=OP.is_gt)
+                V("XD", "tt", ["P0" + hs, "DSC" + hs], ["XD" + hs], HS, 1.0, [P], out=sl(T.XD, h), in0=ps(P, 0), in1=sl(T.DSC, h), op=OP.mult)
+            if es:
+                acc, ak, z, zk = ps(Q, 1), "Q1" + hs, T.Z, "Z"
+                MM("nd", [(acc, T.mNB[:], sl(T.DSC, h), True, False, HS, False)], ["mNB", "DSC" + hs], [ak], Q)
+            else:
+                acc, ak, z, zk = ps(Q, 0), "Q0" + hs, T.ZU, "ZU"
+                MM("kh", [(acc, T.fI[:], sl(T.H, h), True, False, HS, True)], ["fI", "Hs" + hs], [ak], Q)
+                MM("nd", [(acc, T.mNBU[:], sl(T.DSC, h), False, False, HS, False)], ["mNBU", "DSC" + hs], [ak], Q)
             for c in range(4):
-                b = ring[0] % 4
-                ring[0] += 1
                 ks = range(4 * c, 4 * c + 4)
-                byS = c >= 4 - CFG["es"][h]
-                lst = []
-                for j, k in enumerate(ks):
-                    lst.append((ps(b, j), T.mI[:], T.YG[:, h * 2048 + k:(h + 1) * 2048:16], True, not byS, HS, False))
-                    if byS:
+
+                def yg(k, h=h):
+                    return T.YG[:, h * 2048 + k:(h + 1) * 2048:16]
+
+                def ek(k, h=h, m=1):
+                    return T.E[:, h * 2048 + k * 128:h * 2048 + (k + m) * 128]
+                if c >= 4 - es:
+                    b = ring[0] % 4
+                    ring[0] += 1
+                    lst = []
+                    for j, k in enumerate(ks):
+                        lst.append((ps(b, j), T.mI[:], yg(k), True, False, HS, False))
                         lst.append((ps(b, j), T.mNI[:], sl(L1, h), False, True, HS, False))
-                MM(lst, ygk + ["mI"] + (["mNI", "L1" + hs] if byS else []), ["ring%d" % b], [b])
-                if byS:
-                    A(["ring%d" % b], ["EA" + hs], 512, [b], out=T.EA[:, h * 512:(h + 1) * 512], in_=T["pb%d" % b][:, 0:512], func=AF.Abs)
-                    A(["EA" + hs], ["E%d_%d" % (h, k) for k in ks], 512, out=T.E[:, h * 2048 + c * 512:h * 2048 + (c + 1) * 512], in_=T.EA[:, h * 512:(h + 1) * 512],
-                      func=AF.Relu, scale=-1.0, bias=1.0)
-                for j, k in enumerate(ks if not byS else ()):
-                    V("tt", ["ring%d" % b, "L1" + hs], ["E%d_%d" % (h, k)], HS, 1.0, [b],
-                      out=T.E[:, h * 2048 + k * 128:h * 2048 + (k + 1) * 128], in0=ps(b, j), in1=sl(L1, h), op=OP.is_equal)
-                MM([(ps(b6, 0), T.SEL[:, k * 128:(k + 1) * 128], T.E[:, h * 2048 + k * 128:h * 2048 + (k + 1) * 128], False, k == 15, HS, False) for k in ks],
-                   allsel + ["E%d_%d" % (h, k) for k in ks], ["key" + hs], [b6])
-            V("tr", ["key" + hs], ["KT" + hs], HS, 1.0, [b6], out=sl(T.KT, h), in_=ps(b6, 0))
-            A(["key" + hs], ["KH" + hs], HS, [b6], out=sl(T.KH, h), in_=ps(b6, 0), func=AF.Relu, scale=-1.0)
-            V("scan", ["KT" + hs, "SD"], ["SC" + hs], HS, 1.0, out=sl(T.SC, h), data0=T.SD[:], data1=sl(T.KT, h), initial=-4096.0, op0=OP.add, op1=OP.max)
+                    MM("dy%d" % c, lst, ygk + ["mI", "mNI", l1k], ["ring%d" % b], b)
+                    A("ES%d" % c, ["ring%d" % b], ["E%d_%d" % (h, k) for k in ks], 512, [b], out=ek(4 * c, m=4), in_=T["pb%d" % b][:, 0:512], func=AF.Relu, scale=512.0, bias=1.0)
+                else:
+                    for k in ks:
+                        V("E%d" % c, "tt", ygk + ["P0" + hs], ["E%d_%d" % (h, k)], HS, 1.0, [P], out=ek(k), in0=yg(k), in1=ps(P, 0), op=OP.is_equal)
+                    join(4)
+                MM("key%d" % c, [(acc, sel(z, k), ek(k), False, k == 15, HS, False) for k in ks], [zk] + ["E%d_%d" % (h, k) for k in ks], [ak], Q)
+            if es:
+                V("RND", "ts", [ak], ["RND" + hs], HS, 1.0, [Q], out=sl(T.RND, h), in0=acc, scalar1=1.5 * 2.0 ** 32, scalar2=-1.5 * 2.0 ** 32, op0=OP.add, op1=OP.add)
+                V("MS", "tt", [ak, "RND" + hs], ["MS" + hs], HS, 1.0, [Q], out=sl(T.MS, h), in0=acc, in1=sl(T.RND, h), op=OP.subtract)
+                MM("kh", [(ps(Q, 0), T.fI[:], sl(T.H, h), True, False, HS, True)], ["fI", "Hs" + hs], ["Q0" + hs], Q)
+                MM("km", [(ps(Q, 0), T.mU[:], sl(T.MS, h), False, True, HS, False)], ["mU", "MS" + hs], ["Q0" + hs], Q)
+            V("KT", "tr", ["Q0" + hs], ["KT" + hs], HS, 1.0, [Q], out=sl(T.KT, h), in_=ps(Q, 0))
+            A("KH", ["Q0" + hs], ["KH" + hs], HS, [Q], out=sl(T.KH, h), in_=ps(Q, 0), func=AF.Relu, scale=-1.0)
+            V("SC", "scan", ["KT" + hs, "SD"], ["SC" + hs], HS, 1.0, out=sl(T.SC, h), data0=T.SD[:], data1=sl(T.KT, h), initial=0.0, op0=OP.add, op1=OP.max)
             lst = []
             for hh in range(2):
                 for g2 in range(2):
-                    lst.append((T["pb%d" % b6][:, 128 + hh:136:2], T.fP[:, (2 * hh + g2) * 128:(2 * hh + g2 + 1) * 128],
+                    lst.append((T["pb%d" % Q][:, 128 + hh:136:2], T.fP[:, (2 * hh + g2) * 128:(2 * hh + g2 + 1) * 128],
                                 T.SC[:, h * HS + g2 * 16 + 15:(h + 1) * HS:32], g2 == 0, g2 == 1, 4, True))
-            MM(lst, ["fP", "SC" + hs], ["mk" + hs], [b6])
+            MM("mk", lst, ["fP%d" % j for j in range(4)] + ["SC" + hs], ["Q1" + hs], Q)
             ws = slice(8 * h, 8 * h + 8)
-            V("ts", ["mk" + hs], ["K32" + hs], 8, 1.0, [b6], out=T.K32[:, ws], in0=T["pb%d" % b6][:, 128:136], scalar1=131072.0, scalar2=None, op0=OP.mult)
-            V("ts", ["K32" + hs], ["N32" + hs], 8, out=T.N32[:, ws], in0=T.K32[:, ws], scalar1=4095, scalar2=None, op0=OP.bitwise_and)
-            V("cp", ["N32" + hs], ["NS" + hs], 8, out=NS[:, ws], in_=T.N32[:, ws])
-            send(t, "2%d" % h, spk, NS[:, ws], LN[:, ws], ["NS" + hs], ["LN" + hs], CFG["hop"] - 100)
-            V("ts", ["K32" + hs], ["KK" + hs], 8, out=T.KK[:, ws], in0=T.K32[:, ws], scalar1=12, scalar2=15, op0=OP.arith_shift_right, op1=OP.bitwise_and)
-            V("tt", ["KK" + hs, "CI"], ["OF" + hs], 8, out=T.OF[:, ws], in0=T.CI[:, 0:8], in1=T.KK[:, ws], op=OP.subtract)
-            V("cp", ["OF" + hs], ["OF16" + hs], 8, out=T.OF16[:, ws], in_=T.OF[:, ws])
+            V("K32", "tt", ["Q1" + hs, "CB"], ["K32" + hs], 8, 1.0, [Q], out=T.K32[:, ws], in0=T["pb%d" % Q][:, 128:136], in1=T.CB[:], op=OP.add)
+            V("N32", "ts", ["K32" + hs], ["N32" + hs], 8, out=T.N32[:, ws], in0=T.K32[:, ws], scalar1=4095, scalar2=None, op0=OP.bitwise_and)
+            V("NS", "cp", ["N32" + hs], ["NS" + th], 8, out=NS[:, ws], in_=T.N32[:, ws])
+            send(t, "2" + hs, spk, NS[:, ws], LN[:, ws], ["NS" + th], ["LN" + th], -100)
+            MM("q", [(ps(Q, 3), T.fI[:], sl(T.C, h), True, False, HS, True), (ps(Q, 3), T.mN4k[:], T.ONES[:], False, False, HS, False),
+                     (ps(Q, 3), T.mN4k[:], sl(T.SG, h), False, True, HS, False)], ["fI", "mN4k", "ONES", "Cs" + hs, "SG" + hs], ["Q3" + hs], Q)
+            V("KK", "ts", ["K32" + hs], ["KK" + hs], 8, out=T.KK[:, ws], in0=T.K32[:, ws], scalar1=12, scalar2=0xF0F, op0=OP.arith_shift_right, op1=OP.bitwise_and)
+            V("OF", "ts", ["KK" + hs, "cOF"], ["OF16" + hs], 8, out=T.OF16[:, ws], in0=T.KK[:, ws], scalar1=-1.0, scalar2=col(cOF), op0=OP.mult, op1=OP.add)
             ysrc = T.YG[:, h * 2048:(h + 1) * 2048].indirect(T.OF16[:, ws])
             if not last:
-                V("tt", ygk + ["OF16" + hs, "UND" + hs], ["YU" + hs], HS, GR, (), 40, out=sl(T.YU, h), in0=ysrc, in1=sl(T.UND, h), op=OP.mult)
-            V("tt", ygk + ["OF16" + hs, "L0" + hs], ["DM" + hs], HS, GR, (), 40, out=sl(T.DM, h), in0=ysrc, in1=m0(L0, h, 0), op=OP.not_equal)
-            V("tt", ["wc" + hs, "DM" + hs], ["DMW" + hs], HS, 1.0, [b6], out=sl(T.DMW, h), in0=ps(b6, 3), in1=sl(T.DM, h), op=OP.mult)
-            MM([(ps(b6, 2), T.mNB[:], sl(T.DM, h), True, False, HS, False), (ps(b6, 2), T.mI[:], m0(L0, h, 2), False, True, HS, False),
-                (ps(b6, 3), T.mTB[:], sl(T.DMW, h), True, True, HS, False)], ["mNB", "mI", "mTB", "DM" + hs, "DMW" + hs, "L0" + hs], ["tt" + hs, "wc" + hs, "xc" + hs], [b6])
-            A(["tt" + hs, "bias"], ["TH" + hs], HS, [b6], out=sl(T.TH, h), in_=ps(b6, 2), func=AF.Relu, scale=2.0 ** 96, bias=col(13))
-            V("tt", ["tt" + hs, "TH" + hs], ["FF%d_%d" % (t, h)], HS, 1.0, [b6], out=sl(FF, h), in0=ps(b6, 3), in1=sl(T.TH, h), op=OP.is_gt)
-            send(t, "3%d" % h, spk, sl(FF, h), sl(LF, h), ["FF%d_%d" % (t, h)], ["LF%d_%d" % (t, h)], CFG["hop"])
+                V("YU", "tt", ygk + ["OF16" + hs, "UND" + hs], ["YU" + hs], HS, "g", out=sl(T.YU, h), in0=ysrc, in1=sl(T.UND, h), op=OP.mult)
+            V("DM", "tt", ygk + ["OF16" + hs, l0k], ["DM" + hs], HS, "g", out=sl(T.DM, h), in0=ysrc, in1=m0(L0, h, 0), op=OP.not_equal)
+            MM("wc", [(ps(P, 1), T.mI[:], m0(L0, h, 1), True, True, HS, False)], ["mI", l0k], ["P1" + hs], P)
+            V("DMW", "tt", ["P1" + hs, "DM" + hs], ["DMW" + hs], HS, 1.0, [P], out=sl(T.DMW, h), in0=ps(P, 1), in1=sl(T.DM, h), op=OP.mult)
+            MM("u", [(ps(Q, 2), T.mTH[:], m0(L0, h, 2), True, False, HS, False), (ps(Q, 2), T.mNB[:], sl(T.DM, h), False, True, HS, False)],
+               ["mNB", "mTH", "DM" + hs, l0k], ["Q2" + hs], Q)
+            A("TH", ["Q2" + hs, "cT"], ["TH" + hs], HS, [Q], out=sl(T.TH, h), in_=ps(Q, 2), func=AF.Relu, scale=2.0 ** 96, bias=col(cT))
+            MM("tt", [(ps(P, 2), T.mTB[:], sl(T.DMW, h), True, True, HS, False)], ["mTB", "DMW" + hs], ["P2" + hs], P)
+            V("FF", "tt", ["P2" + hs, "TH" + hs], ["FF" + th], HS, 1.0, [P], out=sl(FF, h), in0=ps(P, 2), in1=sl(T.TH, h), op=OP.is_gt)
+            send(t, "3" + hs, spk, sl(FF, h), sl(LF, h), ["FF" + th], ["LF" + th], 0)
         if not last:
             for h in range(NH):
                 hs = str(h)
-                cur_h[0] = h
-                V("tt", ["YU" + hs, "XD" + hs, "OF16" + hs], ["X"], HS, 3.5, (), 40, out=T.X[:, h * 2048:(h + 1) * 2048].indirect(T.OF16[:, 8 * h:8 * h + 8]),
+                at["h"] = h
+                V("PUT", "tt", ["YU" + hs, "XD" + hs, "OF16" + hs], ["X"], HS, "sc", out=T.X[:, h * 2048:(h + 1) * 2048].indirect(T.OF16[:, 8 * h:8 * h + 8]),
                   in0=sl(T.YU, h), in1=sl(T.XD, h), op=OP.add)
         for h in range(NH):
             hs = str(h)
-            cur_h[0] = h
-            b4, b6 = 4 + h, 6 + h
+            th = "%d_%d" % (t, h)
+            at["h"] = h
+            P, Q = 4 + h, 6 + h
             ws = slice(8 * h, 8 * h + 8)
-            V("tt", ["ASI", "LN" + hs, "KAP" + hs], ["CM" + hs], HS, 1.5, (), 40, out=sl(T.CM, h), in0=T.ASI[:].indirect(LN[:, ws]), in1=sl(T.KAP, h), op=OP.min)
-            V("tt", ["CM" + hs, "q" + hs], ["Cs" + hs], HS, 1.0, [b4], out=sl(T.C, h), in0=ps(b4, 2), in1=sl(T.CM, h), op=OP.max)
+            V("CM", "tt", ["ASI", "LN" + th, "SG" + hs], ["CM" + hs], HS, "g", out=sl(T.CM, h), in0=T.ASI[:].indirect(LN[:, ws]), in1=sl(T.SG, h), op=OP.mult)
+            V("Cs", "tt", ["CM" + hs, "Q3" + hs], ["Cs" + hs], HS, 1.0, [Q], out=sl(T.C, h), in0=ps(Q, 3), in1=sl(T.CM, h), op=OP.max)
             if not last:
-                V("cp", ["Cs" + hs], ["C16" + hs], HS, 1.0, out=sl(T.C16, h), in_=sl(T.C, h))
-            V("tt", ["ASH", "NS" + hs, "KH" + hs], ["HM" + hs], HS, 1.5, (), 40, out=sl(T.HM, h), in0=T.ASH[:].indirect(NS[:, ws]), in1=sl(T.KH, h), op=OP.min)
-            V("tt", ["HM" + hs, "key" + hs], ["HK" + hs], HS, 1.0, [b6], out=sl(T.HK, h), in0=ps(b6, 0), in1=sl(T.HM, h), op=OP.max)
+                V("C16", "cp", ["Cs" + hs], ["C16" + hs], HS, 1.0, out=sl(T.C16, h), in_=sl(T.C, h))
+            V("HM", "tt", ["ASI", "NS" + th, "KH" + hs], ["HM" + hs], HS, "g", out=sl(T.HM, h), in0=T.ASI[:].indirect(NS[:, ws]), in1=sl(T.KH, h), op=OP.min)
+            V("Hs", "tt", ["HM" + hs, "Q0" + hs], ["Hs" + hs], HS, 1.0, [Q], out=sl(T.H, h), in0=ps(Q, 0), in1=sl(T.HM, h), op=OP.max)
             if not last:
-                V("ts", ["HK" + hs, "cH"], ["H16" + hs], HS, 1.0, out=sl(T.H16, h), in0=sl(T.HK, h), scalar1=131072.0, scalar2=col(cH), op0=OP.mult, op1=OP.subtract)
+                V("H16", "cp", ["Hs" + hs], ["H16" + hs], HS, 1.0, out=sl(T.H16, h), in_=sl(T.H, h))
+            ff, lf, fk, lk = sl(FF, h), sl(LF, h), "FF" + th, "LF" + th
+            r, rm, ma, la, mb, lb = [sl(b, h) for b in (T.R, T.RM, T.MA, T.LA, T.MB, T.LB)]
+            V("MB", "tt", ["P3" + hs, fk], ["MB" + hs], HS, 1.0, [P], out=mb, in0=ps(P, 3), in1=ff, op=OP.mult)
+            MM("b", [(ps(Q, 1), T.mB[:], mb, True, True, HS, False)], ["mB", "MB" + hs], ["Q1" + hs], Q)
+            V("LB", "tt", ["Rs" + hs, "Q1" + hs], ["LB" + hs], HS, 1.0, [Q], out=lb, in0=ps(Q, 1), in1=r, op=OP.is_gt)
+            MM("rm", [(ps(P, 1), T.mI[:], r, True, False, HS, False), (ps(P, 1), T.mNI[:], mb, False, False, HS, False), (ps(P, 1), T.mIB[:], ff, False, False, HS, False),
+                      (ps(P, 1), T.mI[:], lb, False, True, HS, False)], ["mI", "mNI", "mIB", "Rs" + hs, "MB" + hs, "LB" + hs, fk], ["P1" + hs], P)
+            A("RM", ["P1" + hs], ["RM" + hs], HS, [P], out=rm, in_=ps(P, 1), func=AF.Copy)
+            V("MA", "tt", ["P1" + hs, lk], ["MA" + hs], HS, 1.0, [P], out=ma, in0=ps(P, 1), in1=lf, op=OP.mult)
+            MM("a", [(ps(Q, 1), T.mN16[:], ff, True, False, HS, False), (ps(Q, 1), T.mB[:], ma, False, True, HS, False)], ["mB", "mN16", "MA" + hs, fk], ["Q1" + hs], Q)
+            MM("r1", [(ps(P, 3), T.mI[:], rm, True, False, HS, False), (ps(P, 3), T.mBI[:], ff, False, False, HS, False), (ps(P, 3), T.mNI[:], ma, False, False, HS, False)],
+               ["mI", "mNI", "mBI", "RM" + hs, "MA" + hs, fk], ["P3" + hs], P)
+            V("LA", "tt", ["RM" + hs, "Q1" + hs], ["LA" + hs], HS, 1.0, [Q], out=la, in0=ps(Q, 1), in1=rm, op=OP.is_gt)
+            MM("r2", [(ps(P, 3), T.mI[:], la, False, True, HS, False)], ["mI", "LA" + hs], ["P3" + hs], P)
+            if not last:
+                orders(h, t + 1, ps(P, 3), ["P3" + hs], [P])
+                A("Rs", ["P3" + hs], ["Rs" + hs], HS, [P], out=r, in_=ps(P, 3), func=AF.Copy)
+                MM("z", [(ps(Q, 2), T.mZ0[:], m0(M0, h, 2), True, False, HS, False), (ps(Q, 2), T.mB[:], lf, False, True, HS, False)], ["mZ0", "mB", "th" + th, lk], ["Q2" + hs], Q)
+                A("th", ["Q2" + hs, "cTH"], ["th%d_%d" % (t + 1, h)], HS, [Q], out=m0(T["M0_%d" % (t + 1)], h, 2), in_=ps(Q, 2), func=AF.Relu, bias=col(cTH))
             else:
-                V("ts", ["HK" + hs, "cH"], ["OH" + hs], HS, 1.0, out=sl(T.OH, h), in0=sl(T.HK, h), scalar1=131072.0, scalar2=col(cH), op0=OP.mult, op1=OP.subtract)
-            if t == 0:
-                MM([(ps(b4, 3), T.mI[:], sl(T.R, h), True, True, HS, False)], ["mI", "Rs" + hs], ["t2" + hs], [b4])
-            cur, ck, pc, pk = T.R, "Rs" + hs, 3, "t2" + hs
-            for role, (f, fk) in enumerate([(LF, "LF%d_%d" % (t, h)), (FF, "FF%d_%d" % (t, h))]):
-                V("tt", [pk, fk], ["MA" + hs], HS, 1.0, [b4], out=sl(T.MA, h), in0=ps(b4, pc), in1=sl(f, h), op=OP.mult)
-                MM([(ps(b4, 1), T.mB[:], sl(T.MA, h), True, True, HS, False)], ["mB", "MA" + hs], ["cnt" + hs, "dB" + hs], [b4])
-                V("tt", [ck, "cnt" + hs], ["LA" + hs], HS, 1.0, [b4], out=sl(T.LA, h), in0=ps(b4, 1), in1=sl(cur, h), op=OP.is_gt)
-                nc, nk = (2, "q" + hs) if role == 0 else (3, "t2" + hs)
-                MM([(ps(b4, nc), T.mI[:], sl(cur, h), True, False, HS, False), (ps(b4, nc), T.mNI[:], sl(T.MA, h), False, False, HS, False),
-                    (ps(b4, nc), T.mI[:], sl(T.LA, h), False, True, HS, False)], ["mI", "mNI", ck, "MA" + hs, "LA" + hs], [nk], [b4])
-                if role == 0:
-                    A([nk], ["Rq" + hs], HS, [b4], out=sl(T.R1, h), in_=ps(b4, nc), func=AF.Copy)
-                    cur, ck = T.R1, "Rq" + hs
-                elif not last:
-                    orders(h, t + 1, ps(b4, nc), [nk], [b4])
-                    A([nk], ["Rs" + hs], HS, [b4], out=sl(T.R, h), in_=ps(b4, nc), func=AF.Copy)
-                else:
-                    A([nk], ["OR" + hs], HS, [b4], out=sl(T.OR, h), in_=ps(b4, nc), func=AF.Copy)
-                pc, pk = nc, nk
-            lfs = ["LF%d_%d" % (u, h) for u in range(t + 1)]
-            if not last:
-                q0, qk = m0(M0, h, 2), "th%d_%d" % (t, h)
-                MM([(ps(b6, 1), T.mI[:], q0, True, False, HS, False), (ps(b6, 1), T.mB[:], sl(LF, h), False, True, HS, False)], ["mI", "mB", qk, lfs[t]], ["mk" + hs], [b6])
-                V("ts", ["mk" + hs], ["IND" + hs], HS, 1.0, [b6], out=sl(T.IND, h), in0=ps(b6, 1), scalar1=3.5, scalar2=-4.0, op0=OP.is_gt, op1=OP.mult)
-                MM([(ps(b6, 2), T.mI[:], q0, True, False, HS, False), (ps(b6, 2), T.mB[:], sl(LF, h), False, False, HS, False), (ps(b6, 2), T.mI[:], sl(T.IND, h), False, True, HS, False)],
-                   ["mI", "mB", qk, lfs[t], "IND" + hs], ["tt" + hs, "xc" + hs], [b6])
-                A(["tt" + hs], ["th%d_%d" % (t + 1, h)], HS, [b6], out=m0(T["M0_%d" % (t + 1)], h, 2), in_=ps(b6, 2), func=AF.Copy)
-            else:
-                MM([(ps(b6, 1), T.mI[:], sl(T.AB, h), True, False, HS, False)] + [(ps(b6, 1), T.mB[:], sl(T["LF_%d" % u], h), False, u == t, HS, False) for u in range(t + 1)],
-                   ["mI", "mB", "AB"] + lfs, ["mk" + hs], [b6])
-                A(["mk" + hs], ["OA" + hs], HS, [b6], out=sl(T.OA, h), in_=ps(b6, 1), func=AF.Copy)
+                A("Rs", ["P3" + hs], ["OR" + hs], HS, [P], out=sl(T.OR, h), in_=ps(P, 3), func=AF.Copy)
+                oa = T["pb%d" % Q][0:8, 256:384]
+                MM("z", [(oa, T.mI[0:8, 0:8], T.A8[:, h * HS:(h + 1) * HS], True, False, HS, False)] +
+                   [(oa, T.mB[:, 0:128:16], sl(T.LF, NH * u + h), False, u == t, HS, False) for u in range(RO)],
+                   ["mI", "mB", "A8"] + ["LF%d_%d" % (u, h) for u in range(RO)], ["Q2" + hs], Q)
+                A("th", ["Q2" + hs], ["OA" + hs], HS, [Q], out=sl(T.OA, h), in_=oa, func=AF.Copy)
 
     def store(i, q, dst, src, rd):
         e = g.sync if q == "Y" else g.scalar
-        add(q, lambda: e.dma_start(out=dst, in_=src), rd, ["out%d" % i], 60, sem="st_%d" % i, val=16, lat=2000)
+        add(q, "st%d" % i, lambda: e.dma_start(out=dst, in_=src), rd, ["out%d" % i], "dma", sem="st_%d" % i, val=16, lat=2000)
     for h in range(NH):
         store(h, "Y", sl(T.yctx, h), sl(T.C, h), ["Cs%d" % h])
-        store(2 + h, "Y", sl(T.ycand, h), sl(T.OH, h), ["OH%d" % h])
+        store(2 + h, "Y", sl(T.ycand, h), sl(T.H, h), ["Hs%d" % h])
         store(4 + h, "Y", sl(T.ypref, h), sl(T.OR, h), ["OR%d" % h])
-        store(6 + h, "Y", sl(T.yfail, h), T.OA[0:128:16, h * HS:(h + 1) * HS], ["OA%d" % h])
+        store(6 + h, "Y", sl(T.yfail, h), sl(T.OA, h), ["OA%d" % h])
     return ops
 
 
+def price(o, m):
+    q, c = o["q"], o["cost"]
+    if c == "dma":
+        return 60.0, 60.0 + o["lat"] * m["dma"]
+    if q == "N":
+        return 0.0, m["hop"] + o["lat"]
+    if q == "G":
+        d = m["issue"] if c == "issue" else 130.0 + 2 * c * m["cy"]
+    elif q == "T":
+        d = c * m["pe"] + m["ovT"]
+    else:
+        n, rate = c
+        if rate in ("g", "sc"):
+            d = n * m[rate] * m["cy"] + (50.0 if q == "V" else max(65.0, m["ovS"]))
+        elif q == "V":
+            d = max(64, n * rate) * m["cy"] + m["ovV"]
+        else:
+            d = n * m["cy"] + m["ovS"]
+        d *= 1 + len(o.get("more", ()))
+    return d, d
+
+
 def depend(ops):
-    lastw, readers, lastb = {}, {}, {}
+    lastw, readers = {}, {}
     deps = []
     for i, o in enumerate(ops):
-        d = {}
-        for k in o["rd"]:
-            for w in lastw.get(k, ()):
-                d[w] = True
+        d = set()
+        for k in o["rd"] + o["wr"]:
+            if k in lastw:
+                d.add(lastw[k])
         for k in o["wr"]:
-            for w in lastw.get(k, ()):
-                d[w] = True
-            for r in readers.get(k, ()):
-                if r != i:
-                    d[r] = True
-        for b in o["bk"]:
-            if b in lastb:
-                d.setdefault(lastb[b], False)
+            d.update(readers.get(k, ()))
         if "after" in o:
-            d[o["after"]] = True
+            d.add(o["after"])
         deps.append(d)
         for k in o["rd"]:
             readers.setdefault(k, []).append(i)
         for k in o["wr"]:
-            lastw[k] = [i]
+            lastw[k] = i
             readers[k] = []
-        for b in o["bk"]:
-            lastb[b] = i
     return deps
 
 
-BIAS = {'SYG1': -7000, 'Gsnd0': -8000, 'Gsnd1': -8000, 'VSC0': 40000, 'VSC1': 20000, 'VX1': 20000, 'VX0': 20000, 'SG1': -4000, 'VXD0': 20000, 'VMA0': -1000, 'Sw0': 23000, 'SIW0': 17000, 'SIW1': 17000, 'VN0': 2000, 'VN1': 1000, 'SABS0': -2000, 'SABS1': -2000, 'VASH0': 1000, 'VH0': 3000, 'VTMP0': 6000, 'Tkey1': -2000, 'VTJ0': 20000, 'VTJ1': 20000, 'YFIN0': 8000, 'YFIN1': 8000, 'SG0': -3000, 'VXG0': 1000, 'VKT1': 1000, 'VMK0': 8000, 'VMK1': 8000, 'VMA1': 1000, 'Tmk0': -2000, 'Tmk1': -1000, 'SRs0': 8000, 'VTI1': 1000, 'VmKC0': 8000, 'VmKC1': 8000, 'Twc0': 3000, 'VDSC0': 1000, 'VcKC0': 20000, 'VcKC1': 20000, 'VCNT0': -1000, 'VCNT1': -1000, 'NLF0': -17000, 'NLF1': -20000, 'Tq1': -3000, 'Tq0': -3000, 'SE0': -20000, 'Sw1': -6000, 'NLN1': -1000, 'SYG0': -2000, 'Vx0p1': 3000, 'Vx0p0': 3000, 'VmI0': 3000, 'VmI1': 3000, 'Tkey0': 1000, 'STH1': -12000, 'STH0': -9000, 'VOF1': -1000, 'Tring0': -2000, 'VDSC1': 3000, 'VHM0': 20000, 'VK1': -3000, 'SRq0': 48000, 'SX0': -20000, 'SX1': -20000, 'VUND0': -1000, 'VUND1': -1000, 'VIND0': 1000, 'VKT0': 20000, 'SOR1': -20000, 'SOR0': -20000, 'Tring1': -1000, 'SRq1': 28000, 'VKK1': 20000, 'VHM1': -3000, 'GIMK0': -8000, 'VTMP1': 9000, 'VHK0': 20000, 'VHK1': 20000, 'Tt0': 20000, 'Tt1': 20000, 'VLA1': 22000, 'SEA1': 1000, 'GCII0': 8000, 'VLA0': 2000, 'Vbias0': 8000, 'VDMW1': 3000, 'VcPm0': 8000, 'VcPm1': 8000, 'VKAP1': 3000, 'Vc16P0': -1000, 'Vc16P1': -1000, 'VFF0': 3000, 'VYU0': -1000}
+def gap(a, b, m):
+    if b == "N":
+        return 0.0
+    if a != b:
+        return m["wake"]
+    return 0.0 if a in "TG" else m["self"]
 
 
-def klass(o):
-    w = o["wr"][0] if o["wr"] else "snd" + o["remote"][0].split("_")[1][0]
-    a = w.split("_")[0]
-    while a and a[-1].isdigit():
-        a = a[:-1]
-    return "%s%s%d" % (o["q"], a, o["h"])
-
-
-def schedule(ops, deps):
+def sequence(ops, deps, off, m):
     n = len(ops)
-    succ = [[] for _ in range(n)]
-    for i, d in enumerate(deps):
-        for j in d:
-            succ[j].append(i)
-    WAKE, alpha, win = CFG["wake"], CFG["alpha"], CFG["win"]
-    prio = [0.0] * n
+    key = [None] * n
     for i in range(n - 1, -1, -1):
-        m = 0.0
-        for j in succ[i]:
-            m = max(m, prio[j] + (WAKE if ops[j]["q"] != ops[i]["q"] else 30.0))
-        prio[i] = m + ops[i]["cost"] + ops[i]["lat"]
+        o = ops[i]
+        if o["name"] in off:
+            key[i] = o["t"] * PERIOD + off[o["name"]]
+        elif key[i] is None:
+            key[i] = RO * PERIOD * 2
+        for j in deps[i]:
+            if ops[j]["name"] not in off:
+                k = key[i] - price(ops[j], m)[1]
+                key[j] = k if key[j] is None else min(key[j], k)
     for i in range(n):
-        if ops[i]["h"] == 0:
-            prio[i] += CFG["bonus"]
-        prio[i] += BIAS.get(klass(ops[i]), 0.0)
-    left = [len(d) for d in deps]
-    ready = [0.0] * n
-    fin = [0.0] * n
-    beg = [0.0] * n
-    avail = {}
-    free = {}
-    for i in range(n):
-        avail.setdefault(ops[i]["q"], [])
-        free.setdefault(ops[i]["q"], 0.0)
-        if left[i] == 0:
-            avail[ops[i]["q"]].append(i)
-    order = []
-    while True:
-        best = None
-        for q in avail:
-            if not avail[q]:
-                continue
-            fq = free[q] if q != "N" else 0.0
-            est = min(max(fq, ready[i]) for i in avail[q])
-            i, top = None, None
-            for z in avail[q]:
-                zs = max(fq, ready[z])
-                if zs <= est + win:
-                    sc = prio[z] - alpha * (zs - est)
-                    if top is None or sc > top:
-                        i, top = z, sc
-            st = max(fq, ready[i])
-            if best is None or st < best[0]:
-                best = (st, i, q)
-        if best is None:
-            break
-        st, i, q = best
-        avail[q].remove(i)
-        order.append(i)
-        beg[i] = st
-        free[q] = st + ops[i]["cost"]
-        fin[i] = st + ops[i]["cost"] + ops[i]["lat"]
-        for j in succ[i]:
-            ready[j] = max(ready[j], fin[i] + (WAKE if ops[j]["q"] != q else (30.0 if deps[j][i] else 0.0)))
-            left[j] -= 1
-            if left[j] == 0:
-                avail[ops[j]["q"]].append(j)
-    return order, beg, fin
+        for j in deps[i]:
+            key[i] = max(key[i], key[j])
+    return sorted(range(n), key=lambda i: (key[i], i))
+
+
+def place(ops, deps, seq, m):
+    busy = {q: [] for q in "VSTGY"}
+    bank = {b: [] for b in range(8)}
+    n = len(ops)
+    beg, fin = [0.0] * n, [0.0] * n
+    wake = m["wake"]
+    for i in seq:
+        o = ops[i]
+        q = o["q"]
+        d, e = price(o, m)
+        st = 0.0
+        for j in deps[i]:
+            st = max(st, fin[j] + gap(ops[j]["q"], q, m))
+        if q != "N":
+            moved = True
+            while moved:
+                moved = False
+                for lst, pad in [(busy[q], 0.0)] + [(bank[b], wake) for b in o["bk"]]:
+                    k = len(lst) - 1
+                    while k >= 0 and lst[k][0] + 3000.0 > st:
+                        k -= 1
+                    for a, z, w in lst[k + 1:]:
+                        if pad and w == q:
+                            continue
+                        if a - pad >= st + d:
+                            break
+                        if z + pad > st:
+                            st = z + pad
+                            moved = True
+            for lst in [busy[q]] + [bank[b] for b in o["bk"]]:
+                k = len(lst)
+                while k and lst[k - 1][0] > st:
+                    k -= 1
+                lst.insert(k, (st, st + d, q))
+        beg[i], fin[i] = st, st + e
+    return beg, fin
+
+
+def settle(ops, deps, beg):
+    order = sorted(range(len(ops)), key=lambda i: (beg[i], i))
+    used = {b: {} for b in range(8)}
+    full = [None] * len(ops)
+    for i in order:
+        full[i] = set(deps[i])
+        for b in ops[i]["bk"]:
+            full[i].update(j for e, j in used[b].items() if e != ops[i]["q"])
+            used[b][ops[i]["q"]] = i
+    return order, full
 
 
 def rank_program(g, core, T, topo):
@@ -578,10 +619,10 @@ def rank_program(g, core, T, topo):
     if rank is None:
         return
     ops = build(g, T, topo, rank, core)
-    deps = depend(ops)
     if "o" not in _ORDER:
-        _ORDER["o"] = schedule(ops, deps)[0]
-    order = _ORDER["o"]
+        deps = depend(ops)
+        _ORDER["o"] = settle(ops, deps, place(ops, deps, sequence(ops, deps, OFF, COST), COST)[0])
+    order, full = _ORDER["o"]
     eng = {"V": g.vector, "S": g.scalar, "T": g.tensor, "G": g, "Y": g.sync}
     cnt = {}
     done = {}
@@ -596,11 +637,8 @@ def rank_program(g, core, T, topo):
             cnt[o["sem"]] = o["val"]
             continue
         need = {}
-        for d, raw in deps[i].items():
-            od = ops[d]
-            if od["q"] == q and od["sem"] is None and (not raw or q in "TG"):
-                if not (q == "G"):
-                    continue
+        for d in full[i]:
+            if ops[d]["q"] == q and q in "TG":
                 continue
             s, v = done[d]
             if know[q].get(s, 0) < v and (s not in need or need[s][0] < v):
@@ -620,18 +658,17 @@ def rank_program(g, core, T, topo):
         ins = o["fn"]()
         if "remote" in o:
             cnt[o["remote"][0]] = o["remote"][1]
-            done[i] = None
             continue
         s = o["sem"] or "s" + q
         inc = o["val"] if o["sem"] else 1
         ins.then_inc(T.sem[s], inc)
         cnt[s] = cnt.get(s, 0) + inc
+        for fn in o.get("more", ()):
+            fn().then_inc(T.sem[s], 1)
+            cnt[s] += 1
         done[i] = (s, cnt[s])
-        c = dict(know[q])
-        c[s] = cnt[s]
-        if o["sem"] is None:
-            know_self = c
-        clock[i] = c
+        clock[i] = dict(know[q])
+        clock[i][s] = cnt[s]
     for s in cnt:
         if know["G"].get(s, 0) < cnt[s]:
             g.wait_ge(T.sem[s], cnt[s])

@@ -16,14 +16,16 @@ CFG = {"npc": 4,
        "vc0": ((0, 1), (0, 3)),
        "vh": (),
        "ns": (0, 0),
-       "es": (0, 0),
-       "nq": (2, 1),
-       "bitV": (1, 1)}
-COST = {"cy": 1.0, "g": 1.5, "sc": 3.5, "ovV": 12.0, "ovS": 40.0, "pe": 0.51, "ovT": 20.0, "wake": 120.0, "self": 40.0, "issue": 700.0, "hop": 2000.0, "dma": 1.0}
+       "es": (0, 2),
+       "esL": (0, 0),
+       "nq": (2, 2),
+       "nk": (4, 8),
+       "bitV": (1, 1), "mbS": (1, 0), "maS": (0, 0), "dmwS": (1, 0), "yS": (0, 0), "x0G": (1, 1), "xbS": (1, 1), "early": 1, "own": (3,)}
 PERIOD = 20000.0
-OFF = {_a.split(":")[0]: float(_a.split(":")[1]) for _a in """
-DW3A:-23230 dx2A:-14900 DW0A:-13545 dx1A:-10886 UNDB:-10371 DSCA:-9718 DW1A:-8670 G0A:-6534 N32A:-6519 dx3A:-6242 sk3A:-6101 wordA:-5862 sk4A:-5804 DW6A:-5704 cnt0A:-5186 ABSA:-4432 G2A:-3850 DW2A:-3792 TIA:-3131 sk2A:-2716 DW7A:-2456 TJA:-1046 key0A:-1036 dx0B:-893 dx7A:-562 sk7A:-429 dx5A:56 E3B:474 x0pB:489 x0pA:662 BITB:722 XG1A:727 RMA:775 ABSB:867 XG0A:1080 cnt3A:1126 G1A:1226 sk0A:1321 dx2B:1401 DW4A:1505 XG3A:1664 send1A:2090 XG2A:2270 ndA:2356 G0B:2496 G2B:2513 E1B:2554 dx0A:2671 XG1B:2735 dx1B:2786 YUB:2827 DW0B:2843 key0B:2856 G3A:3378 FFB:3395 KHA:3711 send2A:3755 LBB:3978 DW5A:4115 cnt1A:4305 sk6A:4562 dx4A:4598 G1B:4646 DW3B:4650 cnt3B:4675 khB:4676 E2B:4681 dx6A:4745 sk1A:4753 sk5A:4822 cnt2A:4882 XG0B:4887 C16B:5010 wB:5139 xbA:5171 XG3B:5197 TJB:5270 K32A:5322 BITA:5322 sk3B:5459 DW2B:5472 N32B:5591 G3B:5639 DW1B:5791 x0A:6035 dx3B:6138 YG0B:6178 mkB:6205 ndB:6244 XG2B:6309 DSCB:6377 qA:6760 dBB:7123 sk2B:7230 UNDA:7984 wcA:8010 NSB:8126 SGA:8140 KKA:8273 KKB:8405 wordB:8819 sk1B:8884 sk0B:9088 send1B:9095 zB:9176 YG2A:9315 uA:9577 key2A:9686 send0B:9697 MBA:10018 E1A:10219 dBA:10387 x0B:10534 YG1A:11012 HsA:11044 DMA:11054 E0A:11189 KTB:11484 YG0A:11992 YG3A:12060 mkA:12076 cnt2B:12371 xbB:12484 YG3B:12494 TIB:12994 key3A:13077 E0B:13159 cnt1B:13428 wcB:13614 CsB:13909 LBA:13973 FFA:13979 E2A:14039 RMB:14075 cnt0B:14207 xpA:14259 K32B:14284 ttA:14292 IWA:14389 NSA:14422 OFA:14840 SCA:14867 YUA:14875 H16A:15146 YG2B:15304 KTA:15529 r2A:15650 key2B:15980 r1B:16147 YG1B:16238 THB:16317 key3B:16379 aB:16401 H16B:16406 r2B:16502 DMB:16679 uB:16725 xpB:16934 khA:16935 key1A:17150 E3A:17163 CsA:17401 key1B:17444 CMB:17514 ttB:17536 DMWA:18081 SCB:18496 XDA:19051 send3A:19116 MAA:19416 PUTB:19487 PUTA:19540 THA:19755 IWB:20130 LAA:20132 OFB:20134 MBB:20231 LAB:20249 SGB:20291 CMA:20358 r1A:20359 bA:20398 aA:20438 rmB:20538 C16A:20542 zA:20594 XDB:20842 rmA:20917 bB:21439 thB:21478 DMWB:21478 qB:21863 wA:22018 thA:23025 MAB:24069 RsA:24194 RsB:24327 send2B:25729 send3B:26436 HMA:26503 KHB:27771 HMB:29276 HsB:35289
-""".split()}
+PLACES = """
+XG1A RMA3+ MBB+ aA+ XG1A3 ZDA_+ mBIA_+ mIBA_+ thB_+ zA_+ thA_+ send4A XG0A LAA+ qB+ bB+ r2A+ dx1A3 HMB+ LBB+ dx2A MAA3+ CMB+ XG2A dx0A dx1A dx0A3 dx2A3 send3B+ XG2A3 dx3A3 dx3A rmB+ send2B3+ CsB+ C16B+ wA+ DW0A3 st1B3++ XG3A3 HsB3+ sk0A3 dx4A3 fP1A_+ DW2A3 st5B3++ XG3A ldASIA_+ DW1A3 dx6A3 sk1A3 RMB3+ DW2A dx6A CMB3+ CsB3+ thA3+ fP2A_+ DW0A dx5A3 DW1A aA3+ LAA3+ DW3A MAB+ DW3A3 dx7A3 r1A3+ cN16A_ DW4A3 DW6A send3B3+ cEA_ XG0B XG1B dx4A sk0A dx5A sk2A3 sk3A3 sk4A3 XG1B3 DW4A aB+ sk1A dx7A XG0B3 DW6A3 DW5A RMB+ DW5A3 DW7A3 DW7A TMPA_+ HMA+ MAB3+ XG2B x0A3 sk2A sk3A sk4A XG2B3 zB3+ inH16A_+ LAB+ HsA+ sk5A3 sk6A3 HsB+ inHsA_+ sk7A3 ABSA3 H16A+ cTA_+ H16B+ G0A3 G3A3 G1A3 G2A3 sk5A sk6A sk7A ABSA dx1B3 XG3B r1B+ dx0B r2B+ dx1B XG3B3 wB+ IWA+ xbA xbA3 YG0A3 IWB+ cOFA_+ G3A G2A G0A G1A DW0B dx4B DW4B DW1B fP0A_+ dx0B3 DW0B3 ORA3+ dx4B3 HsA3+ cnt0A3 cnt1A3 cnt0A cnt1A DW4B3 DW1B3 cnt2A cnt3A dx5B sk0B cnt2A3 fIA_+ YG0A BITA cnt3A3 dx5B3 DW5B YG1A YG0B BITA3 wordA TIA sk1B TJA sk0B3 sk4B x0A YG0B3 YG3A3 DW5B3 x0pA mTHA_+ wordA3 TIA3 TJA3 aB3+ IWB_+ sk5B sk1B3 sk4B3 ONESA_ ABSB G0B cnt0B G1B cnt1B G2B cnt2B G3B cnt3B BITB x0B x0B3 x0pA3 send1A3 mCWA_+ YG2A YG3A xbB sk5B3 ABSB3 G0B3 cnt0B3 G1B3 cnt1B3 G2B3 cnt2B3 G3B3 cnt3B3 xbB3 wordB cDWA_ BITB3 KIA_ YG1A3 cKA_ cK0A_ cPA_ zB+ wordB3 r1B3+ dBB inCsA_+ cG16A_ RsA+ xpA3 TIB cWA_ dBA3 khA3 send1A xpA TIB3 TJB3 x0pB3 TJB x0pB send1B IMGA_ cNHA_ DSCA dBB3 khB3 E1A E0A send1B3 YG2A3 DSCA3 E1A3 E0A3 khB E2A dBA cZ1A_ cQbA_ YG2B3 E3A ndA3 E2A3 key0A3 key1A3 key2A3 khA ndA key0A key1A key2A key3A E3A3 cZA_ key3A3 KTA3 DSCB3 ldRINA_ YG2B c16PA_ YG3B3 thB+ YG1B YG3B mN32A_+ YG1B3 fP3A_+ xpB3 KTA CBIA_+ send0B3 SCA st4B3+ SGB3 CBA_+ cy2B xpB UNDA SCA3 ndB3 m16A_+ send0B IMA_ SGA XDA mHIA_+ E1B DSCB dy2B E1B3 E0B3 st2B3+ mkA cy3B SGA3 dy3B K32A N32A KKA E2B3 NSA mkA3 ldXA_ mBA_ key0B3 key1B3 key2B3 E3B3 mNBA_+ OFA DMA UNDB mZ0A_ K32A3 KKA3 OFA3 ES2B mIA_ key2B cb2A_ DMA3 send2A E0B key3B3 KTB3 ZA_ ndB mN16A_+ KHA3 SCB3 YUA N32A3 st0B3+ ES3B st3B3+ ZUA_ cQaA_ wcA wcB3 st6B3+ uA NSA3 DMWA THA key3B Z1A_ ttA wcA3 DMWA3 mNIA_ zdA_ RNDB key0B uA3 ldFINA_ mkB3 cKCA_ MSB FFA tbA_ key1B KHA XDB inRB_ inRA_ mUA_+ mN4kA_+ kmB KTB SCB PUTA CMA THA3 ldCINA_ A8A_ SGB qA cTHA_ mbA ttA3 RsB+ K32B3 qA3 mkB MBA FFA3 CsA K32B send2A3 wcB bA KKB3 OFB3 DMB3 uB3 THB3 cbwA_ Q8IA_ mNBUA_ KKB mG8A_ N32B OFB NSB ldHINA_ N32B3 DMB uB NSB3 LAB3+ ORB3+ Q8A_ DMWB3 LBA rmA mbA3 inC16A_ thB3+ ttB3 FFB3 YUB MBB3 CMA3 MBA3 bA3 LBA3 cQA_ THB qB3 r0B_ KHB DMWB ttB PUTB C16A CsA3 send3A3 FFB wB_ RMA bB3 LBB3 IWA_ rmA3 mTBA_ ibA_ rmB3 send3A MAA zA thA XG0A3- HMA3 wA_ mWBA_ send2B IPA_- KHB3 HMB3 zA3 st7B3+ zB_ r1A SDA_
+""".split()
+OFF = {_a.rstrip("+-"): (_i + 0.5) * PERIOD / len(PLACES) + PERIOD * (_a.count("+") - _a.count("-")) for _i, _a in enumerate(PLACES)}
 
 SCRATCH = {}
 for _n, _s, _d in [
@@ -33,7 +35,7 @@ for _n, _s, _d in [
     ("A8", [8, S], "bfloat16"), ("Q8", [8, S], "bfloat16"),
     ("C", [128, S], "float32"), ("C16", [128, S], "uint16"), ("H", [128, S], "float32"), ("H16", [128, S], "uint16"),
     ("R", [128, S], "bfloat16"), ("RM", [128, S], "bfloat16"), ("MA", [128, S], "bfloat16"), ("LA", [128, S], "bfloat16"),
-    ("MB", [128, S], "bfloat16"), ("LB", [128, S], "bfloat16"), ("IW", [128, S], "bfloat16"),
+    ("MB", [128, S], "bfloat16"), ("LB", [128, S], "bfloat16"), ("IW", [128, S], "bfloat16"), ("WB", [128, S], "bfloat16"), ("YS", [128, S], "bfloat16"),
     ("AB1", [128, S], "bfloat16"), ("BIT", [128, S], "bfloat16"), ("TI", [128, S], "int32"), ("TJ", [128, S], "int32"), ("SG", [128, S], "bfloat16"),
     ("CM", [128, S], "float32"), ("KH", [128, S], "float32"), ("HM", [128, S], "float32"), ("UND", [128, S], "bfloat16"), ("DSC", [128, S], "bfloat16"),
     ("XD", [128, S], "bfloat16"), ("YU", [128, S], "bfloat16"), ("KT", [128, S], "float32"), ("SC", [128, S], "float32"),
@@ -41,37 +43,31 @@ for _n, _s, _d in [
     ("K32", [128, 16], "int32"), ("N32", [128, 16], "int32"), ("KK", [128, 16], "int32"), ("OF16", [128, 16], "uint16"),
     ("DM", [128, S], "bfloat16"), ("DMW", [128, S], "bfloat16"), ("TH", [128, S], "float32"),
     ("OR", [128, S], "float32"), ("OA", [8, S], "float32"),
-    ("IP", [128, 1], "int32"), ("KI", [128, 1], "int32"), ("B4I", [128, 1], "int32"), ("COL", [128, 24], "float32"), ("THC", [128, 16], "float32"), ("COLB", [128, 2], "bfloat16"),
+    ("IP", [128, 1], "int32"), ("KI", [128, 1], "int32"), ("B4I", [128, 1], "int32"), ("COL", [128, 32], "float32"), ("THC", [128, 16], "float32"), ("COLB", [128, 2], "bfloat16"),
     ("IM", [128, 160], "bfloat16"), ("IMG", [128, 128], "bfloat16"), ("IMK", [128, 128], "bfloat16"),
     ("Z", [128, 144], "bfloat16"), ("ZU", [128, 144], "bfloat16"), ("Z1", [128, 144], "bfloat16"), ("ZD", [128, 144], "bfloat16"), ("ZH", [128, 144], "bfloat16"), ("ZDH", [128, 144], "bfloat16"),
-    ("mB", [128, 128], "bfloat16"), ("mI", [128, 128], "bfloat16"), ("mNI", [128, 128], "bfloat16"), ("mNB", [128, 128], "bfloat16"), ("mNBU", [128, 128], "bfloat16"),
-    ("mTB", [128, 128], "bfloat16"), ("mWB", [128, 128], "bfloat16"), ("mCW", [128, 128], "bfloat16"),
-    ("mIB", [128, 128], "bfloat16"), ("mBI", [128, 128], "bfloat16"), ("mN16", [128, 128], "bfloat16"), ("mN4k", [128, 128], "bfloat16"), ("mU", [128, 128], "bfloat16"),
-    ("mTH", [128, 128], "bfloat16"), ("mZ0", [128, 128], "bfloat16"),
-    ("ONES", [128, 128], "bfloat16"), ("BIG", [128, 128], "bfloat16"), ("mI2", [128, 128], "bfloat16"), ("TMP", [128, 128], "bfloat16"), ("MK0", [128, 128], "bfloat16"),
     ("fI", [128, 128], "float32"), ("fP", [128, 512], "float32"), ("SD", [128, 128], "float32"), ("CB", [128, 8], "float32"), ("CBI", [128, 8], "float32"),
     ("mG8", [8, 128], "bfloat16"),
 ]:
     SCRATCH[_n] = ("sbuf", _s, _d)
-for _n in ("FF", "LF"):
+for _n in "mB mI mNI mNB mNBU mTB mWB mCW mIB mBI mN16 mN4k mU mTH mZ0 ONES BIG TMP MK0 m16 mHI mN32".split():
+    SCRATCH[_n] = ("sbuf", [128, 128], "bfloat16")
+for _n in ("FF", "LF", "M1", "L1"):
     SCRATCH[_n] = ("sbuf", [128, RO * S], "bfloat16")
-for _t in range(RO):
-    SCRATCH["M0_%d" % _t] = ("sbuf", [128, 3 * S], "bfloat16")
-    SCRATCH["L0_%d" % _t] = ("sbuf", [128, 3 * S], "bfloat16")
-    for _n in ("M1_", "L1_"):
-        SCRATCH[_n + str(_t)] = ("sbuf", [128, S], "bfloat16")
-    for _n in ("NS_", "LN_"):
-        SCRATCH[_n + str(_t)] = ("sbuf", [128, 16], "uint16")
+for _n in ("M0", "L0"):
+    SCRATCH[_n] = ("sbuf", [128, RO * 3 * S], "bfloat16")
+for _n in ("NS", "LN"):
+    SCRATCH[_n] = ("sbuf", [128, RO * 16], "uint16")
 for _b in range(8):
     SCRATCH["pb%d" % _b] = ("psum", [128, 512], "float32")
 
-SEMAPHORES = ["sT", "sV", "sS", "sG"]
+SEMAPHORES = ["sT", "sV", "sS", "sG", "r0_4", "l0_4"]
 SEMAPHORES += ["ld_%s" % _n for _n in ("x", "ctx", "cand", "pref", "assoc", "fail0")] + ["st_%d" % _i for _i in range(8)]
 for _t in range(RO):
     for _m in ("0", "10", "11", "20", "21", "30", "31"):
         SEMAPHORES += ["r%d_%s" % (_t, _m), "l%d_%s" % (_t, _m)]
 
-cP, cK, cG16, cZ, cZ1, cPp, cPm, cS0, cS1, cKC, cOF, c16P, cW, cT, cE, cTH, cQa, cQb, cQ, cK0, c80, c81 = range(22)
+cP, cK, cG16, cZ, cZ1, cPp, cPm, cS0, cS1, cKC, cOF, c16P, cW, cT, cE, cTH, cQa, cQb, cQ, cK0, c80, c81, cN16, cNH, cDW = range(25)
 
 _ORDER = {}
 
@@ -114,14 +110,19 @@ def build(g, T, topo, rank, core):
         lock = ["bank%d" % bank]
         add("T", name, fn, rd + (lock if whole else []), wr + ([] if whole else lock), sum(max(64, n) * (4 if f else 1) for o, l, r, a, b, n, f in lst), [bank])
 
+    def SUM(name, bank, region, terms, start=True, stop=True):
+        o = ps(bank, region)
+        MM(name, [(o, T[m][:], x, start and j == 0, stop and j == len(terms) - 1, HS, m == "fI") for j, (m, x, k) in enumerate(terms)],
+           [m for m, x, k in terms] + [z for m, x, k in terms for z in (k if isinstance(k, list) else [k])], ["ps%d%d" % (bank, region)], bank)
+
     def col(i):
         return T.COL[:, i:i + 1]
 
     def sl(b, h):
         return b[:, h * HS:(h + 1) * HS]
 
-    def m0(b, h, j):
-        return b[:, (3 * h + j) * HS:(3 * h + j + 1) * HS]
+    def m0(b, t, h, j):
+        return sl(b, NH * (3 * t + j) + h)
 
     def ps(b, r):
         return T["pb%d" % b][:, r * 128:(r + 1) * 128]
@@ -139,7 +140,7 @@ def build(g, T, topo, rank, core):
     ldw("Y", "fail0", "FIN", T.FIN[:], T.fail0[:], 2400)
     ldw("Y", "cand", "HIN", T.HIN[:], T.cand[:], 2400)
     ldw("Y", "assoc", "ASI", T.ASI[:], T.assoc[:], 6500)
-    ops[-1]["rd"] = ["X"]
+    ops[-1]["rd"] = ops[-2]["rd"] = ["X"]
 
     def iota(dst, key, pattern, base, cm, n, flag=True):
         if flag:
@@ -151,8 +152,10 @@ def build(g, T, topo, rank, core):
     iota(T.IP[:], "IP", [[1, 1]], 0, 1, 1, False)
     iota(T.IM[:], "IM", [[1, 160]], 0, 0, 160)
     iota(T.IMG[:], "IMG", [[16, 8], [0, 16]], 0, 0, 128)
-    iota(T.IMK[:], "IMK", [[0, 8], [1, 16]], 0, 0, 128)
     iota(T.CBI[:], "CBI", [[-16, 8]], 127, 0, 8)
+
+    def pick(key, out, src, skey, pattern, op, other, base, cm):
+        add("G", key, lambda: g.affine_select(out, src, pattern, op, other, base, cm), [skey], [key], 148)
 
     def ts(key, out, src, skeys, n, rate, a, b=None, op0=OP.add, op1=None):
         if op1 is None:
@@ -169,10 +172,7 @@ def build(g, T, topo, rank, core):
     def scaled(key, skey, c, n=128):
         A(key, [skey], [key], n, out=T[key][:, 0:n], in_=T[skey][:, 0:n], func=AF.Copy, scale=c)
 
-    def less(key, a, b, n=128):
-        V(key, "tt", [a, b], [key], n, 2.0, out=T[key][:], in0=T[a][:], in1=T[b][:], op=OP.subtract)
-
-    for key, dst, src in (("C16", T.C16, "CIN"), ("Rs", T.R, "RIN"), ("H16", T.H16, "HIN"), ("Cs", T.C, "CIN"), ("Hs", T.H, "HIN")):
+    for key, dst, src in (("C16", T.C16, "CIN"), ("H16", T.H16, "HIN"), ("Cs", T.C, "CIN"), ("Hs", T.H, "HIN")):
         V("in" + key, "cp", [src], [key + "0", key + "1"], S, out=dst[:], in_=T[src][:])
     ts("KI", T.KI[:], T.IP[:], ["IP"], 1, 1.0, 15, op0=OP.bitwise_and)
     V("cP", "cp", ["IP"], ["cP"], 1, out=col(cP), in_=T.IP[:])
@@ -186,14 +186,15 @@ def build(g, T, topo, rank, core):
     scol(cZ1, "cZ1", col(cG16), ["cG16"], 16.0)
     mat("Z", "IM", col(cZ), "cZ", n=144)
     mat("Z1", "IM", col(cZ1), "cZ1", n=144)
-    less("ZD", "Z", "Z1", 144)
+    MM("zd", [(T.pb0[:, 0:144], T.mI[:], T.Z[:], True, False, 144, False), (T.pb0[:, 0:144], T.mNI[:], T.Z1[:], False, True, 144, False)], ["mI", "mNI", "Z", "Z1"], ["ring0"], 0)
+    A("ZD", ["ring0"], ["ZD"], 144, [0], out=T.ZD[:], in_=T.pb0[:, 0:144], func=AF.Copy)
     scaled("ZU", "Z", U, 144)
     ns = CFG["ns"]
     if max(ns):
         scaled("ZH", "Z", 0.5, 144)
         scaled("ZDH", "ZD", 0.5, 144)
-    for h in range(NH):
-        scol(c80 + h, "c8%d" % h, col(cK), ["cK"], float(16 - ns[h]), 8.0, OP.is_equal, OP.mult)
+        for h in range(NH):
+            scol(c80 + h, "c8%d" % h, col(cK), ["cK"], float(16 - ns[h]), 8.0, OP.is_equal, OP.mult)
     for r in range(16 - max(ns), 16):
         fill("thr%d" % r, T.THC[:, r:r + 1], -0.6 * 2.0 ** (WT - 11 * r))
 
@@ -203,37 +204,48 @@ def build(g, T, topo, rank, core):
         return sel(T.ZD if r < 15 else T.Z, r)
     mat("mB", "IMG", col(cG16), "cG16")
     fill("ONES", T.ONES[:], 1.0, 128)
-    fill("BIG", T.BIG[:], 32768.0, 128)
+    if not min(CFG["xbS"]):
+        fill("BIG", T.BIG[:], 32768.0, 128)
     A("cb2", ["cK", "cE"], ["cb2"], 1300, out=T.COLB[:, 0:1], in_=col(cK), func=AF.Exp, bias=col(cE), scale=-LN2)
     A("cbw", ["cK", "cW", "cb2"], ["cbw"], 1, out=T.COLB[:, 1:2], in_=col(cK), func=AF.Exp, bias=col(cW), scale=-11.0 * LN2)
 
+    def wloc(t, h):
+        return (sl(T.WB, h), "w%d" % h) if CFG["dmwS"][h] else (m0(T.M0, t, h, 1), "w%d_%d" % (t, h))
+
+    def rloc(t, h):
+        return (m0(T.M0, t, h, 1), "R%d_%d" % (t, h)) if CFG["dmwS"][h] else (sl(T.R, h), "R%d" % h)
+
     def orders(h, t, src, rd, banks=()):
-        A("w", rd + ["cW", "cb2"], ["w%d_%d" % (t, h)], HS, banks, out=m0(T["M0_%d" % t], h, 1), in_=src, func=AF.Exp, bias=col(cW), scale=-11.0 * LN2)
+        A("w", rd + ["cW", "cb2"], [wloc(t, h)[1]], HS, banks, out=wloc(t, h)[0], in_=src, func=AF.Exp, bias=col(cW), scale=-11.0 * LN2)
         A("IW", rd + ["cb2"], ["IW%d" % h], HS, banks, out=sl(T.IW, h), in_=src, func=AF.Exp, scale=LN2)
 
     mat("mWB", "mB", T.COLB[:, 0:1], "cb2", OP.mult)
     ts("TMP", T.TMP[:], T.mB[:], ["mB", "cbw"], 128, 0.5, T.COLB[:, 1:2], -0.6, OP.mult, OP.mult)
-    ts("MK0", T.MK0[:], T.IMK[:], ["IMK"], 128, 0.5, 0.5, op0=OP.is_gt)
-    V("mCW", "tt", ["TMP", "MK0"], ["mCW"], 128, 2.0, out=T.mCW[:], in0=T.TMP[:], in1=T.MK0[:], op=OP.mult)
+    pick("mCW", T.mCW[:], T.TMP[:], "TMP", [[0, 8], [1, 16]], OP.not_equal, 0.0, 0, 0)
     scol(cKC, "cKC", col(cK), ["cK"], 0.0, -(2.0 ** -90), OP.is_equal, OP.add)
-    for key, skey, c in (("fI", "mI", 1.0), ("mN4k", "mI", -4096.0), ("mNB", "mB", -1.0), ("mNBU", "mB", -U), ("mI2", "mI", 2.0), ("mN16", "mI", -16.0)):
+    for key, skey, c in (("fI", "mI", 1.0), ("mN4k", "mI", -4096.0), ("mNB", "mB", -1.0), ("mNBU", "mB", -U), ("mN16", "mI", -16.0)):
         scaled(key, skey, c)
     if max(CFG["es"]):
         scaled("mU", "mI", U)
-    less("mTB", "mI2", "mB")
-    less("mIB", "mI", "mB")
-    scaled("mBI", "mIB", -1.0)
-    ts("B4I", T.B4I[:], T.IP[:], ["IP"], 1, 1.0, 4, 1, OP.arith_shift_right, OP.bitwise_and)
-    V("cS1", "cp", ["B4I"], ["cS1"], 1, out=col(cS1), in_=T.B4I[:])
-    scol(cS0, "cS0", col(cS1), ["cS1"], -1.0, 1.0, OP.mult, OP.add)
-    scol(cPp, "cPp", col(cP), ["cP"], 16.0)
-    scol(cPm, "cPm", col(cP), ["cP"], -16.0)
+    if max(CFG["mbS"] + CFG["maS"]):
+        scaled("m16", "mI", 16.0)
+        scaled("mHI", "mI", 0.5)
+        fill("cN16", col(cN16), -16.0)
+        fill("cNH", col(cNH), -0.5)
+    if max(CFG["dmwS"]):
+        scaled("mN32", "mI", -32.0)
+        fill("cDW", col(cDW), -64.0 * LN2)
+    SUM("ib", 1, 0, [("mI", T.mI[:], "mI"), ("mNI", T.mB[:], "mB")])
+    SUM("tb", 1, 1, [("mI", T.mI[:], "mI"), ("mI", T.mI[:], "mI"), ("mNI", T.mB[:], "mB")])
+    for key, r, c in (("mIB", 0, 1.0), ("mBI", 0, -1.0), ("mTB", 1, 1.0)):
+        A(key, ["ps1%d" % r, "ring1"], [key], 128, [1], out=T[key][:], in_=ps(1, r), func=AF.Copy, scale=c)
     scol(cOF, "cOF", col(cK), ["cK"], 16.0, 1807.0, OP.mult, OP.add)
     scol(c16P, "c16P", col(cP), ["cP"], 16.0, op0=OP.mult)
-    for j, (c, ck, s, sk) in enumerate([(cP, "cP", cS0, "cS0"), (cPp, "cPp", cS0, "cS0"), (cPm, "cPm", cS1, "cS1"), (cP, "cP", cS1, "cS1")]):
-        ts("fP%d" % j, T.fP[:, j * 128:(j + 1) * 128], T.IM[:, 0:128], ["IM", ck, sk], 128, 1.0, col(c), col(s), OP.is_equal, OP.mult)
-    fill("SD", T.SD[:], 4096.0, 256)
-    fill("SD", T.SD[:, 0:128:16], -(2.0 ** 22), 16)
+    for j in range(4):
+        a, b = j // 2, j % 2
+        pick("fP%d" % j, T.fP[:, j * 128:(j + 1) * 128], T.ONES[:], "ONES", [[-32, 4], [1000, 2], [-1, 16]], OP.is_equal, 0.0, -16 * a - 1000 * b, 1)
+    iota(T.SD[:], "SD", [[0, 128]], 4096, 0, 128)
+    pick("SD", T.SD[:], T.SD[:], "SD", [[0, 8], [1, 16]], OP.not_equal, -(2.0 ** 22), 0, 0)
     scaled("CB", "CBI", U, 8)
     ts("mG8", T.mG8[:], T.IMG[0:8, :], ["IMG", "c16P"], 128, 0.5, T.COL[0:8, c16P:c16P + 1], op0=OP.is_equal)
     V("A8", "cp", ["FIN"], ["A8"], S, out=T.A8[:], in_=T.FIN[:])
@@ -248,10 +260,14 @@ def build(g, T, topo, rank, core):
     mat("mZ0", "mB", col(cK0), "cK0", OP.mult)
     for h in range(NH):
         at["h"] = h
-        orders(h, 0, sl(T.R, h), ["Rs%d" % h])
-        MM("z", [(ps(6 + h, 2), T.mG8[:], T.Q8[:, h * HS:(h + 1) * HS], True, True, HS, False)], ["mG8", "Q8"], ["Q2%d" % h], 6 + h)
-        A("th", ["Q2%d" % h, "cTH"], ["th0_%d" % h], HS, [6 + h], out=m0(T.M0_0, h, 2), in_=ps(6 + h, 2), func=AF.Relu, bias=col(cTH))
-        MM("r0", [(ps(4 + h, 3), T.mI[:], sl(T.R, h), True, True, HS, False)], ["mI", "Rs%d" % h], ["P3%d" % h], 4 + h)
+        P, Q = 4 + h, 6 + h
+        r, rk = rloc(0, h)
+        V("inR", "cp", ["RIN"], [rk], HS, out=r, in_=sl(T.RIN, h))
+        orders(h, 0, r, [rk])
+        SUM("z", Q, 2, [("mG8", sl(T.Q8, h), "Q8")])
+        A("th", ["ps%d2" % Q, "cTH"], ["th0_%d" % h], HS, [Q], out=m0(T.M0, 0, h, 2), in_=ps(Q, 2), func=AF.Relu, bias=col(cTH))
+        if not CFG["mbS"][h]:
+            SUM("r0", P, 3, [("mI", r, rk)])
 
     def send(t, m, dst, src_ap, dst_ap, rd, wr, more):
         rid, pid, _s = topo.addr(dst)
@@ -282,13 +298,17 @@ def build(g, T, topo, rank, core):
     for t in range(RO):
         hear = T.cores[(rank + DIST[t]) % N]
         spk = T.cores[(rank - DIST[t]) % N]
-        M0, L0 = T["M0_%d" % t], T["L0_%d" % t]
-        M1, L1 = T["M1_%d" % t], T["L1_%d" % t]
-        NS, LN = T["NS_%d" % t], T["LN_%d" % t]
-        FF, LF = T.FF[:, t * S:(t + 1) * S], T.LF[:, t * S:(t + 1) * S]
+        M1, L1, FF, LF = [b[:, t * S:(t + 1) * S] for b in (T.M1, T.L1, T.FF, T.LF)]
+        NS, LN = T.NS[:, t * 16:(t + 1) * 16], T.LN[:, t * 16:(t + 1) * 16]
         last = t == RO - 1
         at["t"] = t
-        l0k = "L0_%d" % t
+        wth = [k for h in range(NH) for k in ((rloc if CFG["dmwS"][h] else wloc)(t, h)[1], "th%d_%d" % (t, h))]
+        l0k = l4k = "L0_%d" % t
+        early = t == 0 and CFG["early"]
+        if early:
+            l4k = "L4"
+            at["h"] = 0
+            send(t, "4", hear, T.M0[:, S:3 * S], T.L0[:, S:3 * S], wth, [l4k], 300)
         for h in range(NH):
             hs = str(h)
             th = "%d_%d" % (t, h)
@@ -308,10 +328,11 @@ def build(g, T, topo, rank, core):
 
                 def dw(k, h=h, q=q, qs=qs):
                     return T.DW[:, h * 2048 + k * 128 + q * qs:h * 2048 + k * 128 + (q + 1) * qs]
-                wq = M0[:, (3 * h + 1) * HS + q * qs:(3 * h + 1) * HS + (q + 1) * qs]
+                wq = wloc(t, h)[0][:, q * qs:(q + 1) * qs]
                 sk = T["pb%d" % P][:, q * qs:(q + 1) * qs]
-                for c in range(4):
-                    ks = range(1 + 4 * c, min(16, 5 + 4 * c))
+                nk = CFG["nk"][h]
+                for c in range(16 // nk):
+                    ks = range(1 + nk * c, min(16, 1 + nk + nk * c))
                     b = ring[0] % 4
                     ring[0] += 1
                     lst = []
@@ -322,39 +343,47 @@ def build(g, T, topo, rank, core):
                     nm = str(4 * q + c)
                     MM("dx" + nm, lst, qk + ["mI", "mNI"], ["ring%d" % b], b)
                     for j, k in enumerate(ks):
-                        V("DW" + nm, "tt", ["ring%d" % b, "w" + th], ["DW%d%d_%d" % (h, q, k)], qs, 1.0, [b],
+                        V("DW" + nm, "tt", ["ring%d" % b, wloc(t, h)[1]], ["DW%d%d_%d" % (h, q, k)], qs, 1.0, [b],
                           out=dw(k), in0=T["pb%d" % b][:, j * qs:(j + 1) * qs], in1=wq, op=OP.mult)
                     join(len(ks))
                     MM("sk" + nm, [(sk, sel(T.Z, k), dw(k), k == 1, k == 15, qs, False) for k in ks],
-                       ["Z"] + ["DW%d%d_%d" % (h, q, k) for k in ks], ["P0" + hs], P)
-            MM("xb", [(ps(Q, 3), T.mI[:], T.BIG[:], True, False, HS, False), (ps(Q, 3), T.mI[:], x0, False, True, HS, False)], xgk + ["mI", "BIG"], ["Q3" + hs], Q)
-            A("x0", xgk, ["x0" + th], HS, out=m0(M0, h, 0), in_=x0, func=AF.Copy)
-            A("ABS", ["P0" + hs], ["ABS" + hs], HS, [P], out=sl(T.AB1, h), in_=ps(P, 0), func=AF.Abs)
+                       ["Z"] + ["DW%d%d_%d" % (h, q, k) for k in ks], ["ps%d0" % P], P)
+            if CFG["xbS"][h]:
+                A("xb", xgk, ["ps%d3" % Q], HS, [Q], out=ps(Q, 3), in_=x0, func=AF.Identity, bias=32768.0)
+            else:
+                SUM("xb", Q, 3, [("mI", T.BIG[:], "BIG"), ("mI", x0, xgk)])
+            if CFG["x0G"][h]:
+                add("G", "x0", lambda o=m0(T.M0, t, h, 0), i=x0: g.affine_select(o, i, [[0, HS]], OP.is_ge, 0.0, 0, 0), xgk, ["x0" + th], HS + 20)
+            else:
+                A("x0", xgk, ["x0" + th], HS, out=m0(T.M0, t, h, 0), in_=x0, func=AF.Copy)
+            ab, bit = sl(T.AB1, h), sl(T.BIT, h)
+            A("ABS", ["ps%d0" % P], ["ABS" + hs], HS, [P], out=ab, in_=ps(P, 0), func=AF.Abs)
 
             def G(r, h=h):
                 return T.G[:, h * 2048 + r * 128:h * 2048 + (r + 1) * 128]
             for r in range(16):
                 if r >= 16 - ns[h]:
-                    A("GS%d" % (r // 4), ["ABS" + hs, "thr%d" % r], ["G%d_%d" % (h, r)], HS, out=G(r), in_=sl(T.AB1, h), func=AF.Sign, bias=T.THC[:, r:r + 1])
+                    A("GS%d" % (r // 4), ["ABS" + hs, "thr%d" % r], ["G%d_%d" % (h, r)], HS, out=G(r), in_=ab, func=AF.Sign, bias=T.THC[:, r:r + 1])
                 else:
-                    V("G%d" % (r // 4), "ts", ["ABS" + hs], ["G%d_%d" % (h, r)], HS, 0.5, out=G(r), in0=sl(T.AB1, h), scalar1=0.6 * 2.0 ** (WT - 11 * r), scalar2=None, op0=OP.is_ge)
+                    V("G%d" % (r // 4), "ts", ["ABS" + hs], ["G%d_%d" % (h, r)], HS, 0.5, out=G(r), in0=ab, scalar1=0.6 * 2.0 ** (WT - 11 * r), scalar2=None, op0=OP.is_ge)
                 if r % 4 == 3:
                     join(4)
                     MM("cnt%d" % (r // 4), [(ps(P, 1), cntm(q, h), G(q), q == 0, q == 15, HS, False) for q in range(r - 3, r + 1)],
-                       ["Z", "ZD", "ZH", "ZDH"] + ["G%d_%d" % (h, q) for q in range(r - 3, r + 1)], ["P1" + hs], P)
+                       ["Z", "ZD", "ZH", "ZDH"] + ["G%d_%d" % (h, q) for q in range(r - 3, r + 1)], ["ps%d1" % P], P)
+            c8 = col(c80 + h) if max(ns) else 0.0
             if CFG["bitV"][h]:
-                V("BIT", "ts", ["P1" + hs, "c8" + hs], ["BIT" + hs], HS, 1.0, [P], out=sl(T.BIT, h), in0=ps(P, 1), scalar1=col(c80 + h), scalar2=0.5, op0=OP.add, op1=OP.is_gt)
+                V("BIT", "ts", ["ps%d1" % P, "c8" + hs], ["BIT" + hs], HS, 1.0, [P], out=bit, in0=ps(P, 1), scalar1=c8, scalar2=0.5, op0=OP.add, op1=OP.is_gt)
             else:
-                A("BIT", ["P1" + hs, "c8" + hs], ["BIT" + hs], HS, [P], out=sl(T.BIT, h), in_=ps(P, 1), func=AF.Sign, bias=col(c80 + h))
-            MM("word", [(ps(P, 0), T.mWB[:], sl(T.BIT, h), True, True, HS, False)], ["mWB", "BIT" + hs], ["P0" + hs], P)
-            V("TI", "tt", ["P0" + hs, "IW" + hs], ["TI" + hs], HS, 1.0, [P], out=sl(T.TI, h), in0=ps(P, 0), in1=sl(T.IW, h), op=OP.mult)
+                A("BIT", ["ps%d1" % P, "c8" + hs], ["BIT" + hs], HS, [P], out=bit, in_=ps(P, 1), func=AF.Sign, bias=c8)
+            SUM("word", P, 0, [("mWB", bit, "BIT" + hs)])
+            V("TI", "tt", ["ps%d0" % P, "IW" + hs], ["TI" + hs], HS, 1.0, [P], out=sl(T.TI, h), in0=ps(P, 0), in1=sl(T.IW, h), op=OP.mult)
             V("TJ", "ts", ["TI" + hs], ["TJ" + hs], HS, 1.0, out=sl(T.TJ, h), in0=sl(T.TI, h), scalar1=32768, scalar2=None, op0=OP.bitwise_and)
-            V("x0p", "tt", ["TJ" + hs, "Q3" + hs], ["x0p" + th], HS, 1.0, [Q], out=sl(M1, h), in0=ps(Q, 3), in1=sl(T.TJ, h), op=OP.subtract)
+            V("x0p", "tt", ["TJ" + hs, "ps%d3" % Q], ["x0p" + th], HS, 1.0, [Q], out=sl(M1, h), in0=ps(Q, 3), in1=sl(T.TJ, h), op=OP.subtract)
             send(t, "1" + hs, hear, sl(M1, h), sl(L1, h), ["x0p" + th], ["L1" + th], 0)
-            MM("dB", [(ps(Q, 1), T.mI[:], sl(T.AB1, h), True, False, HS, False), (ps(Q, 1), T.mCW[:], sl(T.BIT, h), False, True, HS, False)],
-               ["ABS" + hs, "mI", "mCW", "BIT" + hs], ["Q1" + hs], Q)
-            A("SG", ["Q1" + hs, "cKC"], ["SG" + hs], HS, [Q], out=sl(T.SG, h), in_=ps(Q, 1), func=AF.Sign, bias=col(cKC))
-        send(t, "0", hear, M0[:], L0[:], [k + "%d_%d" % (t, h) for k in ("x0", "w", "th") for h in range(NH)], [l0k], 500)
+            SUM("dB", Q, 1, [("mI", ab, "ABS" + hs), ("mCW", bit, "BIT" + hs)])
+            A("SG", ["ps%d1" % Q, "cKC"], ["SG" + hs], HS, [Q], out=sl(T.SG, h), in_=ps(Q, 1), func=AF.Sign, bias=col(cKC))
+        piece = slice(3 * t * S, (3 * t + (1 if early else 3)) * S)
+        send(t, "0", hear, T.M0[:, piece], T.L0[:, piece], ["x0%d_%d" % (t, h) for h in range(NH)] + ([] if early else wth), [l0k], 0 if early else 500)
         for h in range(NH):
             at["h"] = h
             gather(h, T.H16, T.YG, "YG", "H16", CFG["vh"])
@@ -364,77 +393,79 @@ def build(g, T, topo, rank, core):
             at["h"] = h
             P, Q = 4 + h, 6 + h
             ygk = ["YG%d%d" % (h, j) for j in range(CFG["npc"])]
-            l1k = "L1" + th
-            es = CFG["es"][h]
+            l1, l1k = sl(L1, h), "L1" + th
+            es = CFG["esL" if last else "es"][h]
             if es < 4 or not last:
-                MM("xp", [(ps(P, 0), T.mI[:], sl(L1, h), True, True, HS, False)], ["mI", l1k], ["P0" + hs], P)
-            V("DSC", "ts", [l1k], ["DSC" + hs], HS, 0.5, out=sl(T.DSC, h), in0=sl(L1, h), scalar1=1000.0, scalar2=None, op0=OP.is_lt)
+                SUM("xp", P, 0, [("mI", l1, l1k)])
+            V("DSC", "ts", [l1k], ["DSC" + hs], HS, 0.5, out=sl(T.DSC, h), in0=l1, scalar1=1000.0, scalar2=None, op0=OP.is_lt)
             if not last:
-                V("UND", "ts", [l1k], ["UND" + hs], HS, 0.5, out=sl(T.UND, h), in0=sl(L1, h), scalar1=1000.0, scalar2=None, op0=OP.is_gt)
-                V("XD", "tt", ["P0" + hs, "DSC" + hs], ["XD" + hs], HS, 1.0, [P], out=sl(T.XD, h), in0=ps(P, 0), in1=sl(T.DSC, h), op=OP.mult)
-            if es:
-                acc, ak, z, zk = ps(Q, 1), "Q1" + hs, T.Z, "Z"
-                MM("nd", [(acc, T.mNB[:], sl(T.DSC, h), True, False, HS, False)], ["mNB", "DSC" + hs], [ak], Q)
-            else:
-                acc, ak, z, zk = ps(Q, 0), "Q0" + hs, T.ZU, "ZU"
-                MM("kh", [(acc, T.fI[:], sl(T.H, h), True, False, HS, True)], ["fI", "Hs" + hs], [ak], Q)
-                MM("nd", [(acc, T.mNBU[:], sl(T.DSC, h), False, False, HS, False)], ["mNBU", "DSC" + hs], [ak], Q)
+                V("UND", "ts", [l1k], ["UND" + hs], HS, 0.5, out=sl(T.UND, h), in0=l1, scalar1=1000.0, scalar2=None, op0=OP.is_gt)
+                V("XD", "tt", ["ps%d0" % P, "DSC" + hs], ["XD" + hs], HS, 1.0, [P], out=sl(T.XD, h), in0=ps(P, 0), in1=sl(T.DSC, h), op=OP.mult)
+            key, kk = ps(Q, 0), "ps%d0" % Q
+            SUM("kh", Q, 0, [("fI", sl(T.H, h), "Hs" + hs)], stop=False)
+            SUM("nd", Q, 0, [("mNBU", sl(T.DSC, h), "DSC" + hs)], start=False, stop=False)
+            vb = ring[0] % 4
+            ring[0] += 1 if es else 0
             for c in range(4):
-                ks = range(4 * c, 4 * c + 4)
-
-                def yg(k, h=h):
-                    return T.YG[:, h * 2048 + k:(h + 1) * 2048:16]
-
-                def ek(k, h=h, m=1):
-                    return T.E[:, h * 2048 + k * 128:h * 2048 + (k + m) * 128]
+                ks = range(c, 16, 4)
+                eks = ["E%d_%d" % (h, k) for k in ks]
+                ec = T.E[:, h * 2048 + c * 512:h * 2048 + (c + 1) * 512]
                 if c >= 4 - es:
+                    ring[0] += 1 if ring[0] % 4 == vb else 0
                     b = ring[0] % 4
                     ring[0] += 1
-                    lst = []
-                    for j, k in enumerate(ks):
-                        lst.append((ps(b, j), T.mI[:], yg(k), True, False, HS, False))
-                        lst.append((ps(b, j), T.mNI[:], sl(L1, h), False, True, HS, False))
-                    MM("dy%d" % c, lst, ygk + ["mI", "mNI", l1k], ["ring%d" % b], b)
-                    A("ES%d" % c, ["ring%d" % b], ["E%d_%d" % (h, k) for k in ks], 512, [b], out=ek(4 * c, m=4), in_=T["pb%d" % b][:, 0:512], func=AF.Relu, scale=512.0, bias=1.0)
+                    pb = T["pb%d" % b]
+                    MM("cy%d" % c, [(pb[:, 0:512], T.mI[:], T.YG[:, h * 2048 + c:(h + 1) * 2048:4], True, False, 512, False)], ygk + ["mI"], ["ring%d" % b], b)
+                    MM("dy%d" % c, [(pb[:, j:512:4], T.mNI[:], l1, False, j == 3, HS, False) for j in range(4)], ["mNI", l1k], ["ring%d" % b], b)
+                    A("ES%d" % c, ["ring%d" % b], eks, 512, [b], out=ec, in_=pb[:, 0:512], func=AF.Relu, scale=512.0, bias=1.0)
+                    MM("key%d" % c, [(ps(vb, 0), sel(T.Z, k), ec[:, j:512:4], k == 4 - es, k == 15, HS, False) for j, k in enumerate(ks)], ["Z"] + eks, ["ring%d" % vb], vb)
                 else:
-                    for k in ks:
-                        V("E%d" % c, "tt", ygk + ["P0" + hs], ["E%d_%d" % (h, k)], HS, 1.0, [P], out=ek(k), in0=yg(k), in1=ps(P, 0), op=OP.is_equal)
+                    for j, k in enumerate(ks):
+                        V("E%d" % c, "tt", ygk + ["ps%d0" % P], ["E%d_%d" % (h, k)], HS, 1.0, [P], out=sl(ec, j), in0=T.YG[:, h * 2048 + k:(h + 1) * 2048:16], in1=ps(P, 0), op=OP.is_equal)
                     join(4)
-                MM("key%d" % c, [(acc, sel(z, k), ek(k), False, k == 15, HS, False) for k in ks], [zk] + ["E%d_%d" % (h, k) for k in ks], [ak], Q)
+                    MM("key%d" % c, [(key, sel(T.ZU, k), sl(ec, j), False, k == 15, HS, False) for j, k in enumerate(ks)], ["ZU"] + eks, [kk], Q)
             if es:
-                V("RND", "ts", [ak], ["RND" + hs], HS, 1.0, [Q], out=sl(T.RND, h), in0=acc, scalar1=1.5 * 2.0 ** 32, scalar2=-1.5 * 2.0 ** 32, op0=OP.add, op1=OP.add)
-                V("MS", "tt", [ak, "RND" + hs], ["MS" + hs], HS, 1.0, [Q], out=sl(T.MS, h), in0=acc, in1=sl(T.RND, h), op=OP.subtract)
-                MM("kh", [(ps(Q, 0), T.fI[:], sl(T.H, h), True, False, HS, True)], ["fI", "Hs" + hs], ["Q0" + hs], Q)
-                MM("km", [(ps(Q, 0), T.mU[:], sl(T.MS, h), False, True, HS, False)], ["mU", "MS" + hs], ["Q0" + hs], Q)
-            V("KT", "tr", ["Q0" + hs], ["KT" + hs], HS, 1.0, [Q], out=sl(T.KT, h), in_=ps(Q, 0))
-            A("KH", ["Q0" + hs], ["KH" + hs], HS, [Q], out=sl(T.KH, h), in_=ps(Q, 0), func=AF.Relu, scale=-1.0)
+                V("RND", "ts", ["ring%d" % vb], ["RND" + hs], HS, 1.0, [vb], out=sl(T.RND, h), in0=ps(vb, 0), scalar1=1.5 * 2.0 ** 32, scalar2=-1.5 * 2.0 ** 32, op0=OP.add, op1=OP.add)
+                V("MS", "tt", ["ring%d" % vb, "RND" + hs], ["MS" + hs], HS, 1.0, [vb], out=sl(T.MS, h), in0=ps(vb, 0), in1=sl(T.RND, h), op=OP.subtract)
+                SUM("km", Q, 0, [("mU", sl(T.MS, h), "MS" + hs)], start=False)
+            V("KT", "tr", [kk], ["KT" + hs], HS, 1.0, [Q], out=sl(T.KT, h), in_=key)
+            A("KH", [kk], ["KH" + hs], HS, [Q], out=sl(T.KH, h), in_=key, func=AF.Relu, scale=-1.0)
             V("SC", "scan", ["KT" + hs, "SD"], ["SC" + hs], HS, 1.0, out=sl(T.SC, h), data0=T.SD[:], data1=sl(T.KT, h), initial=0.0, op0=OP.add, op1=OP.max)
             lst = []
             for hh in range(2):
                 for g2 in range(2):
                     lst.append((T["pb%d" % Q][:, 128 + hh:136:2], T.fP[:, (2 * hh + g2) * 128:(2 * hh + g2 + 1) * 128],
                                 T.SC[:, h * HS + g2 * 16 + 15:(h + 1) * HS:32], g2 == 0, g2 == 1, 4, True))
-            MM("mk", lst, ["fP%d" % j for j in range(4)] + ["SC" + hs], ["Q1" + hs], Q)
+            MM("mk", lst, ["fP%d" % j for j in range(4)] + ["SC" + hs], ["ps%d1" % Q], Q)
             ws = slice(8 * h, 8 * h + 8)
-            V("K32", "tt", ["Q1" + hs, "CB"], ["K32" + hs], 8, 1.0, [Q], out=T.K32[:, ws], in0=T["pb%d" % Q][:, 128:136], in1=T.CB[:], op=OP.add)
+            V("K32", "tt", ["ps%d1" % Q, "CB"], ["K32" + hs], 8, 1.0, [Q], out=T.K32[:, ws], in0=T["pb%d" % Q][:, 128:136], in1=T.CB[:], op=OP.add)
             V("N32", "ts", ["K32" + hs], ["N32" + hs], 8, out=T.N32[:, ws], in0=T.K32[:, ws], scalar1=4095, scalar2=None, op0=OP.bitwise_and)
             V("NS", "cp", ["N32" + hs], ["NS" + th], 8, out=NS[:, ws], in_=T.N32[:, ws])
             send(t, "2" + hs, spk, NS[:, ws], LN[:, ws], ["NS" + th], ["LN" + th], -100)
-            MM("q", [(ps(Q, 3), T.fI[:], sl(T.C, h), True, False, HS, True), (ps(Q, 3), T.mN4k[:], T.ONES[:], False, False, HS, False),
-                     (ps(Q, 3), T.mN4k[:], sl(T.SG, h), False, True, HS, False)], ["fI", "mN4k", "ONES", "Cs" + hs, "SG" + hs], ["Q3" + hs], Q)
+            SUM("q", Q, 3, [("fI", sl(T.C, h), "Cs" + hs), ("mN4k", T.ONES[:], "ONES"), ("mN4k", sl(T.SG, h), "SG" + hs)])
             V("KK", "ts", ["K32" + hs], ["KK" + hs], 8, out=T.KK[:, ws], in0=T.K32[:, ws], scalar1=12, scalar2=0xF0F, op0=OP.arith_shift_right, op1=OP.bitwise_and)
             V("OF", "ts", ["KK" + hs, "cOF"], ["OF16" + hs], 8, out=T.OF16[:, ws], in0=T.KK[:, ws], scalar1=-1.0, scalar2=col(cOF), op0=OP.mult, op1=OP.add)
             ysrc = T.YG[:, h * 2048:(h + 1) * 2048].indirect(T.OF16[:, ws])
+            if CFG["yS"][h] and not last:
+                A("YS", ygk + ["OF16" + hs], ["YS" + hs], HS, (), "g", out=sl(T.YS, h), in_=ysrc, func=AF.Copy)
+                SUM("ys", Q, 1, [("mI", sl(T.YS, h), "YS" + hs)])
+                ysrc, yk, yr, yb = ps(Q, 1), ["ps%d1" % Q], 1.0, [Q]
+            else:
+                yk, yr, yb = ygk + ["OF16" + hs], "g", []
+            dm, dmk = sl(T.DM, h), "DM" + hs
+            V("DM", "tt", yk + [l0k], [dmk], HS, yr, yb, out=dm, in0=ysrc, in1=m0(T.L0, t, h, 0), op=OP.not_equal)
             if not last:
-                V("YU", "tt", ygk + ["OF16" + hs, "UND" + hs], ["YU" + hs], HS, "g", out=sl(T.YU, h), in0=ysrc, in1=sl(T.UND, h), op=OP.mult)
-            V("DM", "tt", ygk + ["OF16" + hs, l0k], ["DM" + hs], HS, "g", out=sl(T.DM, h), in0=ysrc, in1=m0(L0, h, 0), op=OP.not_equal)
-            MM("wc", [(ps(P, 1), T.mI[:], m0(L0, h, 1), True, True, HS, False)], ["mI", l0k], ["P1" + hs], P)
-            V("DMW", "tt", ["P1" + hs, "DM" + hs], ["DMW" + hs], HS, 1.0, [P], out=sl(T.DMW, h), in0=ps(P, 1), in1=sl(T.DM, h), op=OP.mult)
-            MM("u", [(ps(Q, 2), T.mTH[:], m0(L0, h, 2), True, False, HS, False), (ps(Q, 2), T.mNB[:], sl(T.DM, h), False, True, HS, False)],
-               ["mNB", "mTH", "DM" + hs, l0k], ["Q2" + hs], Q)
-            A("TH", ["Q2" + hs, "cT"], ["TH" + hs], HS, [Q], out=sl(T.TH, h), in_=ps(Q, 2), func=AF.Relu, scale=2.0 ** 96, bias=col(cT))
-            MM("tt", [(ps(P, 2), T.mTB[:], sl(T.DMW, h), True, True, HS, False)], ["mTB", "DMW" + hs], ["P2" + hs], P)
-            V("FF", "tt", ["P2" + hs, "TH" + hs], ["FF" + th], HS, 1.0, [P], out=sl(FF, h), in0=ps(P, 2), in1=sl(T.TH, h), op=OP.is_gt)
+                V("YU", "tt", yk + ["UND" + hs], ["YU" + hs], HS, yr, yb, out=sl(T.YU, h), in0=ysrc, in1=sl(T.UND, h), op=OP.mult)
+            if CFG["dmwS"][h]:
+                SUM("wc", P, 1, [("mI", m0(T.L0, t, h, 1), l4k), ("mN32", dm, dmk)])
+                A("DMW", ["ps%d1" % P, "cDW"], ["DMW" + hs], HS, [P], out=sl(T.DMW, h), in_=ps(P, 1), func=AF.Exp, scale=-2.0 * LN2, bias=col(cDW))
+            else:
+                SUM("wc", P, 1, [("mI", m0(T.L0, t, h, 1), l4k)])
+                V("DMW", "tt", ["ps%d1" % P, dmk], ["DMW" + hs], HS, 1.0, [P], out=sl(T.DMW, h), in0=ps(P, 1), in1=dm, op=OP.mult)
+            SUM("u", Q, 2, [("mTH", m0(T.L0, t, h, 2), l4k), ("mNB", dm, dmk)])
+            A("TH", ["ps%d2" % Q, "cT"], ["TH" + hs], HS, [Q], out=sl(T.TH, h), in_=ps(Q, 2), func=AF.Relu, scale=2.0 ** 96, bias=col(cT))
+            SUM("tt", P, 2, [("mTB", sl(T.DMW, h), "DMW" + hs)])
+            V("FF", "tt", ["ps%d2" % P, "TH" + hs], ["FF" + th], HS, 1.0, [P], out=sl(FF, h), in0=ps(P, 2), in1=sl(T.TH, h), op=OP.is_gt)
             send(t, "3" + hs, spk, sl(FF, h), sl(LF, h), ["FF" + th], ["LF" + th], 0)
         if not last:
             for h in range(NH):
@@ -449,39 +480,54 @@ def build(g, T, topo, rank, core):
             P, Q = 4 + h, 6 + h
             ws = slice(8 * h, 8 * h + 8)
             V("CM", "tt", ["ASI", "LN" + th, "SG" + hs], ["CM" + hs], HS, "g", out=sl(T.CM, h), in0=T.ASI[:].indirect(LN[:, ws]), in1=sl(T.SG, h), op=OP.mult)
-            V("Cs", "tt", ["CM" + hs, "Q3" + hs], ["Cs" + hs], HS, 1.0, [Q], out=sl(T.C, h), in0=ps(Q, 3), in1=sl(T.CM, h), op=OP.max)
+            V("Cs", "tt", ["CM" + hs, "ps%d3" % Q], ["Cs" + hs], HS, 1.0, [Q], out=sl(T.C, h), in0=ps(Q, 3), in1=sl(T.CM, h), op=OP.max)
             if not last:
                 V("C16", "cp", ["Cs" + hs], ["C16" + hs], HS, 1.0, out=sl(T.C16, h), in_=sl(T.C, h))
             V("HM", "tt", ["ASI", "NS" + th, "KH" + hs], ["HM" + hs], HS, "g", out=sl(T.HM, h), in0=T.ASI[:].indirect(NS[:, ws]), in1=sl(T.KH, h), op=OP.min)
-            V("Hs", "tt", ["HM" + hs, "Q0" + hs], ["Hs" + hs], HS, 1.0, [Q], out=sl(T.H, h), in0=ps(Q, 0), in1=sl(T.HM, h), op=OP.max)
+            V("Hs", "tt", ["HM" + hs, "ps%d0" % Q], ["Hs" + hs], HS, 1.0, [Q], out=sl(T.H, h), in0=ps(Q, 0), in1=sl(T.HM, h), op=OP.max)
             if not last:
                 V("H16", "cp", ["Hs" + hs], ["H16" + hs], HS, 1.0, out=sl(T.H16, h), in_=sl(T.H, h))
-            ff, lf, fk, lk = sl(FF, h), sl(LF, h), "FF" + th, "LF" + th
-            r, rm, ma, la, mb, lb = [sl(b, h) for b in (T.R, T.RM, T.MA, T.LA, T.MB, T.LB)]
-            V("MB", "tt", ["P3" + hs, fk], ["MB" + hs], HS, 1.0, [P], out=mb, in0=ps(P, 3), in1=ff, op=OP.mult)
-            MM("b", [(ps(Q, 1), T.mB[:], mb, True, True, HS, False)], ["mB", "MB" + hs], ["Q1" + hs], Q)
-            V("LB", "tt", ["Rs" + hs, "Q1" + hs], ["LB" + hs], HS, 1.0, [Q], out=lb, in0=ps(Q, 1), in1=r, op=OP.is_gt)
-            MM("rm", [(ps(P, 1), T.mI[:], r, True, False, HS, False), (ps(P, 1), T.mNI[:], mb, False, False, HS, False), (ps(P, 1), T.mIB[:], ff, False, False, HS, False),
-                      (ps(P, 1), T.mI[:], lb, False, True, HS, False)], ["mI", "mNI", "mIB", "Rs" + hs, "MB" + hs, "LB" + hs, fk], ["P1" + hs], P)
-            A("RM", ["P1" + hs], ["RM" + hs], HS, [P], out=rm, in_=ps(P, 1), func=AF.Copy)
-            V("MA", "tt", ["P1" + hs, lk], ["MA" + hs], HS, 1.0, [P], out=ma, in0=ps(P, 1), in1=lf, op=OP.mult)
-            MM("a", [(ps(Q, 1), T.mN16[:], ff, True, False, HS, False), (ps(Q, 1), T.mB[:], ma, False, True, HS, False)], ["mB", "mN16", "MA" + hs, fk], ["Q1" + hs], Q)
-            MM("r1", [(ps(P, 3), T.mI[:], rm, True, False, HS, False), (ps(P, 3), T.mBI[:], ff, False, False, HS, False), (ps(P, 3), T.mNI[:], ma, False, False, HS, False)],
-               ["mI", "mNI", "mBI", "RM" + hs, "MA" + hs, fk], ["P3" + hs], P)
-            V("LA", "tt", ["RM" + hs, "Q1" + hs], ["LA" + hs], HS, 1.0, [Q], out=la, in0=ps(Q, 1), in1=rm, op=OP.is_gt)
-            MM("r2", [(ps(P, 3), T.mI[:], la, False, True, HS, False)], ["mI", "LA" + hs], ["P3" + hs], P)
-            if not last:
-                orders(h, t + 1, ps(P, 3), ["P3" + hs], [P])
-                A("Rs", ["P3" + hs], ["Rs" + hs], HS, [P], out=r, in_=ps(P, 3), func=AF.Copy)
-                MM("z", [(ps(Q, 2), T.mZ0[:], m0(M0, h, 2), True, False, HS, False), (ps(Q, 2), T.mB[:], lf, False, True, HS, False)], ["mZ0", "mB", "th" + th, lk], ["Q2" + hs], Q)
-                A("th", ["Q2" + hs, "cTH"], ["th%d_%d" % (t + 1, h)], HS, [Q], out=m0(T["M0_%d" % (t + 1)], h, 2), in_=ps(Q, 2), func=AF.Relu, bias=col(cTH))
+            ff, lf, r = (sl(FF, h), "FF" + th), (sl(LF, h), "LF" + th), rloc(t, h)
+            rm, ma, la, mb, lb = [(sl(T[b], h), b + hs) for b in ("RM", "MA", "LA", "MB", "LB")]
+            q1, qk, one = ps(Q, 1), "ps%d1" % Q, ("mHI", T.ONES[:], "ONES")
+            if CFG["mbS"][h]:
+                SUM("mb", Q, 1, [("mI",) + r, ("m16",) + ff])
+                A("MB", [qk, "cN16"], [mb[1]], HS, [Q], out=mb[0], in_=q1, func=AF.Relu, bias=col(cN16))
+                SUM("b", Q, 1, [("mNI",) + r, ("mB",) + mb])
+                A("LB", [qk, "cNH"], [lb[1]], HS, [Q], out=lb[0], in_=q1, func=AF.Sign, bias=col(cNH))
+                SUM("rm", P, 1, [one, ("mI",) + r, ("mNI",) + mb, ("mIB",) + ff, ("mHI",) + lb])
             else:
-                A("Rs", ["P3" + hs], ["OR" + hs], HS, [P], out=sl(T.OR, h), in_=ps(P, 3), func=AF.Copy)
+                V("MB", "tt", ["ps%d3" % P, ff[1]], [mb[1]], HS, 1.0, [P], out=mb[0], in0=ps(P, 3), in1=ff[0], op=OP.mult)
+                SUM("b", Q, 1, [("mB",) + mb])
+                V("LB", "tt", [r[1], qk], [lb[1]], HS, 1.0, [Q], out=lb[0], in0=q1, in1=r[0], op=OP.is_gt)
+                SUM("rm", P, 1, [("mI",) + r, ("mNI",) + mb, ("mIB",) + ff, ("mI",) + lb])
+            A("RM", ["ps%d1" % P], [rm[1]], HS, [P], out=rm[0], in_=ps(P, 1), func=AF.Copy)
+            if CFG["maS"][h] and not last:
+                SUM("ma", Q, 1, [("mI",) + rm, ("m16",) + lf])
+                A("MA", [qk, "cN16"], [ma[1]], HS, [Q], out=ma[0], in_=q1, func=AF.Relu, bias=col(cN16))
+                SUM("a", Q, 1, [("mN16",) + ff, ("mNI",) + rm, ("mB",) + ma])
+                SUM("r1", P, 3, [one, ("mI",) + rm, ("mBI",) + ff, ("mNI",) + ma], stop=False)
+                A("LA", [qk, "cNH"], [la[1]], HS, [Q], out=la[0], in_=q1, func=AF.Sign, bias=col(cNH))
+                SUM("r2", P, 3, [("mHI",) + la], start=False)
+            else:
+                V("MA", "tt", ["ps%d1" % P, lf[1]], [ma[1]], HS, 1.0, [P], out=ma[0], in0=ps(P, 1), in1=lf[0], op=OP.mult)
+                SUM("a", Q, 1, [("mN16",) + ff, ("mB",) + ma])
+                SUM("r1", P, 3, [("mI",) + rm, ("mBI",) + ff, ("mNI",) + ma], stop=last)
+                V("LA", "tt", [rm[1], qk], [la[1]], HS, 1.0, [Q], out=la[0], in0=q1, in1=rm[0], op=OP.is_gt)
+                if not last:
+                    SUM("r2", P, 3, [("mI",) + la], start=False)
+            if not last:
+                orders(h, t + 1, ps(P, 3), ["ps%d3" % P], [P])
+                A("Rs", ["ps%d3" % P], [rloc(t + 1, h)[1]], HS, [P], out=rloc(t + 1, h)[0], in_=ps(P, 3), func=AF.Copy)
+                SUM("z", Q, 2, [("mZ0", m0(T.M0, t, h, 2), "th" + th), ("mB",) + lf])
+                A("th", ["ps%d2" % Q, "cTH"], ["th%d_%d" % (t + 1, h)], HS, [Q], out=m0(T.M0, t + 1, h, 2), in_=ps(Q, 2), func=AF.Relu, bias=col(cTH))
+            else:
+                V("OR", "tt", ["ps%d3" % P, la[1]], ["OR" + hs], HS, 1.0, [P], out=sl(T.OR, h), in0=ps(P, 3), in1=la[0], op=OP.add)
                 oa = T["pb%d" % Q][0:8, 256:384]
                 MM("z", [(oa, T.mI[0:8, 0:8], T.A8[:, h * HS:(h + 1) * HS], True, False, HS, False)] +
                    [(oa, T.mB[:, 0:128:16], sl(T.LF, NH * u + h), False, u == t, HS, False) for u in range(RO)],
-                   ["mI", "mB", "A8"] + ["LF%d_%d" % (u, h) for u in range(RO)], ["Q2" + hs], Q)
-                A("th", ["Q2" + hs], ["OA" + hs], HS, [Q], out=sl(T.OA, h), in_=oa, func=AF.Copy)
+                   ["mI", "mB", "A8"] + ["LF%d_%d" % (u, h) for u in range(RO)], ["ps%d2" % Q], Q)
+                A("th", ["ps%d2" % Q], ["OA" + hs], HS, [Q], out=sl(T.OA, h), in_=oa, func=AF.Copy)
 
     def store(i, q, dst, src, rd):
         e = g.sync if q == "Y" else g.scalar
@@ -490,30 +536,8 @@ def build(g, T, topo, rank, core):
         store(h, "Y", sl(T.yctx, h), sl(T.C, h), ["Cs%d" % h])
         store(2 + h, "Y", sl(T.ycand, h), sl(T.H, h), ["Hs%d" % h])
         store(4 + h, "Y", sl(T.ypref, h), sl(T.OR, h), ["OR%d" % h])
-        store(6 + h, "Y", sl(T.yfail, h), sl(T.OA, h), ["OA%d" % h])
+        store(6 + h, "S", sl(T.yfail, h), sl(T.OA, h), ["OA%d" % h])
     return ops
-
-
-def price(o, m):
-    q, c = o["q"], o["cost"]
-    if c == "dma":
-        return 60.0, 60.0 + o["lat"] * m["dma"]
-    if q == "N":
-        return 0.0, m["hop"] + o["lat"]
-    if q == "G":
-        d = m["issue"] if c == "issue" else 130.0 + 2 * c * m["cy"]
-    elif q == "T":
-        d = c * m["pe"] + m["ovT"]
-    else:
-        n, rate = c
-        if rate in ("g", "sc"):
-            d = n * m[rate] * m["cy"] + (50.0 if q == "V" else max(65.0, m["ovS"]))
-        elif q == "V":
-            d = max(64, n * rate) * m["cy"] + m["ovV"]
-        else:
-            d = n * m["cy"] + m["ovS"]
-        d *= 1 + len(o.get("more", ()))
-    return d, d
 
 
 def depend(ops):
@@ -537,73 +561,18 @@ def depend(ops):
     return deps
 
 
-def gap(a, b, m):
-    if b == "N":
-        return 0.0
-    if a != b:
-        return m["wake"]
-    return 0.0 if a in "TG" else m["self"]
+def named(o):
+    return o["name"] + ("_" if o["t"] < 0 else str(o["t"]) if o["t"] in CFG["own"] else "")
 
 
-def sequence(ops, deps, off, m):
-    n = len(ops)
-    key = [None] * n
-    for i in range(n - 1, -1, -1):
-        o = ops[i]
-        if o["name"] in off:
-            key[i] = o["t"] * PERIOD + off[o["name"]]
-        elif key[i] is None:
-            key[i] = RO * PERIOD * 2
-        for j in deps[i]:
-            if ops[j]["name"] not in off:
-                k = key[i] - price(ops[j], m)[1]
-                key[j] = k if key[j] is None else min(key[j], k)
-    for i in range(n):
-        for j in deps[i]:
-            key[i] = max(key[i], key[j])
-    return sorted(range(n), key=lambda i: (key[i], i))
+def sequence(ops, deps):
+    key = []
+    for i, o in enumerate(ops):
+        key.append(max([o["t"] * PERIOD + OFF.get(named(o), -1e9)] + [key[j] for j in deps[i]]))
+    return sorted(range(len(ops)), key=lambda i: (key[i], i))
 
 
-def place(ops, deps, seq, m):
-    busy = {q: [] for q in "VSTGY"}
-    bank = {b: [] for b in range(8)}
-    n = len(ops)
-    beg, fin = [0.0] * n, [0.0] * n
-    wake = m["wake"]
-    for i in seq:
-        o = ops[i]
-        q = o["q"]
-        d, e = price(o, m)
-        st = 0.0
-        for j in deps[i]:
-            st = max(st, fin[j] + gap(ops[j]["q"], q, m))
-        if q != "N":
-            moved = True
-            while moved:
-                moved = False
-                for lst, pad in [(busy[q], 0.0)] + [(bank[b], wake) for b in o["bk"]]:
-                    k = len(lst) - 1
-                    while k >= 0 and lst[k][0] + 3000.0 > st:
-                        k -= 1
-                    for a, z, w in lst[k + 1:]:
-                        if pad and w == q:
-                            continue
-                        if a - pad >= st + d:
-                            break
-                        if z + pad > st:
-                            st = z + pad
-                            moved = True
-            for lst in [busy[q]] + [bank[b] for b in o["bk"]]:
-                k = len(lst)
-                while k and lst[k - 1][0] > st:
-                    k -= 1
-                lst.insert(k, (st, st + d, q))
-        beg[i], fin[i] = st, st + e
-    return beg, fin
-
-
-def settle(ops, deps, beg):
-    order = sorted(range(len(ops)), key=lambda i: (beg[i], i))
+def banks(ops, deps, order):
     used = {b: {} for b in range(8)}
     full = [None] * len(ops)
     for i in order:
@@ -611,7 +580,7 @@ def settle(ops, deps, beg):
         for b in ops[i]["bk"]:
             full[i].update(j for e, j in used[b].items() if e != ops[i]["q"])
             used[b][ops[i]["q"]] = i
-    return order, full
+    return full
 
 
 def rank_program(g, core, T, topo):
@@ -619,10 +588,9 @@ def rank_program(g, core, T, topo):
     if rank is None:
         return
     ops = build(g, T, topo, rank, core)
-    if "o" not in _ORDER:
-        deps = depend(ops)
-        _ORDER["o"] = settle(ops, deps, place(ops, deps, sequence(ops, deps, OFF, COST), COST)[0])
-    order, full = _ORDER["o"]
+    deps = depend(ops)
+    order = sequence(ops, deps)
+    full = banks(ops, deps, order)
     eng = {"V": g.vector, "S": g.scalar, "T": g.tensor, "G": g, "Y": g.sync}
     cnt = {}
     done = {}
@@ -638,7 +606,7 @@ def rank_program(g, core, T, topo):
             continue
         need = {}
         for d in full[i]:
-            if ops[d]["q"] == q and q in "TG":
+            if ops[d]["q"] == q == "T":
                 continue
             s, v = done[d]
             if know[q].get(s, 0) < v and (s not in need or need[s][0] < v):

import math
from concourse.mybir import AluOpType as OP, ActivationFunctionType as AF

N = 4
DIST = [1, 2, 3, 1]
RO = len(DIST)
S = 256
W = 4096
NH = 2
HS = S // NH
LN2 = math.log(2.0)
WT = 85
U = 65536.0
CFG = {"npc": 4,
       "vc": ((0, 1),),
       "vc0": ((0, 1), (0, 3)),
       "vh": (),
       "ns": (0, 0),
       "es": (0, 2),
       "esL": (0, 0),
       "nq": (2, 2),
       "nk": (4, 8),
       "bitV": (1, 1), "mbS": (1, 0), "maS": (0, 0), "dmwS": (1, 0), "yS": (0, 0), "x0G": (1, 1), "xbS": (1, 1), "early": 1, "own": (3,)}
PERIOD = 20000.0
PLACES = """
XG1A RMA3+ MBB+ aA+ XG1A3 ZDA_+ mBIA_+ mIBA_+ thB_+ zA_+ thA_+ send4A XG0A LAA+ qB+ bB+ r2A+ dx1A3 HMB+ LBB+ dx2A MAA3+ CMB+ XG2A dx0A dx1A dx0A3 dx2A3 send3B+ XG2A3 dx3A3 dx3A rmB+ send2B3+ CsB+ C16B+ wA+ DW0A3 st1B3++ XG3A3 HsB3+ sk0A3 dx4A3 fP1A_+ DW2A3 st5B3++ XG3A ldASIA_+ DW1A3 dx6A3 sk1A3 RMB3+ DW2A dx6A CMB3+ CsB3+ thA3+ fP2A_+ DW0A dx5A3 DW1A aA3+ LAA3+ DW3A MAB+ DW3A3 dx7A3 r1A3+ cN16A_ DW4A3 DW6A send3B3+ cEA_ XG0B XG1B dx4A sk0A dx5A sk2A3 sk3A3 sk4A3 XG1B3 DW4A aB+ sk1A dx7A XG0B3 DW6A3 DW5A RMB+ DW5A3 DW7A3 DW7A TMPA_+ HMA+ MAB3+ XG2B x0A3 sk2A sk3A sk4A XG2B3 zB3+ inH16A_+ LAB+ HsA+ sk5A3 sk6A3 HsB+ inHsA_+ sk7A3 ABSA3 H16A+ cTA_+ H16B+ G0A3 G3A3 G1A3 G2A3 sk5A sk6A sk7A ABSA dx1B3 XG3B r1B+ dx0B r2B+ dx1B XG3B3 wB+ IWA+ xbA xbA3 YG0A3 IWB+ cOFA_+ G3A G2A G0A G1A DW0B dx4B DW4B DW1B fP0A_+ dx0B3 DW0B3 ORA3+ dx4B3 HsA3+ cnt0A3 cnt1A3 cnt0A cnt1A DW4B3 DW1B3 cnt2A cnt3A dx5B sk0B cnt2A3 fIA_+ YG0A BITA cnt3A3 dx5B3 DW5B YG1A YG0B BITA3 wordA TIA sk1B TJA sk0B3 sk4B x0A YG0B3 YG3A3 DW5B3 x0pA mTHA_+ wordA3 TIA3 TJA3 aB3+ IWB_+ sk5B sk1B3 sk4B3 ONESA_ ABSB G0B cnt0B G1B cnt1B G2B cnt2B G3B cnt3B BITB x0B x0B3 x0pA3 send1A3 mCWA_+ YG2A YG3A xbB sk5B3 ABSB3 G0B3 cnt0B3 G1B3 cnt1B3 G2B3 cnt2B3 G3B3 cnt3B3 xbB3 wordB cDWA_ BITB3 KIA_ YG1A3 cKA_ cK0A_ cPA_ zB+ wordB3 r1B3+ dBB inCsA_+ cG16A_ RsA+ xpA3 TIB cWA_ dBA3 khA3 send1A xpA TIB3 TJB3 x0pB3 TJB x0pB send1B IMGA_ cNHA_ DSCA dBB3 khB3 E1A E0A send1B3 YG2A3 DSCA3 E1A3 E0A3 khB E2A dBA cZ1A_ cQbA_ YG2B3 E3A ndA3 E2A3 key0A3 key1A3 key2A3 khA ndA key0A key1A key2A key3A E3A3 cZA_ key3A3 KTA3 DSCB3 ldRINA_ YG2B c16PA_ YG3B3 thB+ YG1B YG3B mN32A_+ YG1B3 fP3A_+ xpB3 KTA CBIA_+ send0B3 SCA st4B3+ SGB3 CBA_+ cy2B xpB UNDA SCA3 ndB3 m16A_+ send0B IMA_ SGA XDA mHIA_+ E1B DSCB dy2B E1B3 E0B3 st2B3+ mkA cy3B SGA3 dy3B K32A N32A KKA E2B3 NSA mkA3 ldXA_ mBA_ key0B3 key1B3 key2B3 E3B3 mNBA_+ OFA DMA UNDB mZ0A_ K32A3 KKA3 OFA3 ES2B mIA_ key2B cb2A_ DMA3 send2A E0B key3B3 KTB3 ZA_ ndB mN16A_+ KHA3 SCB3 YUA N32A3 st0B3+ ES3B st3B3+ ZUA_ cQaA_ wcA wcB3 st6B3+ uA NSA3 DMWA THA key3B Z1A_ ttA wcA3 DMWA3 mNIA_ zdA_ RNDB key0B uA3 ldFINA_ mkB3 cKCA_ MSB FFA tbA_ key1B KHA XDB inRB_ inRA_ mUA_+ mN4kA_+ kmB KTB SCB PUTA CMA THA3 ldCINA_ A8A_ SGB qA cTHA_ mbA ttA3 RsB+ K32B3 qA3 mkB MBA FFA3 CsA K32B send2A3 wcB bA KKB3 OFB3 DMB3 uB3 THB3 cbwA_ Q8IA_ mNBUA_ KKB mG8A_ N32B OFB NSB ldHINA_ N32B3 DMB uB NSB3 LAB3+ ORB3+ Q8A_ DMWB3 LBA rmA mbA3 inC16A_ thB3+ ttB3 FFB3 YUB MBB3 CMA3 MBA3 bA3 LBA3 cQA_ THB qB3 r0B_ KHB DMWB ttB PUTB C16A CsA3 send3A3 FFB wB_ RMA bB3 LBB3 IWA_ rmA3 mTBA_ ibA_ rmB3 send3A MAA zA thA XG0A3- HMA3 wA_ mWBA_ send2B IPA_- KHB3 HMB3 zA3 st7B3+ zB_ r1A SDA_
""".split()
OFF = {_a.rstrip("+-"): (_i + 0.5) * PERIOD / len(PLACES) + PERIOD * (_a.count("+") - _a.count("-")) for _i, _a in enumerate(PLACES)}

SCRATCH = {}
for _n, _s, _d in [
    ("X", [128, W], "bfloat16"), ("ASI", [128, W], "int32"),
    ("XG", [128, W], "bfloat16"), ("YG", [128, W], "bfloat16"), ("DW", [128, W], "bfloat16"), ("E", [128, W], "bfloat16"), ("G", [128, W], "bfloat16"),
    ("CIN", [128, S], "int32"), ("HIN", [128, S], "int32"), ("RIN", [128, S], "int32"), ("FIN", [8, S], "int32"), ("Q8I", [8, S], "int32"),
    ("A8", [8, S], "bfloat16"), ("Q8", [8, S], "bfloat16"),
    ("C", [128, S], "float32"), ("C16", [128, S], "uint16"), ("H", [128, S], "float32"), ("H16", [128, S], "uint16"),
    ("R", [128, S], "bfloat16"), ("RM", [128, S], "bfloat16"), ("MA", [128, S], "bfloat16"), ("LA", [128, S], "bfloat16"),
    ("MB", [128, S], "bfloat16"), ("LB", [128, S], "bfloat16"), ("IW", [128, S], "bfloat16"), ("WB", [128, S], "bfloat16"), ("YS", [128, S], "bfloat16"),
    ("AB1", [128, S], "bfloat16"), ("BIT", [128, S], "bfloat16"), ("TI", [128, S], "int32"), ("TJ", [128, S], "int32"), ("SG", [128, S], "bfloat16"),
    ("CM", [128, S], "float32"), ("KH", [128, S], "float32"), ("HM", [128, S], "float32"), ("UND", [128, S], "bfloat16"), ("DSC", [128, S], "bfloat16"),
    ("XD", [128, S], "bfloat16"), ("YU", [128, S], "bfloat16"), ("KT", [128, S], "float32"), ("SC", [128, S], "float32"),
    ("RND", [128, S], "float32"), ("MS", [128, S], "bfloat16"),
    ("K32", [128, 16], "int32"), ("N32", [128, 16], "int32"), ("KK", [128, 16], "int32"), ("OF16", [128, 16], "uint16"),
    ("DM", [128, S], "bfloat16"), ("DMW", [128, S], "bfloat16"), ("TH", [128, S], "float32"),
    ("OR", [128, S], "float32"), ("OA", [8, S], "float32"),
    ("IP", [128, 1], "int32"), ("KI", [128, 1], "int32"), ("B4I", [128, 1], "int32"), ("COL", [128, 32], "float32"), ("THC", [128, 16], "float32"), ("COLB", [128, 2], "bfloat16"),
    ("IM", [128, 160], "bfloat16"), ("IMG", [128, 128], "bfloat16"), ("IMK", [128, 128], "bfloat16"),
    ("Z", [128, 144], "bfloat16"), ("ZU", [128, 144], "bfloat16"), ("Z1", [128, 144], "bfloat16"), ("ZD", [128, 144], "bfloat16"), ("ZH", [128, 144], "bfloat16"), ("ZDH", [128, 144], "bfloat16"),
    ("fI", [128, 128], "float32"), ("fP", [128, 512], "float32"), ("SD", [128, 128], "float32"), ("CB", [128, 8], "float32"), ("CBI", [128, 8], "float32"),
    ("mG8", [8, 128], "bfloat16"),
]:
    SCRATCH[_n] = ("sbuf", _s, _d)
for _n in "mB mI mNI mNB mNBU mTB mWB mCW mIB mBI mN16 mN4k mU mTH mZ0 ONES BIG TMP MK0 m16 mHI mN32".split():
    SCRATCH[_n] = ("sbuf", [128, 128], "bfloat16")
for _n in ("FF", "LF", "M1", "L1"):
    SCRATCH[_n] = ("sbuf", [128, RO * S], "bfloat16")
for _n in ("M0", "L0"):
    SCRATCH[_n] = ("sbuf", [128, RO * 3 * S], "bfloat16")
for _n in ("NS", "LN"):
    SCRATCH[_n] = ("sbuf", [128, RO * 16], "uint16")
for _b in range(8):
    SCRATCH["pb%d" % _b] = ("psum", [128, 512], "float32")

SEMAPHORES = ["sT", "sV", "sS", "sG", "r0_4", "l0_4"]
SEMAPHORES += ["ld_%s" % _n for _n in ("x", "ctx", "cand", "pref", "assoc", "fail0")] + ["st_%d" % _i for _i in range(8)]
for _t in range(RO):
    for _m in ("0", "10", "11", "20", "21", "30", "31"):
        SEMAPHORES += ["r%d_%s" % (_t, _m), "l%d_%s" % (_t, _m)]

cP, cK, cG16, cZ, cZ1, cPp, cPm, cS0, cS1, cKC, cOF, c16P, cW, cT, cE, cTH, cQa, cQb, cQ, cK0, c80, c81, cN16, cNH, cDW = range(25)

_ORDER = {}


def build(g, T, topo, rank, core):
    ops = []
    at = {"t": -1, "h": 0}

    def add(q, name, fn, rd, wr, cost, banks=(), sem=None, val=1, lat=None):
        ops.append({"q": q, "name": name + "AB"[at["h"]], "fn": fn, "rd": list(rd), "wr": list(wr), "bk": list(banks), "cost": cost,
                    "sem": sem, "val": val, "lat": lat, "t": at["t"]})

    def V(name, call, rd, wr, n, rate=1.0, banks=(), **kw):
        f = {"tt": g.vector.tensor_tensor, "ts": g.vector.tensor_scalar, "cp": g.vector.tensor_copy, "tr": g.vector.transpose,
             "scan": g.vector.tensor_tensor_scan}[call]
        add("V", name, lambda: f(**kw), rd, wr, (n, rate), banks)

    def join(m):
        part = ops[-m:]
        del ops[-m + 1:]
        o = ops[-1]
        for p in part[1:]:
            o["rd"] += p["rd"]
            o["wr"] += p["wr"]
        o["more"] = [p["fn"] for p in part[1:]]

    def fill(key, ap, c, n=1):
        add("V", key, lambda: g.vector.memset(ap, c), [], [key], (n, 0.5))

    def A(name, rd, wr, n, banks=(), rate=1.0, **kw):
        add("S", name, lambda: g.scalar.activation(**kw), rd, wr, (n, rate), banks)

    def MM(name, lst, rd, wr, bank):
        def fn():
            ins = None
            for o, l, r, a, b, n, f in lst:
                ins = g.tensor.matmul(out=o, lhsT=l, rhs=r, start=a, stop=b)
            return ins
        whole = lst[0][3] and lst[-1][4]
        lock = ["bank%d" % bank]
        add("T", name, fn, rd + (lock if whole else []), wr + ([] if whole else lock), sum(max(64, n) * (4 if f else 1) for o, l, r, a, b, n, f in lst), [bank])

    def SUM(name, bank, region, terms, start=True, stop=True):
        o = ps(bank, region)
        MM(name, [(o, T[m][:], x, start and j == 0, stop and j == len(terms) - 1, HS, m == "fI") for j, (m, x, k) in enumerate(terms)],
           [m for m, x, k in terms] + [z for m, x, k in terms for z in (k if isinstance(k, list) else [k])], ["ps%d%d" % (bank, region)], bank)

    def col(i):
        return T.COL[:, i:i + 1]

    def sl(b, h):
        return b[:, h * HS:(h + 1) * HS]

    def m0(b, t, h, j):
        return sl(b, NH * (3 * t + j) + h)

    def ps(b, r):
        return T["pb%d" % b][:, r * 128:(r + 1) * 128]

    def sel(z, k):
        return z[:, 15 - k:143 - k]

    def ldw(q, semn, key, dst, src, lat):
        e = g.sync if q == "Y" else g.scalar
        add(q, "ld" + key, lambda: e.dma_start(out=dst, in_=src), [], [key], "dma", sem="ld_" + semn, val=16, lat=lat)

    ldw("S", "x", "X", T.X[:], T.x[:], 4500)
    ldw("Y", "ctx", "CIN", T.CIN[:], T.ctx[:], 2200)
    ldw("Y", "pref", "RIN", T.RIN[:], T.pref[:], 2300)
    ldw("Y", "fail0", "FIN", T.FIN[:], T.fail0[:], 2400)
    ldw("Y", "cand", "HIN", T.HIN[:], T.cand[:], 2400)
    ldw("Y", "assoc", "ASI", T.ASI[:], T.assoc[:], 6500)
    ops[-1]["rd"] = ops[-2]["rd"] = ["X"]

    def iota(dst, key, pattern, base, cm, n, flag=True):
        if flag:
            fn = lambda: g.iota(dst, pattern, base, cm, allow_small_or_imprecise_dtypes=True)
        else:
            fn = lambda: g.iota(dst, pattern, base, cm)
        add("G", key, fn, [], [key], n)

    iota(T.IP[:], "IP", [[1, 1]], 0, 1, 1, False)
    iota(T.IM[:], "IM", [[1, 160]], 0, 0, 160)
    iota(T.IMG[:], "IMG", [[16, 8], [0, 16]], 0, 0, 128)
    iota(T.CBI[:], "CBI", [[-16, 8]], 127, 0, 8)

    def pick(key, out, src, skey, pattern, op, other, base, cm):
        add("G", key, lambda: g.affine_select(out, src, pattern, op, other, base, cm), [skey], [key], 148)

    def ts(key, out, src, skeys, n, rate, a, b=None, op0=OP.add, op1=None):
        if op1 is None:
            V(key, "ts", skeys, [key], n, rate, out=out, in0=src, scalar1=a, scalar2=None, op0=op0)
        else:
            V(key, "ts", skeys, [key], n, rate, out=out, in0=src, scalar1=a, scalar2=b, op0=op0, op1=op1)

    def scol(i, key, src, skeys, a, b=None, op0=OP.add, op1=None):
        ts(key, col(i), src, skeys, 1, 1.0, a, b, op0, op1)

    def mat(key, skey, c, ckey, op=OP.is_equal, n=128):
        ts(key, T[key][:, 0:n], T[skey][:, 0:n], [skey, ckey], n, 0.5, c, op0=op)

    def scaled(key, skey, c, n=128):
        A(key, [skey], [key], n, out=T[key][:, 0:n], in_=T[skey][:, 0:n], func=AF.Copy, scale=c)

    for key, dst, src in (("C16", T.C16, "CIN"), ("H16", T.H16, "HIN"), ("Cs", T.C, "CIN"), ("Hs", T.H, "HIN")):
        V("in" + key, "cp", [src], [key + "0", key + "1"], S, out=dst[:], in_=T[src][:])
    ts("KI", T.KI[:], T.IP[:], ["IP"], 1, 1.0, 15, op0=OP.bitwise_and)
    V("cP", "cp", ["IP"], ["cP"], 1, out=col(cP), in_=T.IP[:])
    V("cK", "cp", ["KI"], ["cK"], 1, out=col(cK), in_=T.KI[:])
    V("cG16", "tt", ["cP", "cK"], ["cG16"], 1, out=col(cG16), in0=col(cP), in1=col(cK), op=OP.subtract)
    mat("mI", "IM", col(cP), "cP")
    scaled("mNI", "mI", -1.0)
    for i, key, c in ((cW, "cW", WT * LN2), (cT, "cT", 6.5 * 2.0 ** 96), (cE, "cE", 15.0 * LN2)):
        fill(key, col(i), c)
    scol(cZ, "cZ", col(cG16), ["cG16"], 15.0)
    scol(cZ1, "cZ1", col(cG16), ["cG16"], 16.0)
    mat("Z", "IM", col(cZ), "cZ", n=144)
    mat("Z1", "IM", col(cZ1), "cZ1", n=144)
    MM("zd", [(T.pb0[:, 0:144], T.mI[:], T.Z[:], True, False, 144, False), (T.pb0[:, 0:144], T.mNI[:], T.Z1[:], False, True, 144, False)], ["mI", "mNI", "Z", "Z1"], ["ring0"], 0)
    A("ZD", ["ring0"], ["ZD"], 144, [0], out=T.ZD[:], in_=T.pb0[:, 0:144], func=AF.Copy)
    scaled("ZU", "Z", U, 144)
    ns = CFG["ns"]
    if max(ns):
        scaled("ZH", "Z", 0.5, 144)
        scaled("ZDH", "ZD", 0.5, 144)
        for h in range(NH):
            scol(c80 + h, "c8%d" % h, col(cK), ["cK"], float(16 - ns[h]), 8.0, OP.is_equal, OP.mult)
    for r in range(16 - max(ns), 16):
        fill("thr%d" % r, T.THC[:, r:r + 1], -0.6 * 2.0 ** (WT - 11 * r))

    def cntm(r, h):
        if r >= 16 - ns[h]:
            return sel(T.ZDH if r < 15 else T.ZH, r)
        return sel(T.ZD if r < 15 else T.Z, r)
    mat("mB", "IMG", col(cG16), "cG16")
    fill("ONES", T.ONES[:], 1.0, 128)
    if not min(CFG["xbS"]):
        fill("BIG", T.BIG[:], 32768.0, 128)
    A("cb2", ["cK", "cE"], ["cb2"], 1300, out=T.COLB[:, 0:1], in_=col(cK), func=AF.Exp, bias=col(cE), scale=-LN2)
    A("cbw", ["cK", "cW", "cb2"], ["cbw"], 1, out=T.COLB[:, 1:2], in_=col(cK), func=AF.Exp, bias=col(cW), scale=-11.0 * LN2)

    def wloc(t, h):
        return (sl(T.WB, h), "w%d" % h) if CFG["dmwS"][h] else (m0(T.M0, t, h, 1), "w%d_%d" % (t, h))

    def rloc(t, h):
        return (m0(T.M0, t, h, 1), "R%d_%d" % (t, h)) if CFG["dmwS"][h] else (sl(T.R, h), "R%d" % h)

    def orders(h, t, src, rd, banks=()):
        A("w", rd + ["cW", "cb2"], [wloc(t, h)[1]], HS, banks, out=wloc(t, h)[0], in_=src, func=AF.Exp, bias=col(cW), scale=-11.0 * LN2)
        A("IW", rd + ["cb2"], ["IW%d" % h], HS, banks, out=sl(T.IW, h), in_=src, func=AF.Exp, scale=LN2)

    mat("mWB", "mB", T.COLB[:, 0:1], "cb2", OP.mult)
    ts("TMP", T.TMP[:], T.mB[:], ["mB", "cbw"], 128, 0.5, T.COLB[:, 1:2], -0.6, OP.mult, OP.mult)
    pick("mCW", T.mCW[:], T.TMP[:], "TMP", [[0, 8], [1, 16]], OP.not_equal, 0.0, 0, 0)
    scol(cKC, "cKC", col(cK), ["cK"], 0.0, -(2.0 ** -90), OP.is_equal, OP.add)
    for key, skey, c in (("fI", "mI", 1.0), ("mN4k", "mI", -4096.0), ("mNB", "mB", -1.0), ("mNBU", "mB", -U), ("mN16", "mI", -16.0)):
        scaled(key, skey, c)
    if max(CFG["es"]):
        scaled("mU", "mI", U)
    if max(CFG["mbS"] + CFG["maS"]):
        scaled("m16", "mI", 16.0)
        scaled("mHI", "mI", 0.5)
        fill("cN16", col(cN16), -16.0)
        fill("cNH", col(cNH), -0.5)
    if max(CFG["dmwS"]):
        scaled("mN32", "mI", -32.0)
        fill("cDW", col(cDW), -64.0 * LN2)
    SUM("ib", 1, 0, [("mI", T.mI[:], "mI"), ("mNI", T.mB[:], "mB")])
    SUM("tb", 1, 1, [("mI", T.mI[:], "mI"), ("mI", T.mI[:], "mI"), ("mNI", T.mB[:], "mB")])
    for key, r, c in (("mIB", 0, 1.0), ("mBI", 0, -1.0), ("mTB", 1, 1.0)):
        A(key, ["ps1%d" % r, "ring1"], [key], 128, [1], out=T[key][:], in_=ps(1, r), func=AF.Copy, scale=c)
    scol(cOF, "cOF", col(cK), ["cK"], 16.0, 1807.0, OP.mult, OP.add)
    scol(c16P, "c16P", col(cP), ["cP"], 16.0, op0=OP.mult)
    for j in range(4):
        a, b = j // 2, j % 2
        pick("fP%d" % j, T.fP[:, j * 128:(j + 1) * 128], T.ONES[:], "ONES", [[-32, 4], [1000, 2], [-1, 16]], OP.is_equal, 0.0, -16 * a - 1000 * b, 1)
    iota(T.SD[:], "SD", [[0, 128]], 4096, 0, 128)
    pick("SD", T.SD[:], T.SD[:], "SD", [[0, 8], [1, 16]], OP.not_equal, -(2.0 ** 22), 0, 0)
    scaled("CB", "CBI", U, 8)
    ts("mG8", T.mG8[:], T.IMG[0:8, :], ["IMG", "c16P"], 128, 0.5, T.COL[0:8, c16P:c16P + 1], op0=OP.is_equal)
    V("A8", "cp", ["FIN"], ["A8"], S, out=T.A8[:], in_=T.FIN[:])
    ts("Q8I", T.Q8I[:], T.FIN[:], ["FIN"], S, 1.0, 3, op0=OP.bitwise_and)
    V("Q8", "cp", ["Q8I"], ["Q8"], S, out=T.Q8[:], in_=T.Q8I[:])
    scol(cK0, "cK0", col(cK), ["cK"], 0.0, op0=OP.is_equal)
    scol(cQa, "cQa", col(cK), ["cK"], 1.0, -4.0, OP.is_equal, OP.mult)
    scol(cQb, "cQb", col(cK), ["cK"], 2.0, 4.0, OP.is_equal, OP.mult)
    scol(cQ, "cQ", col(cQa), ["cQa", "cQb", "cK0"], col(cQb), col(cK0), OP.add, OP.add)
    scol(cTH, "cTH", col(cQa), ["cQa", "cQb"], 0.75, col(cQb), OP.mult, OP.subtract)
    mat("mTH", "mB", col(cQ), "cQ", OP.mult)
    mat("mZ0", "mB", col(cK0), "cK0", OP.mult)
    for h in range(NH):
        at["h"] = h
        P, Q = 4 + h, 6 + h
        r, rk = rloc(0, h)
        V("inR", "cp", ["RIN"], [rk], HS, out=r, in_=sl(T.RIN, h))
        orders(h, 0, r, [rk])
        SUM("z", Q, 2, [("mG8", sl(T.Q8, h), "Q8")])
        A("th", ["ps%d2" % Q, "cTH"], ["th0_%d" % h], HS, [Q], out=m0(T.M0, 0, h, 2), in_=ps(Q, 2), func=AF.Relu, bias=col(cTH))
        if not CFG["mbS"][h]:
            SUM("r0", P, 3, [("mI", r, rk)])

    def send(t, m, dst, src_ap, dst_ap, rd, wr, more):
        rid, pid, _s = topo.addr(dst)
        mask = topo.mask(core, dst)
        ne = len(topo.engines(core, dst))
        rs, ls = "r%d_%s" % (t, m), "l%d_%s" % (t, m)
        add("G", "send" + m[0], lambda: g.remote_dma(out_ap=dst_ap, in_ap=src_ap, remote_sem=T.sem[rs], local_sem=T.sem[ls], pid=pid, routing_id=rid, dma_engine_mask=mask),
            rd, [], "issue")
        ops[-1]["remote"] = (ls, ne)
        k = len(ops) - 1
        add("N", "land" + m[0], None, [], wr, "hop", sem=rs, val=ne, lat=more)
        ops[-1]["after"] = k

    def gather(h, src16, dst, key, okey, vp):
        npc = CFG["npc"]
        step = HS // npc
        for j in range(npc):
            a = h * HS + j * step
            offs = src16[:, a:a + step]
            o = dst[:, 16 * a:16 * (a + step)]
            if (h, j) in vp:
                V(key + str(j), "cp", ["X", okey + str(h)], [key + "%d%d" % (h, j)], 16 * step, "g", out=o, in_=T.X[:].indirect(offs))
            else:
                A(key + str(j), ["X", okey + str(h)], [key + "%d%d" % (h, j)], 16 * step, (), "g", out=o, in_=T.X[:].indirect(offs), func=AF.Copy)

    ring = [0]

    for t in range(RO):
        hear = T.cores[(rank + DIST[t]) % N]
        spk = T.cores[(rank - DIST[t]) % N]
        M1, L1, FF, LF = [b[:, t * S:(t + 1) * S] for b in (T.M1, T.L1, T.FF, T.LF)]
        NS, LN = T.NS[:, t * 16:(t + 1) * 16], T.LN[:, t * 16:(t + 1) * 16]
        last = t == RO - 1
        at["t"] = t
        wth = [k for h in range(NH) for k in ((rloc if CFG["dmwS"][h] else wloc)(t, h)[1], "th%d_%d" % (t, h))]
        l0k = l4k = "L0_%d" % t
        early = t == 0 and CFG["early"]
        if early:
            l4k = "L4"
            at["h"] = 0
            send(t, "4", hear, T.M0[:, S:3 * S], T.L0[:, S:3 * S], wth, [l4k], 300)
        for h in range(NH):
            hs = str(h)
            th = "%d_%d" % (t, h)
            at["h"] = h
            P, Q = 4 + h, 6 + h
            gather(h, T.C16, T.XG, "XG", "C16", CFG["vc"] if t else CFG["vc0"])
            xgk = ["XG%d%d" % (h, j) for j in range(CFG["npc"])]
            x0 = T.XG[:, h * 2048:(h + 1) * 2048:16]
            nq = CFG["nq"][h]
            qs = HS // nq
            npq = CFG["npc"] // nq
            for q in range(nq):
                qk = xgk[q * npq:(q + 1) * npq]

                def xg(k, h=h, q=q, qs=qs):
                    return T.XG[:, h * 2048 + q * qs * 16 + k:h * 2048 + (q + 1) * qs * 16:16]

                def dw(k, h=h, q=q, qs=qs):
                    return T.DW[:, h * 2048 + k * 128 + q * qs:h * 2048 + k * 128 + (q + 1) * qs]
                wq = wloc(t, h)[0][:, q * qs:(q + 1) * qs]
                sk = T["pb%d" % P][:, q * qs:(q + 1) * qs]
                nk = CFG["nk"][h]
                for c in range(16 // nk):
                    ks = range(1 + nk * c, min(16, 1 + nk + nk * c))
                    b = ring[0] % 4
                    ring[0] += 1
                    lst = []
                    for j, k in enumerate(ks):
                        o = T["pb%d" % b][:, j * qs:(j + 1) * qs]
                        lst.append((o, T.mI[:], xg(k), True, False, qs, False))
                        lst.append((o, T.mNI[:], xg(0), False, True, qs, False))
                    nm = str(4 * q + c)
                    MM("dx" + nm, lst, qk + ["mI", "mNI"], ["ring%d" % b], b)
                    for j, k in enumerate(ks):
                        V("DW" + nm, "tt", ["ring%d" % b, wloc(t, h)[1]], ["DW%d%d_%d" % (h, q, k)], qs, 1.0, [b],
                          out=dw(k), in0=T["pb%d" % b][:, j * qs:(j + 1) * qs], in1=wq, op=OP.mult)
                    join(len(ks))
                    MM("sk" + nm, [(sk, sel(T.Z, k), dw(k), k == 1, k == 15, qs, False) for k in ks],
                       ["Z"] + ["DW%d%d_%d" % (h, q, k) for k in ks], ["ps%d0" % P], P)
            if CFG["xbS"][h]:
                A("xb", xgk, ["ps%d3" % Q], HS, [Q], out=ps(Q, 3), in_=x0, func=AF.Identity, bias=32768.0)
            else:
                SUM("xb", Q, 3, [("mI", T.BIG[:], "BIG"), ("mI", x0, xgk)])
            if CFG["x0G"][h]:
                add("G", "x0", lambda o=m0(T.M0, t, h, 0), i=x0: g.affine_select(o, i, [[0, HS]], OP.is_ge, 0.0, 0, 0), xgk, ["x0" + th], HS + 20)
            else:
                A("x0", xgk, ["x0" + th], HS, out=m0(T.M0, t, h, 0), in_=x0, func=AF.Copy)
            ab, bit = sl(T.AB1, h), sl(T.BIT, h)
            A("ABS", ["ps%d0" % P], ["ABS" + hs], HS, [P], out=ab, in_=ps(P, 0), func=AF.Abs)

            def G(r, h=h):
                return T.G[:, h * 2048 + r * 128:h * 2048 + (r + 1) * 128]
            for r in range(16):
                if r >= 16 - ns[h]:
                    A("GS%d" % (r // 4), ["ABS" + hs, "thr%d" % r], ["G%d_%d" % (h, r)], HS, out=G(r), in_=ab, func=AF.Sign, bias=T.THC[:, r:r + 1])
                else:
                    V("G%d" % (r // 4), "ts", ["ABS" + hs], ["G%d_%d" % (h, r)], HS, 0.5, out=G(r), in0=ab, scalar1=0.6 * 2.0 ** (WT - 11 * r), scalar2=None, op0=OP.is_ge)
                if r % 4 == 3:
                    join(4)
                    MM("cnt%d" % (r // 4), [(ps(P, 1), cntm(q, h), G(q), q == 0, q == 15, HS, False) for q in range(r - 3, r + 1)],
                       ["Z", "ZD", "ZH", "ZDH"] + ["G%d_%d" % (h, q) for q in range(r - 3, r + 1)], ["ps%d1" % P], P)
            c8 = col(c80 + h) if max(ns) else 0.0
            if CFG["bitV"][h]:
                V("BIT", "ts", ["ps%d1" % P, "c8" + hs], ["BIT" + hs], HS, 1.0, [P], out=bit, in0=ps(P, 1), scalar1=c8, scalar2=0.5, op0=OP.add, op1=OP.is_gt)
            else:
                A("BIT", ["ps%d1" % P, "c8" + hs], ["BIT" + hs], HS, [P], out=bit, in_=ps(P, 1), func=AF.Sign, bias=c8)
            SUM("word", P, 0, [("mWB", bit, "BIT" + hs)])
            V("TI", "tt", ["ps%d0" % P, "IW" + hs], ["TI" + hs], HS, 1.0, [P], out=sl(T.TI, h), in0=ps(P, 0), in1=sl(T.IW, h), op=OP.mult)
            V("TJ", "ts", ["TI" + hs], ["TJ" + hs], HS, 1.0, out=sl(T.TJ, h), in0=sl(T.TI, h), scalar1=32768, scalar2=None, op0=OP.bitwise_and)
            V("x0p", "tt", ["TJ" + hs, "ps%d3" % Q], ["x0p" + th], HS, 1.0, [Q], out=sl(M1, h), in0=ps(Q, 3), in1=sl(T.TJ, h), op=OP.subtract)
            send(t, "1" + hs, hear, sl(M1, h), sl(L1, h), ["x0p" + th], ["L1" + th], 0)
            SUM("dB", Q, 1, [("mI", ab, "ABS" + hs), ("mCW", bit, "BIT" + hs)])
            A("SG", ["ps%d1" % Q, "cKC"], ["SG" + hs], HS, [Q], out=sl(T.SG, h), in_=ps(Q, 1), func=AF.Sign, bias=col(cKC))
        piece = slice(3 * t * S, (3 * t + (1 if early else 3)) * S)
        send(t, "0", hear, T.M0[:, piece], T.L0[:, piece], ["x0%d_%d" % (t, h) for h in range(NH)] + ([] if early else wth), [l0k], 0 if early else 500)
        for h in range(NH):
            at["h"] = h
            gather(h, T.H16, T.YG, "YG", "H16", CFG["vh"])
        for h in range(NH):
            hs = str(h)
            th = "%d_%d" % (t, h)
            at["h"] = h
            P, Q = 4 + h, 6 + h
            ygk = ["YG%d%d" % (h, j) for j in range(CFG["npc"])]
            l1, l1k = sl(L1, h), "L1" + th
            es = CFG["esL" if last else "es"][h]
            if es < 4 or not last:
                SUM("xp", P, 0, [("mI", l1, l1k)])
            V("DSC", "ts", [l1k], ["DSC" + hs], HS, 0.5, out=sl(T.DSC, h), in0=l1, scalar1=1000.0, scalar2=None, op0=OP.is_lt)
            if not last:
                V("UND", "ts", [l1k], ["UND" + hs], HS, 0.5, out=sl(T.UND, h), in0=l1, scalar1=1000.0, scalar2=None, op0=OP.is_gt)
                V("XD", "tt", ["ps%d0" % P, "DSC" + hs], ["XD" + hs], HS, 1.0, [P], out=sl(T.XD, h), in0=ps(P, 0), in1=sl(T.DSC, h), op=OP.mult)
            key, kk = ps(Q, 0), "ps%d0" % Q
            SUM("kh", Q, 0, [("fI", sl(T.H, h), "Hs" + hs)], stop=False)
            SUM("nd", Q, 0, [("mNBU", sl(T.DSC, h), "DSC" + hs)], start=False, stop=False)
            vb = ring[0] % 4
            ring[0] += 1 if es else 0
            for c in range(4):
                ks = range(c, 16, 4)
                eks = ["E%d_%d" % (h, k) for k in ks]
                ec = T.E[:, h * 2048 + c * 512:h * 2048 + (c + 1) * 512]
                if c >= 4 - es:
                    ring[0] += 1 if ring[0] % 4 == vb else 0
                    b = ring[0] % 4
                    ring[0] += 1
                    pb = T["pb%d" % b]
                    MM("cy%d" % c, [(pb[:, 0:512], T.mI[:], T.YG[:, h * 2048 + c:(h + 1) * 2048:4], True, False, 512, False)], ygk + ["mI"], ["ring%d" % b], b)
                    MM("dy%d" % c, [(pb[:, j:512:4], T.mNI[:], l1, False, j == 3, HS, False) for j in range(4)], ["mNI", l1k], ["ring%d" % b], b)
                    A("ES%d" % c, ["ring%d" % b], eks, 512, [b], out=ec, in_=pb[:, 0:512], func=AF.Relu, scale=512.0, bias=1.0)
                    MM("key%d" % c, [(ps(vb, 0), sel(T.Z, k), ec[:, j:512:4], k == 4 - es, k == 15, HS, False) for j, k in enumerate(ks)], ["Z"] + eks, ["ring%d" % vb], vb)
                else:
                    for j, k in enumerate(ks):
                        V("E%d" % c, "tt", ygk + ["ps%d0" % P], ["E%d_%d" % (h, k)], HS, 1.0, [P], out=sl(ec, j), in0=T.YG[:, h * 2048 + k:(h + 1) * 2048:16], in1=ps(P, 0), op=OP.is_equal)
                    join(4)
                    MM("key%d" % c, [(key, sel(T.ZU, k), sl(ec, j), False, k == 15, HS, False) for j, k in enumerate(ks)], ["ZU"] + eks, [kk], Q)
            if es:
                V("RND", "ts", ["ring%d" % vb], ["RND" + hs], HS, 1.0, [vb], out=sl(T.RND, h), in0=ps(vb, 0), scalar1=1.5 * 2.0 ** 32, scalar2=-1.5 * 2.0 ** 32, op0=OP.add, op1=OP.add)
                V("MS", "tt", ["ring%d" % vb, "RND" + hs], ["MS" + hs], HS, 1.0, [vb], out=sl(T.MS, h), in0=ps(vb, 0), in1=sl(T.RND, h), op=OP.subtract)
                SUM("km", Q, 0, [("mU", sl(T.MS, h), "MS" + hs)], start=False)
            V("KT", "tr", [kk], ["KT" + hs], HS, 1.0, [Q], out=sl(T.KT, h), in_=key)
            A("KH", [kk], ["KH" + hs], HS, [Q], out=sl(T.KH, h), in_=key, func=AF.Relu, scale=-1.0)
            V("SC", "scan", ["KT" + hs, "SD"], ["SC" + hs], HS, 1.0, out=sl(T.SC, h), data0=T.SD[:], data1=sl(T.KT, h), initial=0.0, op0=OP.add, op1=OP.max)
            lst = []
            for hh in range(2):
                for g2 in range(2):
                    lst.append((T["pb%d" % Q][:, 128 + hh:136:2], T.fP[:, (2 * hh + g2) * 128:(2 * hh + g2 + 1) * 128],
                                T.SC[:, h * HS + g2 * 16 + 15:(h + 1) * HS:32], g2 == 0, g2 == 1, 4, True))
            MM("mk", lst, ["fP%d" % j for j in range(4)] + ["SC" + hs], ["ps%d1" % Q], Q)
            ws = slice(8 * h, 8 * h + 8)
            V("K32", "tt", ["ps%d1" % Q, "CB"], ["K32" + hs], 8, 1.0, [Q], out=T.K32[:, ws], in0=T["pb%d" % Q][:, 128:136], in1=T.CB[:], op=OP.add)
            V("N32", "ts", ["K32" + hs], ["N32" + hs], 8, out=T.N32[:, ws], in0=T.K32[:, ws], scalar1=4095, scalar2=None, op0=OP.bitwise_and)
            V("NS", "cp", ["N32" + hs], ["NS" + th], 8, out=NS[:, ws], in_=T.N32[:, ws])
            send(t, "2" + hs, spk, NS[:, ws], LN[:, ws], ["NS" + th], ["LN" + th], -100)
            SUM("q", Q, 3, [("fI", sl(T.C, h), "Cs" + hs), ("mN4k", T.ONES[:], "ONES"), ("mN4k", sl(T.SG, h), "SG" + hs)])
            V("KK", "ts", ["K32" + hs], ["KK" + hs], 8, out=T.KK[:, ws], in0=T.K32[:, ws], scalar1=12, scalar2=0xF0F, op0=OP.arith_shift_right, op1=OP.bitwise_and)
            V("OF", "ts", ["KK" + hs, "cOF"], ["OF16" + hs], 8, out=T.OF16[:, ws], in0=T.KK[:, ws], scalar1=-1.0, scalar2=col(cOF), op0=OP.mult, op1=OP.add)
            ysrc = T.YG[:, h * 2048:(h + 1) * 2048].indirect(T.OF16[:, ws])
            if CFG["yS"][h] and not last:
                A("YS", ygk + ["OF16" + hs], ["YS" + hs], HS, (), "g", out=sl(T.YS, h), in_=ysrc, func=AF.Copy)
                SUM("ys", Q, 1, [("mI", sl(T.YS, h), "YS" + hs)])
                ysrc, yk, yr, yb = ps(Q, 1), ["ps%d1" % Q], 1.0, [Q]
            else:
                yk, yr, yb = ygk + ["OF16" + hs], "g", []
            dm, dmk = sl(T.DM, h), "DM" + hs
            V("DM", "tt", yk + [l0k], [dmk], HS, yr, yb, out=dm, in0=ysrc, in1=m0(T.L0, t, h, 0), op=OP.not_equal)
            if not last:
                V("YU", "tt", yk + ["UND" + hs], ["YU" + hs], HS, yr, yb, out=sl(T.YU, h), in0=ysrc, in1=sl(T.UND, h), op=OP.mult)
            if CFG["dmwS"][h]:
                SUM("wc", P, 1, [("mI", m0(T.L0, t, h, 1), l4k), ("mN32", dm, dmk)])
                A("DMW", ["ps%d1" % P, "cDW"], ["DMW" + hs], HS, [P], out=sl(T.DMW, h), in_=ps(P, 1), func=AF.Exp, scale=-2.0 * LN2, bias=col(cDW))
            else:
                SUM("wc", P, 1, [("mI", m0(T.L0, t, h, 1), l4k)])
                V("DMW", "tt", ["ps%d1" % P, dmk], ["DMW" + hs], HS, 1.0, [P], out=sl(T.DMW, h), in0=ps(P, 1), in1=dm, op=OP.mult)
            SUM("u", Q, 2, [("mTH", m0(T.L0, t, h, 2), l4k), ("mNB", dm, dmk)])
            A("TH", ["ps%d2" % Q, "cT"], ["TH" + hs], HS, [Q], out=sl(T.TH, h), in_=ps(Q, 2), func=AF.Relu, scale=2.0 ** 96, bias=col(cT))
            SUM("tt", P, 2, [("mTB", sl(T.DMW, h), "DMW" + hs)])
            V("FF", "tt", ["ps%d2" % P, "TH" + hs], ["FF" + th], HS, 1.0, [P], out=sl(FF, h), in0=ps(P, 2), in1=sl(T.TH, h), op=OP.is_gt)
            send(t, "3" + hs, spk, sl(FF, h), sl(LF, h), ["FF" + th], ["LF" + th], 0)
        if not last:
            for h in range(NH):
                hs = str(h)
                at["h"] = h
                V("PUT", "tt", ["YU" + hs, "XD" + hs, "OF16" + hs], ["X"], HS, "sc", out=T.X[:, h * 2048:(h + 1) * 2048].indirect(T.OF16[:, 8 * h:8 * h + 8]),
                  in0=sl(T.YU, h), in1=sl(T.XD, h), op=OP.add)
        for h in range(NH):
            hs = str(h)
            th = "%d_%d" % (t, h)
            at["h"] = h
            P, Q = 4 + h, 6 + h
            ws = slice(8 * h, 8 * h + 8)
            V("CM", "tt", ["ASI", "LN" + th, "SG" + hs], ["CM" + hs], HS, "g", out=sl(T.CM, h), in0=T.ASI[:].indirect(LN[:, ws]), in1=sl(T.SG, h), op=OP.mult)
            V("Cs", "tt", ["CM" + hs, "ps%d3" % Q], ["Cs" + hs], HS, 1.0, [Q], out=sl(T.C, h), in0=ps(Q, 3), in1=sl(T.CM, h), op=OP.max)
            if not last:
                V("C16", "cp", ["Cs" + hs], ["C16" + hs], HS, 1.0, out=sl(T.C16, h), in_=sl(T.C, h))
            V("HM", "tt", ["ASI", "NS" + th, "KH" + hs], ["HM" + hs], HS, "g", out=sl(T.HM, h), in0=T.ASI[:].indirect(NS[:, ws]), in1=sl(T.KH, h), op=OP.min)
            V("Hs", "tt", ["HM" + hs, "ps%d0" % Q], ["Hs" + hs], HS, 1.0, [Q], out=sl(T.H, h), in0=ps(Q, 0), in1=sl(T.HM, h), op=OP.max)
            if not last:
                V("H16", "cp", ["Hs" + hs], ["H16" + hs], HS, 1.0, out=sl(T.H16, h), in_=sl(T.H, h))
            ff, lf, r = (sl(FF, h), "FF" + th), (sl(LF, h), "LF" + th), rloc(t, h)
            rm, ma, la, mb, lb = [(sl(T[b], h), b + hs) for b in ("RM", "MA", "LA", "MB", "LB")]
            q1, qk, one = ps(Q, 1), "ps%d1" % Q, ("mHI", T.ONES[:], "ONES")
            if CFG["mbS"][h]:
                SUM("mb", Q, 1, [("mI",) + r, ("m16",) + ff])
                A("MB", [qk, "cN16"], [mb[1]], HS, [Q], out=mb[0], in_=q1, func=AF.Relu, bias=col(cN16))
                SUM("b", Q, 1, [("mNI",) + r, ("mB",) + mb])
                A("LB", [qk, "cNH"], [lb[1]], HS, [Q], out=lb[0], in_=q1, func=AF.Sign, bias=col(cNH))
                SUM("rm", P, 1, [one, ("mI",) + r, ("mNI",) + mb, ("mIB",) + ff, ("mHI",) + lb])
            else:
                V("MB", "tt", ["ps%d3" % P, ff[1]], [mb[1]], HS, 1.0, [P], out=mb[0], in0=ps(P, 3), in1=ff[0], op=OP.mult)
                SUM("b", Q, 1, [("mB",) + mb])
                V("LB", "tt", [r[1], qk], [lb[1]], HS, 1.0, [Q], out=lb[0], in0=q1, in1=r[0], op=OP.is_gt)
                SUM("rm", P, 1, [("mI",) + r, ("mNI",) + mb, ("mIB",) + ff, ("mI",) + lb])
            A("RM", ["ps%d1" % P], [rm[1]], HS, [P], out=rm[0], in_=ps(P, 1), func=AF.Copy)
            if CFG["maS"][h] and not last:
                SUM("ma", Q, 1, [("mI",) + rm, ("m16",) + lf])
                A("MA", [qk, "cN16"], [ma[1]], HS, [Q], out=ma[0], in_=q1, func=AF.Relu, bias=col(cN16))
                SUM("a", Q, 1, [("mN16",) + ff, ("mNI",) + rm, ("mB",) + ma])
                SUM("r1", P, 3, [one, ("mI",) + rm, ("mBI",) + ff, ("mNI",) + ma], stop=False)
                A("LA", [qk, "cNH"], [la[1]], HS, [Q], out=la[0], in_=q1, func=AF.Sign, bias=col(cNH))
                SUM("r2", P, 3, [("mHI",) + la], start=False)
            else:
                V("MA", "tt", ["ps%d1" % P, lf[1]], [ma[1]], HS, 1.0, [P], out=ma[0], in0=ps(P, 1), in1=lf[0], op=OP.mult)
                SUM("a", Q, 1, [("mN16",) + ff, ("mB",) + ma])
                SUM("r1", P, 3, [("mI",) + rm, ("mBI",) + ff, ("mNI",) + ma], stop=last)
                V("LA", "tt", [rm[1], qk], [la[1]], HS, 1.0, [Q], out=la[0], in0=q1, in1=rm[0], op=OP.is_gt)
                if not last:
                    SUM("r2", P, 3, [("mI",) + la], start=False)
            if not last:
                orders(h, t + 1, ps(P, 3), ["ps%d3" % P], [P])
                A("Rs", ["ps%d3" % P], [rloc(t + 1, h)[1]], HS, [P], out=rloc(t + 1, h)[0], in_=ps(P, 3), func=AF.Copy)
                SUM("z", Q, 2, [("mZ0", m0(T.M0, t, h, 2), "th" + th), ("mB",) + lf])
                A("th", ["ps%d2" % Q, "cTH"], ["th%d_%d" % (t + 1, h)], HS, [Q], out=m0(T.M0, t + 1, h, 2), in_=ps(Q, 2), func=AF.Relu, bias=col(cTH))
            else:
                V("OR", "tt", ["ps%d3" % P, la[1]], ["OR" + hs], HS, 1.0, [P], out=sl(T.OR, h), in0=ps(P, 3), in1=la[0], op=OP.add)
                oa = T["pb%d" % Q][0:8, 256:384]
                MM("z", [(oa, T.mI[0:8, 0:8], T.A8[:, h * HS:(h + 1) * HS], True, False, HS, False)] +
                   [(oa, T.mB[:, 0:128:16], sl(T.LF, NH * u + h), False, u == t, HS, False) for u in range(RO)],
                   ["mI", "mB", "A8"] + ["LF%d_%d" % (u, h) for u in range(RO)], ["ps%d2" % Q], Q)
                A("th", ["ps%d2" % Q], ["OA" + hs], HS, [Q], out=sl(T.OA, h), in_=oa, func=AF.Copy)

    def store(i, q, dst, src, rd):
        e = g.sync if q == "Y" else g.scalar
        add(q, "st%d" % i, lambda: e.dma_start(out=dst, in_=src), rd, ["out%d" % i], "dma", sem="st_%d" % i, val=16, lat=2000)
    for h in range(NH):
        store(h, "Y", sl(T.yctx, h), sl(T.C, h), ["Cs%d" % h])
        store(2 + h, "Y", sl(T.ycand, h), sl(T.H, h), ["Hs%d" % h])
        store(4 + h, "Y", sl(T.ypref, h), sl(T.OR, h), ["OR%d" % h])
        store(6 + h, "S", sl(T.yfail, h), sl(T.OA, h), ["OA%d" % h])
    return ops


def depend(ops):
    lastw, readers = {}, {}
    deps = []
    for i, o in enumerate(ops):
        d = set()
        for k in o["rd"] + o["wr"]:
            if k in lastw:
                d.add(lastw[k])
        for k in o["wr"]:
            d.update(readers.get(k, ()))
        if "after" in o:
            d.add(o["after"])
        deps.append(d)
        for k in o["rd"]:
            readers.setdefault(k, []).append(i)
        for k in o["wr"]:
            lastw[k] = i
            readers[k] = []
    return deps


def named(o):
    return o["name"] + ("_" if o["t"] < 0 else str(o["t"]) if o["t"] in CFG["own"] else "")


def sequence(ops, deps):
    key = []
    for i, o in enumerate(ops):
        key.append(max([o["t"] * PERIOD + OFF.get(named(o), -1e9)] + [key[j] for j in deps[i]]))
    return sorted(range(len(ops)), key=lambda i: (key[i], i))


def banks(ops, deps, order):
    used = {b: {} for b in range(8)}
    full = [None] * len(ops)
    for i in order:
        full[i] = set(deps[i])
        for b in ops[i]["bk"]:
            full[i].update(j for e, j in used[b].items() if e != ops[i]["q"])
            used[b][ops[i]["q"]] = i
    return full


def rank_program(g, core, T, topo):
    rank = T.rank_of(core)
    if rank is None:
        return
    ops = build(g, T, topo, rank, core)
    deps = depend(ops)
    order = sequence(ops, deps)
    full = banks(ops, deps, order)
    eng = {"V": g.vector, "S": g.scalar, "T": g.tensor, "G": g, "Y": g.sync}
    cnt = {}
    done = {}
    clock = {}
    know = {q: {} for q in "VSTGY"}
    for i in order:
        o = ops[i]
        q = o["q"]
        if q == "N":
            done[i] = (o["sem"], o["val"])
            clock[i] = {o["sem"]: o["val"]}
            cnt[o["sem"]] = o["val"]
            continue
        need = {}
        for d in full[i]:
            if ops[d]["q"] == q == "T":
                continue
            s, v = done[d]
            if know[q].get(s, 0) < v and (s not in need or need[s][0] < v):
                need[s] = (v, d)
        for s in list(need):
            v, d = need[s]
            for s2 in need:
                if s2 != s and clock[need[s2][1]].get(s, 0) >= v:
                    del need[s]
                    break
        for s in need:
            v, d = need[s]
            eng[q].wait_ge(T.sem[s], v)
            for k, x in clock[d].items():
                if know[q].get(k, 0) < x:
                    know[q][k] = x
        ins = o["fn"]()
        if "remote" in o:
            cnt[o["remote"][0]] = o["remote"][1]
            continue
        s = o["sem"] or "s" + q
        inc = o["val"] if o["sem"] else 1
        ins.then_inc(T.sem[s], inc)
        cnt[s] = cnt.get(s, 0) + inc
        for fn in o.get("more", ()):
            fn().then_inc(T.sem[s], 1)
            cnt[s] += 1
        done[i] = (s, cnt[s])
        clock[i] = dict(know[q])
        clock[i][s] = cnt[s]
    for s in cnt:
        if know["G"].get(s, 0) < cnt[s]:
            g.wait_ge(T.sem[s], cnt[s])
